import numpy as np, ml_dtypes
CORES = [40,41,42,43,44,45,46,47]
N = 8
BF = ml_dtypes.bfloat16
W, K, I, M, VIS = 4096, 512, 8, 512, 4
def mark(u, a):
    return ((u * u >> 5) + 37 * u + a) & (M - 1)
def parts(rng):
    pop = rng.integers(0, M, (N, 8, 16))
    nm = np.where(rng.random((N, 8, W)) < 0.5, np.take_along_axis(pop, rng.integers(0, 16, (N, 8, W)), 2), rng.integers(0, M, (N, 8, W)))
    vo = rng.integers(0, 256, (N, 8, 16, W)); vn = rng.integers(0, 256, (N, 8, 16, W)); x = rng.integers(0, 256, (N, 8, 16, M))
    c = rng.integers(0, W, (N, 8, K)); s = 2 * rng.integers(0, 512, (N, 8, K)) + 1
    z = np.minimum(rng.integers(0, 160, (N, 8, 1, K)) + rng.integers(0, 64, (N, 8, 16, K)), 255)
    return nm, vo, vn, x, c, s, z
def bf(a):
    return np.ascontiguousarray(a.reshape(N, 128, -1)).astype(np.float32).astype(BF)
def pack(nm, vo, vn, x, c, s, z):
    return {"nm": nm.astype(np.int32), "vo": bf(vo), "vn": bf(vn), "xo": bf(x), "c0": c.astype(np.int32), "s0": s.astype(np.int32), "z0": bf(z)}
def share16(rng, S):
    S = np.asarray(S); b = S >> 4
    v = b[..., None] + (np.arange(16) < (S & 15)[..., None])
    d = (rng.random(S.shape + (8,)) * (np.minimum(b, np.maximum(254 - b, 0))[..., None] + 1)).astype(np.int64)
    v = v + np.concatenate([d, -d], axis=-1)
    return np.take_along_axis(v, np.argsort(rng.random(v.shape), axis=-1), -1)
def sums(rng, lo, hi):
    a = np.arange(lo, hi + 1); h = mark(a, 0); o = np.argsort(h + rng.random(len(a)))
    return a[o[np.minimum(np.searchsorted(h[o], np.arange(M)), len(a) - 1)]]
def setup_inputs(rng):
    return pack(*parts(rng))
def setup_inputs_spread(rng):
    nm, vo, vn, x, c, s, z = parts(rng)
    def sized(n):
        return np.minimum((np.exp2(8 * rng.random((N, 8, 1, n))) * rng.random((N, 8, 16, n))).astype(np.int64), 255)
    nm = np.minimum((M * rng.random((N, 8, W)) ** 3).astype(np.int64), M - 1)
    s = 2 * np.exp2(9 * rng.random((N, 8, K))).astype(np.int64) - 1
    return pack(nm, sized(W), sized(W), sized(M), c, s, sized(K))
def setup_inputs_ends(rng):
    nm, vo, vn, x, c, s, z = parts(rng)
    def ends(n):
        return 255 * np.where(rng.random((N, 8, 1, n)) < 0.5, rng.integers(0, 2, (N, 8, 1, n)), rng.integers(0, 2, (N, 8, 16, n)))
    vo, vn, x, z = ends(W), ends(W), ends(M), ends(K)
    nm = np.where(rng.random(nm.shape) < 0.7, (M - 1) * rng.integers(0, 2, nm.shape), nm)
    c = np.where(rng.random(c.shape) < 0.7, (W - 1) * rng.integers(0, 2, c.shape), c)
    s = np.where(rng.random(s.shape) < 0.7, 1 + 1022 * rng.integers(0, 2, s.shape), s)
    up = rng.integers(0, 2, (N, 8, 1))
    nm[..., W - 1] = M - 1; nm[..., 0] = 0; nm[..., 1:I - 3] = (M - 1) * rng.integers(0, 2, (N, 8, I - 4)); nm[..., I - 3] = 0; nm[..., I - 2] = M - 1
    vo[..., W - 1] = 255 * up; vn[..., I - 2] = 255 * (1 - up); vo[..., 0] = 255 * (1 - up); vn[..., I - 3] = 255 * up
    h = W // 2; vo[..., h:h + I] = 255 * up[..., None]; vn[..., h:h + I] = 255 * up[..., None]
    for k, a in ((0, W - 1), (1, h), (2, h), (K - 1, W - 1)):
        c[..., k] = a; s[..., k] = 1
    z[..., 1] = 0; z[..., 2] = 255; z[..., K - 1] = 255
    return pack(nm, vo, vn, x, c, s, z)
def setup_inputs_corners(rng):
    nm, vo, vn, x, c, s, z = parts(rng); pl = np.arange(W)
    ty = (np.arange(8)[None, :] + 3 * np.arange(N)[:, None] + int(rng.integers(0, 8))) % 8
    first = int(rng.integers(0, N)); ty[(first + 1) % N, int(np.argmin(ty[first]))] = 0
    for q in range(N):
        for g in range(8):
            t = int(ty[q, g])
            if t == 0:
                vo[q, g] = 0; vn[q, g] = rng.integers(0, 4, (16, W)); vn[q, g][:, I - 1::I] = share16(rng, sums(rng, 64, 4080)[rng.permutation(M)]).T
                c[q, g] = I * rng.permutation(np.arange(K) % M); s[q, g] = 1; z[q, g] = 0
            elif t == 1:
                vo[q, g] = vo[q, g] >> 1; vn[q, g] = vn[q, g] >> 1; z[q, g] = 255
            elif t == 2: nm[q, g] = (M - 1) * int(rng.integers(0, 2))
            elif t == 3: nm[q, g] = pl & (M - 1)
            elif t == 4:
                nm[q, g] = np.where(pl % I == I - 1, pl - (I - 1), pl) & (M - 1); c[q, g] = I * rng.integers(0, M, K); s[q, g] = 1
            elif t == 5:
                v = rng.integers(0, 256, (16, 1)); vo[q, g] = v; vn[q, g] = v
                z[q, g] = np.argsort(np.argsort(rng.random((16, K)), axis=0), axis=0) >= rng.choice(np.array([0, 8, 9, 16]), K)
            elif t == 6: x[q, g] = 255 * rng.integers(0, 2, (16, M))
            else:
                c[q, g] = rng.choice(np.array([0, W - 2, W - 1, W - I, W - I + 1]), K); s[q, g] = rng.choice(np.array([1, 3, 1021, 1023]), K)
    return pack(nm, vo, vn, x, c, s, z)
def setup_inputs_crowd(rng):
    nm, vo, vn, x, c, s, z = parts(rng); pl = np.arange(W); vo[:] = 0; z[:] = 0
    for g in range(8):
        for q in range(N):
            if q == 0 or g & 1:
                sm = sums(rng, 960, 3200); pick = sm[2 * rng.integers(0, M // 2, 2) + ((g >> 1) & 1)]
            S = np.full(W, int(pick[0]))
            if g >= 6:
                S = np.where(pl < W // 2, int(pick[0]), int(pick[1])); s[q, g] = 1
            vn[q, g] = share16(rng, S).T
            if g & 3: z[q, g, :, (0, K - 1, int(rng.integers(0, K)))[(g & 3) - 1]] = 255
    v = rng.integers(0, 256, (16, 1)); vo[:, 0] = v; vn[:, 0] = v; nm[:, 0] = np.maximum(nm[:, 0], 1)
    return pack(nm, vo, vn, x, c, s, z)
def setup_inputs_ties(rng):
    nm, vo, vn, x, c, s, z = parts(rng)
    vo[:, ::2] = 85 * rng.integers(0, 4, (N, 4, 16, W)); vn[:, ::2] = 85 * rng.integers(0, 4, (N, 4, 16, W))
    z[:, ::2] = np.minimum(85 * rng.integers(0, 4, (N, 4, 16, K)) + rng.integers(0, 2, (N, 4, 16, K)), 255)
    for q in range(N):
        for g in (1, 3, 5, 7):
            hi = int(rng.integers(1600, 3201)); lo = hi if g > 4 else hi - int(rng.integers(1, 400))
            v1 = share16(rng, hi); v2 = share16(rng, lo); ix = np.argsort(rng.random((16, W)), axis=0)
            vo[q, g] = 0; vn[q, g] = np.where(rng.random(W) < 0.3, v1[ix], v2[ix])
            a = int(np.sort(v1)[7]); b = int(np.sort(v2)[7])
            z[q, g] = rng.choice(np.array([a, a + 1, b, b + 1]), K)
    return pack(nm, vo, vn, x, c, s, z)
def check_inputs(d):
    bad = []
    for k, lo, hi in (("nm", 0, M - 1), ("c0", 0, W - 1), ("s0", 1, 1023), ("vo", 0, 255), ("vn", 0, 255), ("xo", 0, 255), ("z0", 0, 255)):
        v = np.asarray(d[k]).astype(np.float64)
        if not np.all((v >= lo) & (v <= hi)): bad.append("range of " + k)
        elif not np.all(v == np.floor(v)): bad.append("whole numbers in " + k)
    if not np.all((np.asarray(d["s0"]).astype(np.int64) & 1) == 1): bad.append("odd numbers in s0")
    return bad
def reference(nm, vo, vn, xo, c0, s0, z0):
    name = nm.astype(np.int64)
    O = vo.astype(np.float32).astype(np.int32).reshape(N, 8, 16, W); V = vn.astype(np.float32).astype(np.int32).reshape(N, 8, 16, W)
    X = xo.astype(np.float32).astype(np.int32).reshape(N, 8, 16, M); z = z0.astype(np.float32).astype(np.int32).reshape(N, 8, 16, K)
    c = c0.astype(np.int64); s = s0.astype(np.int64); A = np.zeros((N, 8, K), np.int64)
    row = np.arange(I); rule = np.arange(K); obj = np.arange(M); odd = (obj & 1) == 1
    for t in range(VIS):
        e = (c[..., None] + s[..., None] * row) & (W - 1)
        n = np.take_along_axis(name, e.reshape(N, 8, K * I), 2).reshape(N, 8, K, I)
        eq = n[..., :, None] == n[..., None, :]
        head = np.argmax(eq, axis=-1) == row; last = I - 1 - np.argmax(eq[..., ::-1], axis=-1)
        el = np.take_along_axis(e, last, 3)
        D = np.take_along_axis(V, el.reshape(N, 8, 1, K * I), 3) - np.take_along_axis(O, e.reshape(N, 8, 1, K * I), 3)
        D = D.reshape(N, 8, 16, K, I); S = np.add.reduce(np.abs(D), axis=2).astype(np.int64)
        f = np.argmax(np.where(head, S, -1), axis=-1)
        df = np.take_along_axis(D, f[:, :, None, :, None], 4)[..., 0]; B = np.abs(df)
        u = np.take_along_axis(S, f[..., None], 3)[..., 0]
        fire = np.add.reduce((B >= z).astype(np.int64), axis=2) >= 9
        m = mark(u, A)
        low = np.full((N, 8, M), K)
        np.minimum.at(low, (np.arange(N)[:, None, None], np.arange(8)[None, :, None], m), np.where(fire, rule, K))
        act = fire & (np.take_along_axis(low, m, 2) == rule)
        has = low < K; dm = np.take_along_axis(df, np.minimum(low, K - 1)[:, :, None, :], 3)
        has = np.where(odd, np.roll(has, 1, axis=0), has); dm = np.where(odd, np.roll(dm, 1, axis=0), dm)
        hw = has[:, :, None, :]; X2 = np.where(hw, np.clip(X + dm, 0, 255), X); a, b = t * M, (t + 1) * M
        name[..., a:b] = np.where(has, obj, name[..., a:b]); O[..., a:b] = np.where(hw, X, O[..., a:b]); V[..., a:b] = np.where(hw, X2, V[..., a:b])
        X = X2
        c = np.where(act, c + I * s, c + s * (f + 1)) & (W - 1); s = np.where(act, 2 * (u & 511) + 1, s)
        z = np.where(act[:, :, None, :], (z + B) >> 1, np.maximum(z - 1, 0)); A = (fire & ~act).astype(np.int64)
        if t < VIS - 1:
            c, s, z, A = np.roll(c, 1, axis=0), np.roll(s, 1, axis=0), np.roll(z, 1, axis=0), np.roll(A, 1, axis=0)
    L = VIS * M
    return {"yn": name[..., :L].astype(np.float32), "yo": O[..., :L].reshape(N, 128, L).astype(np.float32).astype(BF), "yv": V[..., :L].reshape(N, 128, L).astype(np.float32).astype(BF),
            "yx": X.reshape(N, 128, M).astype(np.float32).astype(BF), "yc": c.astype(np.float32), "ys": s.astype(np.float32), "ya": A.astype(np.float32), "yz": z.reshape(N, 128, K).astype(np.float32).astype(BF)}

@@ -1,0 +1,592 @@
+import math
+from concourse.bass import DstId, RemoteDMATransfer
+from concourse.mybir import AluOpType, AxisListType, ActivationFunctionType
+
+VIS = 4
+XP, NXP, WEND = 4096, 4608, 6656
+STW = 544
+BF, F32, I32, U16 = "bfloat16", "float32", "int32", "uint16"
+
+SCRATCH = {}
+for _d, _l in (
+    (BF, dict(OW=WEND, VW=WEND, NW=WEND, NG=4096, OG=4096, DD=4096, AD=4096, ZL=4 * 512, LND=4 * 1024, ZS=512, SB=1792,
+              XO=512, XN=512, YX=512, NMB=256, IDW=10 * 128, ZA=144, ZN=144, ZK=144, ZB=176, ZT=4 * 176, BI=8, KH=256,
+              KC=128, CB=32, EQ=2 * 7 * 128, ABB=64, GG=512, XH=128, OH=2048, AQ=512, DFW=1024, VT=512, OE=256, NE=256, ZW=1024)),
+    (F32, dict(STL=4 * STW, SST=STW, CSF=64, CSW=64, PF=16, XI=192, RS=128, M8=256, D1=256, W64=64, WA=64, WB=64, WC=64, WP=1,
+               JT=128, DL=128, RID=512, C256=128, NS=128, LY=256, KS=256, T3=32, T4=32, AT=32, HY=288, HQ=288, HE=288, HS=288,
+               WIN=32, UU=32, U2=32, U3=32, U4=32, DC=32, CN=32, DS=32, SA=32, FI=32, ACT=32, R1=32, R2=32, R3=32, R4=32, R5=32,
+               ZH=512, Z1=512, Z2=512, FO=96, FT=96)),
+    (I32, dict(NMI=256, CSI=64, PI=8, EI=256, EJ=256, KI=32, KX=32, UI=32, T1=32, T2=32, T5=32, T6=32, T7=32, T8=32, AB=64,
+               YI=32, YS=32, FC=32, FD=32)),
+    (U16, dict(OFL=4 * 256, SOF=256, OFE=256, OFD=32, OFB=32, OF1=32, OF2=32, OF3=32, OFZ=32)),
+):
+    for _k, _n in _l.items():
+        SCRATCH[_k] = ("sbuf", [128, _n], _d)
+ROWS = ("P0", "P1", "P3", "NS", "EQ")
+for _i in range(8):
+    SCRATCH["P%d" % _i] = ("psum", [128, 512], F32)
+for _k in ROWS:
+    SCRATCH[_k] = (SCRATCH[_k][0], [128, SCRATCH[_k][1][1] // 8, 8], SCRATCH[_k][2])
+
+SEMAPHORES = (["qv", "qs", "qp", "qg"] + ["d%d" % i for i in range(40)] + ["l%d" % i for i in range(24)]
+              + ["pre0", "pre1"] + ["a%s%d" % (k, t) for k in "LOPSZ" for t in range(VIS)])
+
+MAG = float(2 ** 23)
+LN2 = math.log(2.0)
+LEV = 1.9
+TOP = 62.0
+
+
+def R(n, c0, c1, st=1, p0=0, p1=128):
+    return (n, p0, p1, c0, c1, st)
+
+
+def R3(n, c0, c1, k0=0, k1=8):
+    return (n, 0, 128, c0, c1, 1 if k1 - k0 == 8 else 0, k0, k1)
+
+
+def overlap(a, b):
+    if a[2] <= b[1] or b[2] <= a[1] or a[4] <= b[3] or b[4] <= a[3]:
+        return False
+    if a[5] > 1 and a[5] == b[5]:
+        return (a[3] - b[3]) % a[5] == 0
+    return True
+
+
+def rank_program(g, core, T, topo):
+    rank = T.rank_of(core)
+    if rank is None:
+        return
+    A = AluOpType
+    AF = ActivationFunctionType
+    n = len(T.cores)
+    nxt, prv = T.cores[(rank + 1) % n], T.cores[(rank - 1) % n]
+    Q = {"v": g.vector, "s": g.scalar, "p": g.tensor, "g": g, "y": g.sync}
+    QS = {"v": "qv", "s": "qs", "p": "qp", "g": "qg"}
+    cnt = {k: 0 for k in QS}
+    clock = {k: {} for k in Q}
+    hist = {}
+    total = {}
+    nd = [0, 0]
+
+    def ap(r):
+        if r[0] == "ind":
+            return ap(r[1]).indirect(ap(r[2]))
+        if len(r) == 8:
+            return T[r[0]][:, r[3] // 8:r[4] // 8, r[6]:r[7]]
+        if r[5] == 1:
+            return T[r[0]][r[1]:r[2], r[3]:r[4]]
+        return T[r[0]][r[1]:r[2], r[3]:r[4]:r[5]]
+
+    def flat(rs):
+        o = []
+        for r in rs:
+            if isinstance(r, tuple):
+                o += [r[1], r[2]] if r[0] == "ind" else [r]
+        return o
+
+    def sync(q, reads, writes):
+        need = {}
+        for r, w in [(x, False) for x in reads] + [(x, True) for x in writes]:
+            ps = r[0][0] == "P" and r[0][1:].isdigit()
+            for (r2, w2, q2, tok, ck) in hist.get(r[0], []):
+                if q2 == q and q == "p":
+                    continue
+                if (ps and q2 != q) or ((w or w2) and overlap(r, r2)):
+                    if need.get(tok[0], (0, None))[0] < tok[1]:
+                        need[tok[0]] = (tok[1], ck)
+        for s, (v, ck) in sorted(need.items(), key=lambda kv: -len(kv[1][1])):
+            if clock[q].get(s, 0) < v:
+                Q[q].wait_ge(T.sem[s], v)
+                clock[q][s] = v
+                for s2, v2 in ck.items():
+                    if clock[q].get(s2, 0) < v2:
+                        clock[q][s2] = v2
+
+    def note(q, reads, writes, tok, ck):
+        total[tok[0]] = max(total.get(tok[0], 0), tok[1])
+        for r in writes:
+            h = [x for x in hist.get(r[0], []) if not (r[5] == 1 and r[1] <= x[0][1] and x[0][2] <= r[2] and r[3] <= x[0][3] and x[0][4] <= r[4])]
+            hist[r[0]] = h + [(r, True, q, tok, ck)]
+        for r in reads:
+            hist.setdefault(r[0], []).append((r, False, q, tok, ck))
+
+    def op(q, fn, reads, writes):
+        reads, writes = flat(reads), flat(writes)
+        sync(q, reads, writes)
+        cnt[q] += 1
+        fn().then_inc(T.sem[QS[q]], 1)
+        note(q, reads, writes, (QS[q], cnt[q]), dict(clock[q]))
+
+    def dma(q, out, in_, reads, writes, **kw):
+        sync(q, reads, writes)
+        s = "d%d" % nd[0]
+        nd[0] += 1
+        Q[q].dma_start(out, in_, **kw).then_inc(T.sem[s], 16)
+        note("dma", reads, writes, (s, 16), dict(clock[q]))
+
+    def send(dst, pairs, sem, engs):
+        reads = [p[1] for p in pairs]
+        sync("g", reads, [])
+        s = "l%d" % nd[1]
+        nd[1] += 1
+        rid, pid, _e = topo.addr(dst)
+        per = len(engs) // len(pairs)
+        masks = [sum(1 << e for e in engs[i * per:(i + 1) * per]) for i in range(len(pairs))]
+        if len(pairs) == 1:
+            g.remote_dma(ap(pairs[0][0]), ap(pairs[0][1]), T.sem[sem], T.sem[s], pid, rid, masks[0])
+        else:
+            g.remote_dma_fused([RemoteDMATransfer(dst_ids=[DstId(rid=rid, pnc=pid)], dma_engine_mask=masks[i], remote_sem=T.sem[sem],
+                                                  src=ap(pairs[i][1]), dst=ap(pairs[i][0])) for i in range(len(pairs))], local_sem=T.sem[s])
+        note("dma", reads, [], (s, per * len(pairs)), dict(clock["g"]))
+        note("dma", [], [p[0] for p in pairs], (sem, per * len(pairs)), {})
+
+    def sc(x):
+        return ap(x) if isinstance(x, tuple) else x
+
+    def ts(out, in0, s1, o0, s2=None, o1=None):
+        if o1 is None:
+            op("v", lambda: g.vector.tensor_scalar(ap(out), ap(in0), sc(s1), None, o0), [in0, s1], [out])
+        else:
+            op("v", lambda: g.vector.tensor_scalar(ap(out), ap(in0), sc(s1), sc(s2), o0, o1), [in0, s1, s2], [out])
+
+    def tt(out, in0, in1, o):
+        op("v", lambda: g.vector.tensor_tensor(ap(out), ap(in0), ap(in1), o), [in0, in1], [out])
+
+    def cp(out, in_):
+        op("v", lambda: g.vector.tensor_copy(ap(out), ap(in_)), [in_], [out])
+
+    def ms(out, v):
+        op("v", lambda: g.vector.memset(ap(out), v), [], [out])
+
+    def scan(out, d0, d1, init, o0, o1):
+        op("v", lambda: g.vector.tensor_tensor_scan(ap(out), ap(d0), ap(d1), init, o0, o1), [d0, d1], [out])
+
+    def act(out, in_, f=AF.Identity, bias=None, scale=None):
+        kw = {}
+        if bias is not None:
+            kw["bias"] = sc(bias)
+        if scale is not None:
+            kw["scale"] = sc(scale)
+        op("s", lambda: g.scalar.activation(ap(out), ap(in_), f, **kw), [in_, bias, scale], [out])
+
+    def fill(out, v):
+        w = len(range(out[3], out[4], out[5]))
+        act(out, R("XI", 0, w), AF.Identity, v, 0.0)
+
+    def mm(out, l, r, start, stop):
+        op("p", lambda: g.tensor.matmul(ap(out), ap(l), ap(r), start, stop), [l, r], [out])
+
+    def iota(out, pat, base, mult, flag=True):
+        if flag:
+            op("g", lambda: g.iota(ap(out), pat, base, mult, allow_small_or_imprecise_dtypes=True), [], [out])
+        else:
+            op("g", lambda: g.iota(ap(out), pat, base, mult), [], [out])
+
+    def ind(w, o):
+        return ("ind", w, o)
+
+    def to_w(out, z, src, c0, ncol, start, stop):
+        for r in range(16):
+            mm(out, R(z, 15 - r, 143 - r), R(src, c0 + r, c0 + 16 * ncol, 16), start and r == 0, stop and r == 15)
+
+    def idw(i):
+        return R("IDW", 128 * i, 128 * i + 128)
+
+    def pf(i):
+        return R("PF", i, i + 1)
+
+    def expand(buf, b0, off, o0, cfn, sfn, a, b):
+        sfn(R("D1", a, b, 8), a // 8, b // 8)
+        scan(R(buf, b0 + a, b0 + b), R("M8", a, b), R("D1", a, b), 0.0, A.mult, A.add)
+        cfn(R(buf, b0 + a, b0 + b, 8), a // 8, b // 8)
+        scan(R(buf, b0 + 256 + a, b0 + 256 + b), R("M8", a, b), R(buf, b0 + a, b0 + b), 0.0, A.mult, A.add)
+        cp(R("EI", a, b), R(buf, b0 + 256 + a, b0 + 256 + b))
+        ts(R("EJ", a, b), R("EI", a, b), 4095, A.bitwise_and)
+        cp(R(off, o0 + a, o0 + b), R("EJ", a, b))
+
+    engs = topo.engines(core, nxt)
+    engp = topo.engines(core, prv)
+    qn = len(engp) // 4
+
+    dma("y", T.NMI[:], T.nm[:], [], [R("NMI", 0, 256)])
+    for i, src in enumerate((T.c0, T.s0)):
+        for e in range(2):
+            r = R("CSI", 32 * i + 16 * e, 32 * i + 16 * e + 16)
+            dma("y", ap(r), src[e::2, :], [], [r])
+    dma("s", ap(R("OW", 0, 4096)), T.vo[:], [], [R("OW", 0, 4096)])
+    dma("s", ap(R("VW", 0, 4096)), T.vn[:], [], [R("VW", 0, 4096)])
+    iota(R("PI", 0, 1), [[0, 1]], 0, 1, False)
+    iota(R("XI", 0, 192), [[1, 192]], 0, 0)
+    iota(R("M8", 0, 256), [[0, 256]], 1, 0)
+    iota(R("KH", 0, 256), [[-16, 256]], 4080, 0)
+    iota(R3("EQ", 0, 1792), [[0, 224], [0, 8]], 0, 0)
+    ms(R("NW", 0, 1024), 0.0)
+    ts(R("PI", 1, 2), R("PI", 0, 1), 15, A.bitwise_and)
+    ts(R("PI", 2, 3), R("PI", 0, 1), 4, A.logical_shift_right, 1, A.bitwise_and)
+    ts(R("PI", 3, 4), R("PI", 0, 1), 5, A.logical_shift_right)
+    ts(R("PI", 4, 5), R("PI", 0, 1), 63, A.bitwise_and)
+    ms(R("D1", 0, 256), 0.0)
+    cp(R("PF", 0, 5), R("PI", 0, 5))
+    ms(R("NW", 1024, 1536), 0.0)
+    ts(pf(5), pf(0), pf(1), A.subtract, 15.0, A.add)
+    ts(pf(6), pf(1), 0.0, A.is_equal)
+    ts(idw(0), R("XI", 0, 128), pf(0), A.is_equal)
+    ts(R("ZA", 0, 144), R("XI", 0, 144), pf(5), A.is_equal)
+    ms(R("NW", 1536, 4096), 0.0)
+    ts(R("NMB", 0, 256), R("NMI", 0, 256), -256.0, A.add)
+    dma("y", T.NW[0:128:16, 0:4096], T.NMB[:], [R("NMB", 0, 256)], [R("NW", 0, 4096)])
+    dma("y", ap(R("ZL", 0, 512)), T.z0[:], [], [R("ZL", 0, 512)])
+    dma("y", T.XO[:], T.xo[:], [], [R("XO", 0, 512)])
+    fill(R("M8", 0, 256, 8), 0.0)
+    act(R("ZN", 0, 144), R("ZA", 0, 144), scale=pf(6))
+    for d in range(1, 8):
+        act(idw(d), idw(0), scale=math.exp(d))
+    act(idw(8), idw(0), scale=-float(2 ** 25))
+    fill(R("KC", 0, 128), 592.0 * 4096)
+    act(R3("P3", 0, 256, 7, 8), R("XI", 0, 32), AF.Identity, 0.0, 0.0)
+    act(R("ZK", 0, 144), R("ZA", 0, 144), scale=4096.0)
+    act(pf(7), pf(1), bias=4080.0)
+    act(pf(8), pf(2), bias=48.0, scale=64.0)
+    act(pf(9), pf(2), bias=pf(3), scale=4.0)
+    act(R("JT", 0, 32), R("XI", 0, 32), bias=pf(1), scale=16.0)
+    fill(R("RS", 0, 128), 0.0)
+    act(pf(14), pf(8), bias=pf(1))
+    fill(R("STL", 512, 544), 32 * 312.0)
+    fill(R("CB", 0, 32), -3840.0)
+    fill(R("RS", 0, 128, 8), -1e9)
+    fill(R("XH", 0, 64), 1.0)
+    fill(R("WA", 0, 64), 2.0 ** (-LEV / 2))
+    fill(R("WB", 0, 64), 0.0)
+    cp(R("CSF", 0, 64), R("CSI", 0, 64))
+    op("v", lambda: g.vector.transpose(T.CSW[:], T.CSF[:]), [R("CSF", 0, 64)], [R("CSW", 0, 64)])
+    c0fn = lambda o, a, b: cp(o, R("CSW", a, b))
+    s0fn = lambda o, a, b: cp(o, R("CSW", 32 + a, 32 + b))
+    expand("STL", 0, "OFL", 0, c0fn, s0fn, 0, 256)
+
+    def consts_a():
+        cp(R("STL", 0, 256, 8), R("D1", 0, 256, 8))
+        ts(R("PF", 10, 14), R("XI", 0, 4), pf(3), A.is_equal)
+        ts(R("BI", 0, 8), R("XI", 0, 8), pf(9), A.is_equal, 512.0, A.mult)
+        ts(R("ZB", 0, 176), R("XI", 0, 176), pf(14), A.is_equal)
+        scan(R("W64", 0, 64), R("WA", 0, 64), R("WB", 0, 64), 2.0 ** ((TOP + LEV) / 2), A.mult, A.add)
+        ts(R("WC", 0, 64), R("XI", 0, 64), pf(4), A.is_equal)
+        tt(R("WA", 0, 64), R("WC", 0, 64), R("W64", 0, 64), A.mult)
+        ms(R("P2", 128, 416, 9), 2.0 ** TOP)
+        op("v", lambda: g.vector.tensor_reduce(T.WP[:], T.WA[:], AxisListType.X, A.add), [R("WA", 0, 64)], [R("WP", 0, 1)])
+
+    def consts_b():
+        act(idw(9), idw(0), scale=-1.0)
+        for gp in range(4):
+            act(R("ZT", 176 * gp, 176 * gp + 176), R("ZB", 0, 176), scale=pf(10 + gp))
+
+    def consts_c():
+        act(R("JT", 32, 64), R("JT", 0, 32), bias=float(XP))
+        act(R("JT", 64, 80), R("JT", 0, 16), bias=256.0)
+        act(R("JT", 80, 96), R("JT", 16, 32), bias=-256.0)
+        act(R("JT", 96, 128), R("JT", 0, 32), scale=1.0 / 512)
+
+    def consts_t(t):
+        act(R("DL", 0, 16), R("JT", 0, 16), bias=(512.0 * t - XP) / 512, scale=1.0 / 512)
+        act(R("DL", 16, 32), R("JT", 16, 32), bias=(512.0 * t + NXP - 511 - XP) / 512, scale=1.0 / 512)
+
+    iota(R("SB", 1024, 1280), [[0, 256]], 0, 0)
+    iota(R("RID", 0, 512), [[1, 512]], 0, 0)
+    iota(R("NW", XP, NXP), [[1, 2], [2, 256]], -256, 0)
+    iota(R("C256", 0, 128), [[0, 128]], 256, 0)
+    dma("y", T.yn[:], T.C256[:], [R("C256", 0, 128)], [R("yn", 0, 2048)])
+    send(prv, [(R(w, NXP, WEND), R(w, 0, 2048)) for w in ("OW", "VW", "NW")], "pre0", engp[:3 * qn])
+    send(prv, [(R("XN", 0, 512), R("XO", 0, 512))], "pre1", engp[3 * qn:])
+
+    LOG = lambda w: R(w, 0, 4096)
+    ALL = lambda w: R(w, 0, WEND)
+    XR = lambda a, b: R("OW", XP + a, XP + b)
+
+    def store_slice(t):
+        a, b = 512 * t, 512 * t + 512
+        dma("g", T.yn[:, a:b], T.NW[0:128:16, a:b], [R("NW", a, b), R("yn", 0, 2048)], [], accum_op=A.add)
+        dma("y", T.yv[:, a:b], ap(R("VW", a, b)), [R("VW", a, b)], [])
+        dma("y", T.yo[:, a:b], ap(R("OW", a, b)), [R("OW", a, b)], [])
+
+    def land(t, w):
+        o = R(w, 512 * t + 1, 512 * t + 512, 2)
+        c = 1024 * t + {"OW": 256, "NW": 512, "VW": 768}[w]
+        (cp if w == "VW" else act)(o, R("LND", c, c + 256))
+
+    for t in range(VIS):
+        last = t == VIS - 1
+        sb = STW * t
+        SREP = lambda a, b, st=1: R("STL", sb + a, sb + b, st)
+        ERAW = lambda a, b, st=1: R("STL", sb + 256 + a, sb + 256 + b, st)
+        AFL = R("STL", sb + 512, sb + 544)
+        Z = lambda a, b: R("ZL", 512 * t + a, 512 * t + b)
+        OFF = lambda a, b: R("OFL", 256 * t + a, 256 * t + b)
+        NP = lambda h, a, b, k0=0, k1=8: R3("P%d" % h, a, b, k0, k1)
+        LM = lambda h, k1=8: R3("P3", 128 * h, 128 * h + 128, 0, k1)
+        KEY = lambda h, a, b: R("P%d" % (4 + h), a, b)
+        E = lambda h, d, k0: R3("EQ", 896 * h + 128 * (d - 1), 896 * h + 128 * d, k0, 8)
+
+        def ngv(i):
+            cp(R("NG", 512 * i, 512 * i + 512), ind(LOG("NW"), OFF(32 * i, 32 * i + 32)))
+
+        def ngs(i):
+            act(R("NG", 512 * i, 512 * i + 512), ind(LOG("NW"), OFF(32 * i, 32 * i + 32)))
+
+        def npe(c):
+            to_w(NP(c // 2, 64 * (c % 2), 64 * (c % 2) + 64), "ZN", "NG", 1024 * c, 64, True, True)
+
+        def og(c, a=0, b=1024):
+            act(R("OG", 1024 * c + a, 1024 * c + b), ind(LOG("OW"), OFF(64 * c + a // 16, 64 * c + b // 16)))
+
+        def ogv(c, a=0, b=1024):
+            cp(R("OG", 1024 * c + a, 1024 * c + b), ind(LOG("OW"), OFF(64 * c + a // 16, 64 * c + b // 16)))
+
+        def eq(h):
+            cp(R3("NS", 0, 128), NP(h, 0, 128))
+            for d in range(1, 8):
+                tt(E(h, d, d), NP(h, 0, 128, 0, 8 - d), R3("NS", 0, 128, d, 8), A.is_equal)
+            for d in range(1, 8):
+                mm(LM(h, 8 - d), idw(d), E(h, d, d), d == 1, d == 7)
+            mm(KEY(h, 0, 128), idw(0), R("KH", 128 * h, 128 * h + 128), True, False)
+            mm(KEY(h, 0, 128), idw(0), R("KC", 0, 128), False, False)
+            for d in range(1, 8):
+                mm(KEY(h, 0, 128), idw(8), E(h, d, 0), False, False)
+
+        def ln(h):
+            act(R("LY", 128 * h, 128 * h + 128), LM(h), AF.Ln, math.exp(-0.23), math.exp(-0.23))
+
+        def el(h):
+            a, b = 128 * h, 128 * h + 128
+            ts(R("P7", 0, 128), R("LY", a, b), MAG, A.add, MAG, A.subtract)
+            tt(R("P7", 128, 256), R("P7", 0, 128), SREP(a, b), A.mult)
+            tt(R("EI", a, b), R("P7", 128, 256), ERAW(a, b), A.add)
+            ts(R("EJ", a, b), R("EI", a, b), 4095, A.bitwise_and)
+            cp(R("OFE", a, b), R("EJ", a, b))
+
+        def dg(a, b):
+            tt(R("DD", a, b), ind(LOG("VW"), R("OFE", a // 16, b // 16)), R("OG", a, b), A.subtract)
+
+        def ab(a, b):
+            act(R("AD", a, b), R("DD", a, b), AF.Abs)
+
+        def kpe(c):
+            to_w(KEY(c // 2, 64 * (c % 2), 64 * (c % 2) + 64), "ZK", "AD", 1024 * c, 64, False, c % 2 == 1)
+
+        def kscan(h):
+            scan(R("KS", 128 * h, 128 * h + 128), R("RS", 0, 128), KEY(h, 0, 128), 0.0, A.add, A.max)
+
+        def pick(hh, part):
+            a, b = 16 * hh, 16 * hh + 16
+            if part == 0:
+                cp(R("KI", a, b), R("KS", 8 * a + 7, 8 * b, 8))
+            elif part == 1:
+                ts(R("KX", a, b), R("KI", a, b), 4095, A.bitwise_and)
+            elif part == 2:
+                ts(R("OFD", a, b), R("KX", a, b), -1.0, A.mult, pf(7), A.add)
+            elif part == 3:
+                tt(R("GG", 16 * a, 16 * b), ind(R("AD", 0, 2048 * hh + 2048), R("OFD", a, b)), Z(16 * a, 16 * b), A.is_lt)
+            else:
+                if hh == 0:
+                    mm(R("P6", 128, 160), idw(0), R("CB", 0, 32), True, False)
+                for sub in range(4 * hh, 4 * hh + 4):
+                    for e in range(2):
+                        mm(R("P6", 128 + 4 * sub, 132 + 4 * sub, 1, 64 * e, 64 * e + 64), R("GG", 64 * sub, 64 * sub + 64),
+                           R("BI", 4 * e, 4 * e + 4), False, sub == 7)
+
+        ngv(0); ngs(1); npe(0)
+        ngv(2); ngs(3); npe(1)
+        if t == 0:
+            consts_a()
+        else:
+            land(t - 1, "OW")
+            land(t - 1, "VW")
+        ngv(4)
+        og(0); og(1, 0, 512)
+        eq(0)
+        ngv(6)
+        ln(0)
+        og(1, 512, 1024)
+        el(0)
+        ngs(5); npe(2); ngs(7); npe(3)
+        if t > 0:
+            store_slice(t - 1)
+        dg(0, 1024)
+        og(2)
+        eq(1)
+        ab(0, 1024); kpe(0)
+        dg(1024, 2048)
+        ln(1)
+        og(3)
+        el(1)
+        ab(1024, 2048); kpe(1)
+        dg(2048, 3072)
+        ab(2048, 3072); kpe(2)
+        dg(3072, 3584); ab(3072, 3584)
+        dg(3584, 3840); ab(3584, 3840)
+        dg(3840, 4096); ab(3840, 4096); kpe(3)
+        if t == 0:
+            consts_b()
+        kscan(0)
+        if t == 0:
+            cp(XR(256, 512), R("XN", 1, 512, 2))
+            cp(XR(0, 256), R("XO", 0, 512, 2))
+        else:
+            act(XR(0, 256), ind(R("SB", 768, 1792), R("OF3", 0, 16)))
+        act(R("ZH", 0, 512), Z(0, 512), AF.Identity, -0.5)
+        if t == 0:
+            consts_c()
+        consts_t(t)
+        for part in range(4):
+            pick(0, part)
+        cp(R("SB", 1280, 1536), XR(256, 512))
+        cp(R("SB", 1536, 1792), XR(0, 256))
+        kscan(1)
+        pick(0, 4)
+        ts(R("UI", 0, 32), R("KS", 7, 256, 8), 1.0 / 4096, A.mult, -0.498, A.add)
+        pick(1, 0)
+        tt(R("T1", 0, 32), R("UI", 0, 32), R("UI", 0, 32), A.mult)
+        pick(1, 1)
+        tt(R("T5", 0, 32), R("T1", 0, 32), AFL, A.add)
+        pick(1, 2)
+        act(R("DFW", 0, 512), ind(R("DD", 0, 4096), R("OFD", 0, 32)))
+        ts(R("AB", 0, 32), R("T5", 0, 32), 5, A.logical_shift_right, 30, A.bitwise_and)
+        ts(R("AB", 32, 64), R("T5", 0, 32), 5, A.logical_shift_right, 481, A.bitwise_and)
+        ts(R("ABB", 0, 64), R("AB", 0, 64), -240.0, A.add)
+        for gp in range(4):
+            for w in range(4):
+                mm(R("P7", 256 + gp, 320, 4), R("ZT", 176 * gp + 48 - 16 * w, 176 * gp + 176 - 16 * w), R("ABB", w, 64, 4), w == 0, w == 3)
+        pick(1, 3)
+        pick(1, 4)
+        act(R("ZW", 0, 512), Z(0, 512), AF.Relu, -1.0)
+        mm(R3("P1", 0, 256), idw(0), R("VW", 512 * t, 512 * t + 512, 2), True, False)
+        mm(R3("P1", 0, 256), idw(9), XR(0, 256), False, True)
+        mm(R3("P1", 256, 512), idw(0), R("VW", NXP + 512 * t + 1, NXP + 512 * t + 512, 2), True, False)
+        mm(R3("P1", 256, 512), idw(9), XR(256, 512), False, True)
+        act(R("DFW", 512, 1024), R3("P1", 0, 512))
+        ts(R("T7", 0, 32), R("AB", 32, 64), 513.0, A.mult)
+        ts(R("YI", 0, 32), R("KX", 0, 32), 4, A.logical_shift_right, 7, A.bitwise_and)
+        ts(R("T8", 0, 32), R("UI", 0, 32), 432.0, A.add)
+        ts(R("AT", 0, 32), R("P7", 256, 288), 16.0, A.mult, 3600.0, A.add)
+        cp(R("XH", 64, 128, 2), R("P7", 288, 320))
+        ts(R("XH", 65, 128, 2), R("P7", 288, 320), -1.0, A.add)
+        for e in range(2):
+            tt(R("XH", e, 64, 2, 64 * e, 64 * e + 64), R("P6", 128, 160, 1, 64 * e, 64 * e + 64), R("AT", 0, 32, 1, 64 * e, 64 * e + 64), A.max)
+        for v in range(16):
+            ts(R("OH", v, 2048, 16), R("XH", 0, 128), 32.0 * v - 240, A.is_equal, R("WP", 0, 1), A.mult)
+        for sub in range(8):
+            for gp in range(4):
+                i = 4 * sub + gp
+                mm(R("P2", 136 - sub, 416, 9, 32 * gp, 32 * gp + 32), R("OH", 32 * i, 32 * i + 32), R("OH", 1024 + 32 * i, 1056 + 32 * i), True, True)
+        to_w(R("P6", 0, 32), "ZA", "GG", 0, 32, True, True)
+        act(R("HY", 0, 288), R("P2", 128, 416), AF.Ln, 2.0 ** (TOP - 64 * LEV))
+        act(R("HQ", 0, 288), R("HY", 0, 288), AF.Identity, TOP / LEV, -1.0 / (LEV * LN2))
+        ts(R("T6", 0, 32), R("T7", 0, 32), 5, A.logical_shift_right, 31, A.bitwise_and)
+        ts(R("YS", 0, 32), R("T8", 0, 32), 511, A.bitwise_and)
+        ts(R("T3", 0, 32), SREP(0, 256, 8), 8.0, A.mult)
+        tt(R("DC", 0, 32), R("YI", 0, 32), SREP(0, 256, 8), A.mult)
+        tt(R("Z1", 0, 512), ind(R("AD", 0, 4096), R("OFD", 0, 32)), R("ZH", 0, 512), A.add)
+        cp(R("OFB", 0, 32), R("T6", 0, 32))
+        ts(R("SA", 0, 32), R("YS", 0, 32), 2.0, A.mult, 1.0, A.add)
+        tt(R("T4", 0, 32), R("T3", 0, 32), ERAW(0, 256, 8), A.add)
+        ts(R("HE", 0, 288), R("HY", 0, 288), (TOP - 63.5 * LEV) * LN2, A.is_lt)
+        tt(R("DS", 0, 32), R("SA", 0, 32), SREP(0, 256, 8), A.subtract)
+        tt(R("CN", 0, 32), R("T4", 0, 32), R("DC", 0, 32), A.subtract)
+        act(R("Z2", 0, 512), R("Z1", 0, 512), AF.Identity, MAG, 0.5)
+        act(R("ZW", 512, 1024), R("Z2", 0, 512), AF.Identity, -MAG)
+        scan(R("HS", 0, 288), R("HE", 0, 288), R("HQ", 0, 288), 0.0, A.mult, A.add)
+        ts(R("WIN", 0, 32), R("HS", 8, 288, 9), MAG, A.add, MAG, A.subtract)
+        ts(R("UU", 0, 32), R("HS", 8, 288, 9), 511.5, A.is_ge, 512.0, A.mult)
+
+        def acts(a, b, bank):
+            tt(R("AQ", 16 * a, 16 * b), ind(R("WIN", 0, 32), R("OFB", a, b)), R("RID", 16 * a, 16 * b), A.is_equal)
+            to_w(R(bank, a, b), "ZA", "AQ", 16 * a, b - a, True, True)
+        if not last:
+            acts(0, 32, "P2")
+        tt(R("U2", 0, 32), R("UU", 0, 32), R("DL", 0, 32), A.mult)
+        tt(R("R1", 0, 32), R("UU", 0, 32), R("JT", 96, 128), A.mult)
+        tt(R("U3", 0, 32), R("U2", 0, 32), R("JT", 32, 64), A.add)
+        tt(R("R2", 0, 32), R("R1", 0, 32), R("WIN", 0, 32), A.add)
+        cp(R("OF2", 0, 32), R("U3", 0, 32))
+        cp(R("OF1", 0, 32), R("R2", 0, 32))
+        act(R("SB", 512, 768), ind(ALL("NW"), R("OF2", 16, 32)))
+        act(R("SB", 256, 512), ind(ALL("OW"), R("OF2", 16, 32)))
+        lb = 1024 * t
+        tt(R("VT", 256, 512), ind(R("DFW", 0, 1024), R("OF1", 16, 32)), XR(256, 512), A.add)
+
+        def of3():
+            tt(R("U4", 0, 32), R("UU", 0, 32), R("JT", 64, 96), A.add)
+            cp(R("OF3", 0, 32), R("U4", 0, 32))
+        ACT = R("P2", 0, 32)
+        if last:
+            of3()
+        else:
+            tt(R("R3", 0, 32), ACT, R("DS", 0, 32), A.mult)
+        ts(R("SB", 768, 1024), R("VT", 256, 512), 0.0, A.max, 255.0, A.min)
+        if last:
+            cp(R("SB", 0, 256), ind(R("SB", 768, 1536), R("OF3", 16, 32)))
+            send(nxt, [(R("LND", lb, lb + 1024), R("SB", 0, 1024))], "aL%d" % t, engs)
+            acts(0, 32, "P2")
+            tt(R("R3", 0, 32), ACT, R("DS", 0, 32), A.mult)
+        else:
+            send(nxt, [(R("LND", lb + 256, lb + 1024), R("SB", 256, 1024))], "aL%d" % t, engs)
+        act(R("NE", 0, 256), ind(ALL("NW"), R("OF2", 0, 16)))
+        act(R("OE", 0, 256), ind(ALL("OW"), R("OF2", 0, 16)))
+        ev = lambda w: R(w, 512 * t, 512 * t + 512, 2)
+        act(ev("NW"), R("NE", 0, 256))
+        act(ev("OW"), R("OE", 0, 256))
+        tt(R("R4", 0, 32), ACT, R("DC", 0, 32), A.mult)
+        cfn = lambda o, a, b: tt(o, R("R4", a, b), R("CN", a, b), A.add)
+        sfn = lambda o, a, b: tt(o, R("R3", a, b), SREP(8 * a, 8 * b, 8), A.add)
+        if not last:
+            ob = 256 * t + 256
+            expand("SST", 0, "SOF", 0, cfn, sfn, 0, 128)
+            send(nxt, [(R("OFL", ob, ob + 128), R("SOF", 0, 128))], "aO%d" % t, engs)
+            aout = R("SST", 512, 544)
+        else:
+            cfn(R("FC", 0, 32), 0, 32)
+            sfn(R("FO", 32, 64), 0, 32)
+            aout = R("FO", 64, 96)
+        ts(R("ACT", 0, 32), ACT, 512.0, A.mult)
+        ts(R("FI", 0, 32), R("P6", 0, 32), 7.5, A.is_lt, 1.0 if last else 32.0, A.mult)
+        tt(R("R5", 0, 32), R("ACT", 0, 32), R("JT", 0, 32), A.add)
+        if last:
+            tt(aout, R("FI", 0, 32), ACT, A.subtract)
+        else:
+            ts(R("R2", 0, 32), ACT, -32.0, A.mult, 32 * 312.0, A.add)
+            tt(aout, R("FI", 0, 32), R("R2", 0, 32), A.add)
+        cp(R("OFZ", 0, 32), R("R5", 0, 32))
+        act(R("ZS", 0, 512), ind(R("ZW", 0, 1024), R("OFZ", 0, 32)))
+        if not last:
+            of3()
+            act(XR(256, 512), ind(R("SB", 768, 1536), R("OF3", 16, 32)))
+            expand("SST", 0, "SOF", 0, cfn, sfn, 128, 256)
+            send(nxt, [(R("OFL", ob + 128, ob + 256), R("SOF", 128, 256))], "aP%d" % t, engs)
+            cp(R("SST", 0, 256, 8), R("D1", 0, 256, 8))
+            send(nxt, [(R("STL", sb + STW, sb + 2 * STW), R("SST", 0, STW))], "aS%d" % t, engs)
+            send(nxt, [(R("ZL", 512 * t + 512, 512 * t + 1024), R("ZS", 0, 512))], "aZ%d" % t, engs)
+            land(t, "NW")
+        else:
+            dma("y", T.yz[:], T.ZS[:], [R("ZS", 0, 512)], [])
+            ts(R("FD", 0, 32), R("FC", 0, 32), 4095, A.bitwise_and)
+            cp(R("FO", 0, 32), R("FD", 0, 32))
+            op("v", lambda: g.vector.transpose(T.FT[:], T.FO[:]), [R("FO", 0, 96)], [R("FT", 0, 96)])
+            for i, dst in enumerate((T.yc, T.ys, T.ya)):
+                for e in range(2):
+                    r = R("FT", 32 * i + 16 * e, 32 * i + 16 * e + 16)
+                    dma("y", dst[e::2, :], ap(r), [r], [])
+        tt(R("VT", 0, 256), ind(R("DFW", 0, 1024), R("OF1", 0, 16)), XR(0, 256), A.add)
+        ts(R("SB", 1024, 1280), R("VT", 0, 256), 0.0, A.max, 255.0, A.min)
+        ts(ev("VW"), R("VT", 0, 256), 0.0, A.max, 255.0, A.min)
+        if last:
+            cp(R("OE", 0, 256), ind(R("SB", 768, 1792), R("OF3", 0, 16)))
+            land(t, "NW")
+            land(t, "OW")
+            cp(R("YX", 0, 512, 2), R("OE", 0, 256))
+            land(t, "VW")
+            cp(R("YX", 1, 512, 2), R("LND", lb, lb + 256))
+            dma("s", T.yx[:], T.YX[:], [R("YX", 0, 512)], [])
+            store_slice(t)
+
+    for s, v in total.items():
+        if clock["g"].get(s, 0) < v:
+            g.wait_ge(T.sem[s], v)

@@ -1,56 +1,60 @@
 import math
+import numpy as np
 from concourse.bass import DstId, RemoteDMATransfer
-from concourse.mybir import AluOpType, AxisListType, ActivationFunctionType
+from concourse.mybir import AluOpType, ActivationFunctionType
 
 VIS = 4
-XP, NXP, WEND = 4096, 4608, 6656
-STW = 544
 BF, F32, I32, U16 = "bfloat16", "float32", "int32", "uint16"
 
 SCRATCH = {}
 for _d, _l in (
-    (BF, dict(OW=WEND, VW=WEND, NW=WEND, NG=4096, OG=4096, DD=4096, AD=4096, ZL=4 * 512, LND=4 * 1024, ZS=512, SB=1792,
-              XO=512, XN=512, YX=512, NMB=256, IDW=10 * 128, ZA=144, ZN=144, ZK=144, ZB=176, ZT=4 * 176, BI=8, KH=256,
-              KC=128, CB=32, EQ=2 * 7 * 128, ABB=64, GG=512, XH=128, OH=2048, AQ=512, DFW=1024, VT=512, OE=256, NE=256, ZW=1024)),
-    (F32, dict(STL=4 * STW, SST=STW, CSF=64, CSW=64, PF=16, XI=192, RS=128, M8=256, D1=256, W64=64, WA=64, WB=64, WC=64, WP=1,
-               JT=128, DL=128, RID=512, C256=128, NS=128, LY=256, KS=256, T3=32, T4=32, AT=32, HY=288, HQ=288, HE=288, HS=288,
-               WIN=32, UU=32, U2=32, U3=32, U4=32, DC=32, CN=32, DS=32, SA=32, FI=32, ACT=32, R1=32, R2=32, R3=32, R4=32, R5=32,
-               ZH=512, Z1=512, Z2=512, FO=96, FT=96)),
-    (I32, dict(NMI=256, CSI=64, PI=8, EI=256, EJ=256, KI=32, KX=32, UI=32, T1=32, T2=32, T5=32, T6=32, T7=32, T8=32, AB=64,
-               YI=32, YS=32, FC=32, FD=32)),
-    (U16, dict(OFL=4 * 256, SOF=256, OFE=256, OFD=32, OFB=32, OF1=32, OF2=32, OF3=32, OFZ=32)),
+    (BF, dict(OW0=4096, OW1=4096, OW2=4096, OW3=4096, VW0=4096, VW1=4096, VW2=4096, VW3=4096, NW=4096, NR=4096, NG=4096, OG=4096,
+              DD=4096, AD=4096, SN=1536, XB=23 * 512, DFW=576, BB=512, ZW=1024, ZZ=512, ZL=512, NMB=5 * 256, YO=2048, YV=2048, YX=512,
+              FL=64, FR=5 * 32, IDW=12 * 128, SEL=48, ZA=144, CK=128, C128=128, A16=32, A64=32, CB=64, ONE=512, QM=128,
+              EQ=(224, 8), LY=256, DP=(36, 4), DQ=(36, 4), GG=512, XH=128, OH=16 + 2048, AQ=512, HQ=128, FI=32, VT=512)),
+    (F32, dict(XD=144, XI=48, TB=128, SO=192, SP=128, EX=512, ES=512, PF=16, LF=128, YY=128, XS=64, XF=128, SR=256, NS=(16, 8), RS=128,
+               KS=256, W8=32, SQ=32, FC=32, F7=32, T3=32, T4=32, DX=64, PR=64, YH=256, LL=128, LH=128, HS=128, HM=128, DS=128, MS=128,
+               WIN=32, RID=512, Z2=512, C256=128, FO=256, FN=256, WP=1)),
+    (I32, dict(NMI=256, LI=128, PI=8, EI=256, EJ=256, EK=256, EL=256, T5=32, T8=32, SA=32, AB=64, CI=64, CJ=64)),
+    (U16, dict(OFF=256, OFE=256, OFD=32, OFB=32, OF1=32, OFS=32, OFZ=32)),
 ):
     for _k, _n in _l.items():
-        SCRATCH[_k] = ("sbuf", [128, _n], _d)
-ROWS = ("P0", "P1", "P3", "NS", "EQ")
-for _i in range(8):
-    SCRATCH["P%d" % _i] = ("psum", [128, 512], F32)
-for _k in ROWS:
-    SCRATCH[_k] = (SCRATCH[_k][0], [128, SCRATCH[_k][1][1] // 8, 8], SCRATCH[_k][2])
+        SCRATCH[_k] = ("sbuf", [128] + (list(_n) if isinstance(_n, tuple) else [_n]), _d)
+for _i, _s in enumerate(((64, 8), (64, 8), (64, 8), (2, 256), (2, 256), (512,), (128, 4), (512,))):
+    SCRATCH["P%d" % _i] = ("psum", [128] + list(_s), F32)
 
-SEMAPHORES = (["qv", "qs", "qp", "qg"] + ["d%d" % i for i in range(40)] + ["l%d" % i for i in range(24)]
-              + ["pre0", "pre1"] + ["a%s%d" % (k, t) for k in "LOPSZ" for t in range(VIS)])
+SEMAPHORES = (["qv", "qs", "qp", "qg"] + ["d%d" % i for i in range(48)] + ["l%d" % i for i in range(32)] + ["a%d" % i for i in range(32)])
 
-MAG = float(2 ** 23)
-LN2 = math.log(2.0)
-LEV = 1.9
-TOP = 62.0
+MAG = float(3 * 2 ** 22)
+STEP = 1.75
+MASKS = {}
 
 
 def R(n, c0, c1, st=1, p0=0, p1=128):
-    return (n, p0, p1, c0, c1, st)
+    sh = SCRATCH[n][1] if n in SCRATCH else [128, 4096]
+    if len(sh) == 3:
+        w = sh[2]
+        if c0 // w == (c1 - 1) // w:
+            return mk(n, p0, p1, (c0 // w, slice(c0 % w, (c1 - 1) % w + 1, st)))
+        if st == 1:
+            return R3(n, c0 // w, c1 // w, 0, w, p0, p1)
+        return mk(n, p0, p1, (slice(c0 // w, (c1 + w - 1) // w, st // w), c0 % w))
+    return mk(n, p0, p1, (slice(c0, c1, st),))
 
 
-def R3(n, c0, c1, k0=0, k1=8):
-    return (n, 0, 128, c0, c1, 1 if k1 - k0 == 8 else 0, k0, k1)
+def R3(n, a0, a1, k0, k1, p0=0, p1=128):
+    return mk(n, p0, p1, (slice(a0, a1), slice(k0, k1)))
 
 
-def overlap(a, b):
-    if a[2] <= b[1] or b[2] <= a[1] or a[4] <= b[3] or b[4] <= a[3]:
-        return False
-    if a[5] > 1 and a[5] == b[5]:
-        return (a[3] - b[3]) % a[5] == 0
-    return True
+def mk(n, p0, p1, idx):
+    sh = SCRATCH[n][1][1:] if n in SCRATCH else [4096]
+    key = (tuple(sh), str(idx))
+    if key not in MASKS:
+        cols = np.arange(int(np.prod(sh))).reshape(sh)[idx].reshape(-1)
+        bits = np.zeros(int(np.prod(sh)), np.uint8)
+        bits[cols] = 1
+        MASKS[key] = int.from_bytes(np.packbits(bits, bitorder="little").tobytes(), "little")
+    return (n, p0, p1, idx, MASKS[key])
 
 
 def rank_program(g, core, T, topo):
@@ -60,7 +64,7 @@ def rank_program(g, core, T, topo):
     A = AluOpType
     AF = ActivationFunctionType
     n = len(T.cores)
-    nxt, prv = T.cores[(rank + 1) % n], T.cores[(rank - 1) % n]
+    peer = lambda d: T.cores[(rank + d) % n]
     Q = {"v": g.vector, "s": g.scalar, "p": g.tensor, "g": g, "y": g.sync}
     QS = {"v": "qv", "s": "qs", "p": "qp", "g": "qg"}
     cnt = {k: 0 for k in QS}
@@ -72,11 +76,7 @@ def rank_program(g, core, T, topo):
     def ap(r):
         if r[0] == "ind":
             return ap(r[1]).indirect(ap(r[2]))
-        if len(r) == 8:
-            return T[r[0]][:, r[3] // 8:r[4] // 8, r[6]:r[7]]
-        if r[5] == 1:
-            return T[r[0]][r[1]:r[2], r[3]:r[4]]
-        return T[r[0]][r[1]:r[2], r[3]:r[4]:r[5]]
+        return T[r[0]][(slice(r[1], r[2]),) + r[3]]
 
     def flat(rs):
         o = []
@@ -92,7 +92,7 @@ def rank_program(g, core, T, topo):
             for (r2, w2, q2, tok, ck) in hist.get(r[0], []):
                 if q2 == q and q == "p":
                     continue
-                if (ps and q2 != q) or ((w or w2) and overlap(r, r2)):
+                if (ps and q2 != q) or ((w or w2) and r[1] < r2[2] and r2[1] < r[2] and r[4] & r2[4]):
                     if need.get(tok[0], (0, None))[0] < tok[1]:
                         need[tok[0]] = (tok[1], ck)
         for s, (v, ck) in sorted(need.items(), key=lambda kv: -len(kv[1][1])):
@@ -106,7 +106,7 @@ def rank_program(g, core, T, topo):
     def note(q, reads, writes, tok, ck):
         total[tok[0]] = max(total.get(tok[0], 0), tok[1])
         for r in writes:
-            h = [x for x in hist.get(r[0], []) if not (r[5] == 1 and r[1] <= x[0][1] and x[0][2] <= r[2] and r[3] <= x[0][3] and x[0][4] <= r[4])]
+            h = [x for x in hist.get(r[0], []) if not (r[1] <= x[0][1] and x[0][2] <= r[2] and x[0][4] & ~r[4] == 0)]
             hist[r[0]] = h + [(r, True, q, tok, ck)]
         for r in reads:
             hist.setdefault(r[0], []).append((r, False, q, tok, ck))
@@ -125,21 +125,25 @@ def rank_program(g, core, T, topo):
         Q[q].dma_start(out, in_, **kw).then_inc(T.sem[s], 16)
         note("dma", reads, writes, (s, 16), dict(clock[q]))
 
-    def send(dst, pairs, sem, engs):
-        reads = [p[1] for p in pairs]
+    def send(items):
+        reads = [p[2] for p in items]
         sync("g", reads, [])
-        s = "l%d" % nd[1]
+        s, sem = "l%d" % nd[1], "a%d" % nd[1]
         nd[1] += 1
-        rid, pid, _e = topo.addr(dst)
-        per = len(engs) // len(pairs)
-        masks = [sum(1 << e for e in engs[i * per:(i + 1) * per]) for i in range(len(pairs))]
-        if len(pairs) == 1:
-            g.remote_dma(ap(pairs[0][0]), ap(pairs[0][1]), T.sem[sem], T.sem[s], pid, rid, masks[0])
+        trs = []
+        for i, (d, land, src) in enumerate(items):
+            engs = topo.engines(core, peer(d))
+            per = 1 << int(math.log2(len(engs) // len(items)))
+            rid, pid, _e = topo.addr(peer(d))
+            trs.append((rid, pid, sum(1 << e for e in engs[i * per:(i + 1) * per]), ap(land), ap(src)))
+        if len(items) == 1:
+            rid, pid, mask, land, src = trs[0]
+            g.remote_dma(land, src, T.sem[sem], T.sem[s], pid, rid, mask)
         else:
-            g.remote_dma_fused([RemoteDMATransfer(dst_ids=[DstId(rid=rid, pnc=pid)], dma_engine_mask=masks[i], remote_sem=T.sem[sem],
-                                                  src=ap(pairs[i][1]), dst=ap(pairs[i][0])) for i in range(len(pairs))], local_sem=T.sem[s])
-        note("dma", reads, [], (s, per * len(pairs)), dict(clock["g"]))
-        note("dma", [], [p[0] for p in pairs], (sem, per * len(pairs)), {})
+            g.remote_dma_fused([RemoteDMATransfer(dst_ids=[DstId(rid=rid, pnc=pid)], dma_engine_mask=mask, remote_sem=T.sem[sem], src=src, dst=land)
+                                for rid, pid, mask, land, src in trs], local_sem=T.sem[s])
+        note("dma", reads, [], (s, per * len(items)), dict(clock["g"]))
+        note("dma", [], [p[1] for p in items], (sem, per * len(items)), {})
 
     def sc(x):
         return ap(x) if isinstance(x, tuple) else x
@@ -159,6 +163,9 @@ def rank_program(g, core, T, topo):
     def ms(out, v):
         op("v", lambda: g.vector.memset(ap(out), v), [], [out])
 
+    def tr(out, in_):
+        op("v", lambda: g.vector.transpose(ap(out), ap(in_)), [in_], [out])
+
     def scan(out, d0, d1, init, o0, o1):
         op("v", lambda: g.vector.tensor_tensor_scan(ap(out), ap(d0), ap(d1), init, o0, o1), [d0, d1], [out])
 
@@ -170,9 +177,8 @@ def rank_program(g, core, T, topo):
             kw["scale"] = sc(scale)
         op("s", lambda: g.scalar.activation(ap(out), ap(in_), f, **kw), [in_, bias, scale], [out])
 
-    def fill(out, v):
-        w = len(range(out[3], out[4], out[5]))
-        act(out, R("XI", 0, w), AF.Identity, v, 0.0)
+    def fill(out, w, v):
+        act(out, R("XD", 0, w), AF.Identity, v, 0.0)
 
     def mm(out, l, r, start, stop):
         op("p", lambda: g.tensor.matmul(ap(out), ap(l), ap(r), start, stop), [l, r], [out])
@@ -183,409 +189,427 @@ def rank_program(g, core, T, topo):
         else:
             op("g", lambda: g.iota(ap(out), pat, base, mult), [], [out])
 
-    def ind(w, o):
-        return ("ind", w, o)
+    def asel(out, in_, cmp, fillv, base):
+        op("g", lambda: g.affine_select(ap(out), ap(in_), [[-32, 4], [-2, 16], [0, 8]], cmp, fillv, base, 1), [in_], [out])
 
-    def to_w(out, z, src, c0, ncol, start, stop):
-        for r in range(16):
-            mm(out, R(z, 15 - r, 143 - r), R(src, c0 + r, c0 + 16 * ncol, 16), start and r == 0, stop and r == 15)
+    ind = lambda w, o: ("ind", w, o)
+    idw = lambda i, a=0, st=1: R("IDW", 128 * i + a, 128 * i + 128, st)
+    pf = lambda i: R("PF", i, i + 1)
+    blk = lambda b, k=1: R("XB", 512 * b, 512 * (b + k))
+    rows = lambda w, a, b: T[w][0:128:16, a:b]
+    I1, IPEN, INEG, I4, IHALF = 0, 8, 9, 10, 11
+    SELN, SELK, SELA, SELM = R("SEL", 0, 8), R("SEL", 8, 16), R("SEL", 16, 32), R("SEL", 32, 40)
+    CC, SS = R("XS", 0, 64, 2), R("XS", 1, 64, 2)
+    CNT, AFL = R("P5", 128, 160), R("P5", 160, 192)
+    sub5 = lambda c0, s: R("P5", c0 + 16 * (s >> 1) + (s & 1), c0 + 16 * (s >> 1) + 16, 2)
+    A16 = R("A16", 0, 32)
 
-    def idw(i):
-        return R("IDW", 128 * i, 128 * i + 128)
+    def places():
+        for i in range(4):
+            mm(R3("P3", 0, 2, 32 * i, 32 * i + 32), R("EX", 128 * i, 128 * i + 128), R("YY", 0, 64), True, True)
 
-    def pf(i):
-        return R("PF", i, i + 1)
+    def strides():
+        for i in range(4):
+            mm(R3("P4", 0, 2, 32 * i, 32 * i + 32), R("ES", 128 * i, 128 * i + 128), R("YY", 0, 64), True, True)
 
-    def expand(buf, b0, off, o0, cfn, sfn, a, b):
-        sfn(R("D1", a, b, 8), a // 8, b // 8)
-        scan(R(buf, b0 + a, b0 + b), R("M8", a, b), R("D1", a, b), 0.0, A.mult, A.add)
-        cfn(R(buf, b0 + a, b0 + b, 8), a // 8, b // 8)
-        scan(R(buf, b0 + 256 + a, b0 + 256 + b), R("M8", a, b), R(buf, b0 + a, b0 + b), 0.0, A.mult, A.add)
-        cp(R("EI", a, b), R(buf, b0 + 256 + a, b0 + 256 + b))
-        ts(R("EJ", a, b), R("EI", a, b), 4095, A.bitwise_and)
-        cp(R(off, o0 + a, o0 + b), R("EJ", a, b))
+    def offsets():
+        for h in range(2):
+            cp(R("EI", 128 * h, 128 * h + 128), R("P3", 256 * h, 256 * h + 128))
+        for a in (0, 128):
+            ts(R("EJ", a, a + 128), R("EI", a, a + 128), 4095, A.bitwise_and)
+        for a in (0, 128):
+            cp(R("OFF", a, a + 128), R("EJ", a, a + 128))
 
-    engs = topo.engines(core, nxt)
-    engp = topo.engines(core, prv)
-    qn = len(engp) // 4
+    def t_to_w(out, buf, w, start):
+        for i in range(4):
+            mm(out, R3(buf, 3 - i, 35 - i, 0, 4), idw(w, i, 4), start and i == 0, i == 3)
+
+    padded = lambda buf, h: mk(buf, 0, 128, (slice(3, 35, 4), slice(2 * h, 2 * h + 2)))
 
     dma("y", T.NMI[:], T.nm[:], [], [R("NMI", 0, 256)])
-    for i, src in enumerate((T.c0, T.s0)):
-        for e in range(2):
-            r = R("CSI", 32 * i + 16 * e, 32 * i + 16 * e + 16)
-            dma("y", ap(r), src[e::2, :], [], [r])
-    dma("s", ap(R("OW", 0, 4096)), T.vo[:], [], [R("OW", 0, 4096)])
-    dma("s", ap(R("VW", 0, 4096)), T.vn[:], [], [R("VW", 0, 4096)])
+    dma("y", T.LI[0:32, :], T.c0[:], [], [R("LI", 0, 128, 1, 0, 32)])
+    dma("y", T.LI[32:64, :], T.s0[:], [], [R("LI", 0, 128, 1, 32, 64)])
+    dma("y", T.OW0[:, 0:2048], T.vo[:, 0:2048], [], [R("OW0", 0, 2048)])
     iota(R("PI", 0, 1), [[0, 1]], 0, 1, False)
-    iota(R("XI", 0, 192), [[1, 192]], 0, 0)
-    iota(R("M8", 0, 256), [[0, 256]], 1, 0)
-    iota(R("KH", 0, 256), [[-16, 256]], 4080, 0)
-    iota(R3("EQ", 0, 1792), [[0, 224], [0, 8]], 0, 0)
-    ms(R("NW", 0, 1024), 0.0)
-    ts(R("PI", 1, 2), R("PI", 0, 1), 15, A.bitwise_and)
-    ts(R("PI", 2, 3), R("PI", 0, 1), 4, A.logical_shift_right, 1, A.bitwise_and)
-    ts(R("PI", 3, 4), R("PI", 0, 1), 5, A.logical_shift_right)
-    ts(R("PI", 4, 5), R("PI", 0, 1), 63, A.bitwise_and)
-    ms(R("D1", 0, 256), 0.0)
-    cp(R("PF", 0, 5), R("PI", 0, 5))
-    ms(R("NW", 1024, 1536), 0.0)
-    ts(pf(5), pf(0), pf(1), A.subtract, 15.0, A.add)
-    ts(pf(6), pf(1), 0.0, A.is_equal)
-    ts(idw(0), R("XI", 0, 128), pf(0), A.is_equal)
-    ts(R("ZA", 0, 144), R("XI", 0, 144), pf(5), A.is_equal)
-    ms(R("NW", 1536, 4096), 0.0)
+    iota(R("XD", 0, 144), [[1, 144]], 0, -1)
+    iota(R("TB", 0, 128), [[1, 4], [4, 8], [32, 4]], 0, -1)
+    iota(R("EX", 0, 512), [[0, 64], [1, 8]], 0, 0)
+    asel(R("EX", 0, 512), R("EX", 0, 512), A.is_equal, 0.0, -1)
+    asel(R("EX", 0, 512), R("EX", 0, 512), A.not_equal, 1.0, 0)
+    iota(R("XI", 0, 32), [[1, 32]], 0, 0)
+    iota(R("XI", 32, 48), [[1, 8], [0, 2]], 0, 0)
+    iota(R("CK", 0, 128), [[0, 16], [-2, 8]], 7, 0)
+    iota(R("ES", 0, 512), [[0, 512]], 1, 0)
+    asel(R("ES", 0, 512), R("ES", 0, 512), A.is_equal, 0.0, -1)
+    ms(R("NW", 0, 4096), 0.0)
+    ts(R("SO", 0, 128), R("TB", 0, 128), 0.0, A.is_equal)
+    ts(R("SP", 0, 128), R("TB", 0, 128), 64.0, A.is_equal)
     ts(R("NMB", 0, 256), R("NMI", 0, 256), -256.0, A.add)
-    dma("y", T.NW[0:128:16, 0:4096], T.NMB[:], [R("NMB", 0, 256)], [R("NW", 0, 4096)])
-    dma("y", ap(R("ZL", 0, 512)), T.z0[:], [], [R("ZL", 0, 512)])
-    dma("y", T.XO[:], T.xo[:], [], [R("XO", 0, 512)])
-    fill(R("M8", 0, 256, 8), 0.0)
-    act(R("ZN", 0, 144), R("ZA", 0, 144), scale=pf(6))
+    dma("y", rows("NW", 0, 4096), T.NMB[:, 0:256], [R("NMB", 0, 256)], [R("NW", 0, 4096)])
+    dma("y", T.OW0[:, 2048:4096], T.vo[:, 2048:4096], [], [R("OW0", 2048, 4096)])
+    dma("y", ap(blk(0)), T.xo[:], [], [blk(0)])
+    dma("y", T.VW0[:], T.vn[:], [], [R("VW0", 0, 4096)])
+    dma("y", T.ZZ[:], T.z0[:], [], [R("ZZ", 0, 512)])
+    cp(R("LF", 0, 128, 1, 0, 64), R("LI", 0, 128, 1, 0, 64))
+    for h in range(2):
+        for q in range(2):
+            mm(R("P7", 256 + 32 * h, 288 + 32 * h), R("SP" if q else "SO", 0, 128, 1, 0, 64), R("LF", 2 * h + q, 128, 4, 0, 64), q == 0, q == 1)
+    ts(R("PI", 1, 2), R("PI", 0, 1), 2, A.logical_shift_right, 3, A.bitwise_and)
+    ts(R("PI", 2, 3), R("PI", 0, 1), 1, A.logical_shift_right, 1, A.bitwise_and)
+    ts(R("PI", 3, 4), R("PI", 0, 1), 1, A.bitwise_and)
+    ts(R("PI", 4, 5), R("PI", 0, 1), 15, A.bitwise_and)
+    ts(R("PI", 5, 6), R("PI", 0, 1), 4, A.logical_shift_right)
+    ts(idw(I1), R("XD", 0, 128), 0.0, A.is_equal)
+    cp(R("PF", 0, 5), R("PI", 1, 6))
+    cp(R("YY", 0, 64), R("P7", 256, 320))
+    places()
+    strides()
+    ts(pf(12), pf(3), 0.0, A.is_equal)
+    ts(SELA, R("XI", 32, 48), pf(4), A.is_equal)
+    ms(R3("EQ", 0, 224, 0, 8), 0.0)
+    act(R3("P2", 0, 32, 7, 8), R("XD", 0, 32), AF.Ln, 1.0, 0.0)
+    act(SELN, R("SEL", 16, 32, 2), scale=pf(12))
     for d in range(1, 8):
-        act(idw(d), idw(0), scale=math.exp(d))
-    act(idw(8), idw(0), scale=-float(2 ** 25))
-    fill(R("KC", 0, 128), 592.0 * 4096)
-    act(R3("P3", 0, 256, 7, 8), R("XI", 0, 32), AF.Identity, 0.0, 0.0)
-    act(R("ZK", 0, 144), R("ZA", 0, 144), scale=4096.0)
-    act(pf(7), pf(1), bias=4080.0)
-    act(pf(8), pf(2), bias=48.0, scale=64.0)
-    act(pf(9), pf(2), bias=pf(3), scale=4.0)
-    act(R("JT", 0, 32), R("XI", 0, 32), bias=pf(1), scale=16.0)
-    fill(R("RS", 0, 128), 0.0)
-    act(pf(14), pf(8), bias=pf(1))
-    fill(R("STL", 512, 544), 32 * 312.0)
-    fill(R("CB", 0, 32), -3840.0)
-    fill(R("RS", 0, 128, 8), -1e9)
-    fill(R("XH", 0, 64), 1.0)
-    fill(R("WA", 0, 64), 2.0 ** (-LEV / 2))
-    fill(R("WB", 0, 64), 0.0)
-    cp(R("CSF", 0, 64), R("CSI", 0, 64))
-    op("v", lambda: g.vector.transpose(T.CSW[:], T.CSF[:]), [R("CSF", 0, 64)], [R("CSW", 0, 64)])
-    c0fn = lambda o, a, b: cp(o, R("CSW", a, b))
-    s0fn = lambda o, a, b: cp(o, R("CSW", 32 + a, 32 + b))
-    expand("STL", 0, "OFL", 0, c0fn, s0fn, 0, 256)
+        act(idw(d), idw(I1), scale=math.exp(STEP * d))
+    act(idw(IPEN), idw(I1), scale=-float(2 ** 17))
+    act(idw(I4), idw(I1), scale=4.0)
+    act(idw(INEG), idw(I1), scale=-1.0)
+    fill(R("C128", 0, 128), 128, 128.0)
+    act(SELK, R("SEL", 16, 32, 2), scale=16.0)
+    offsets()
 
-    def consts_a():
-        cp(R("STL", 0, 256, 8), R("D1", 0, 256, 8))
-        ts(R("PF", 10, 14), R("XI", 0, 4), pf(3), A.is_equal)
-        ts(R("BI", 0, 8), R("XI", 0, 8), pf(9), A.is_equal, 512.0, A.mult)
-        ts(R("ZB", 0, 176), R("XI", 0, 176), pf(14), A.is_equal)
-        scan(R("W64", 0, 64), R("WA", 0, 64), R("WB", 0, 64), 2.0 ** ((TOP + LEV) / 2), A.mult, A.add)
-        ts(R("WC", 0, 64), R("XI", 0, 64), pf(4), A.is_equal)
-        tt(R("WA", 0, 64), R("WC", 0, 64), R("W64", 0, 64), A.mult)
-        ms(R("P2", 128, 416, 9), 2.0 ** TOP)
-        op("v", lambda: g.vector.tensor_reduce(T.WP[:], T.WA[:], AxisListType.X, A.add), [R("WA", 0, 64)], [R("WP", 0, 1)])
+    def consts_s():
+        act(SELM, R("SEL", 16, 32, 2), scale=-32.0)
+        act(idw(IHALF), idw(I1), scale=0.5)
+        act(pf(5), pf(0), bias=3.5, scale=16.0)
+        act(pf(8), pf(2), bias=512.0, scale=-512.0)
+        act(pf(6), pf(1), bias=pf(5), scale=2048.0)
+        act(pf(9), pf(2), scale=-512.0)
+        act(pf(7), pf(2), bias=pf(6), scale=8.0)
+        act(pf(10), pf(3), bias=512.0)
+        act(pf(11), pf(3), bias=15.0, scale=-1.0)
+        act(A16, R("XI", 0, 32), scale=16.0)
+        act(R("A64", 0, 32), R("XI", 0, 32), scale=64.0)
+        fill(R("RS", 0, 128), 128, 0.0)
+        fill(R("MS", 0, 128), 128, 1.0)
+        fill(R("DS", 0, 128), 128, -0.25)
+        fill(R("LL", 0, 128), 128, math.exp(-0.5))
+        fill(R("RS", 0, 128, 8), 16, -1e9)
+        fill(R("MS", 0, 128, 4), 32, 0.0)
+        fill(R("DS", 0, 128, 4), 32, 1e6)
+        fill(R("CB", 0, 32), 32, -112.0)
+        fill(R("CB", 32, 64), 32, 32 * 312.0)
+        fill(R("XH", 0, 64), 64, -1.0)
+        fill(R("QM", 0, 128), 128, -0.25)
+        fill(R("DFW", 512, 576), 64, 0.0)
+        fill(R("OH", 0, 16), 16, 0.0)
+        fill(R("SO", 128, 192), 64, 0.0)
+        fill(R("XF", 0, 128), 128, 0.0)
 
-    def consts_b():
-        act(idw(9), idw(0), scale=-1.0)
-        for gp in range(4):
-            act(R("ZT", 176 * gp, 176 * gp + 176), R("ZB", 0, 176), scale=pf(10 + gp))
+    def consts_v():
+        tr(R("XS", 0, 64), R("YY", 0, 64))
+        ts(R("ZA", 0, 144), R("XD", 0, 144), pf(11), A.is_equal, 512.0, A.mult)
+        scan(R("LH", 0, 128), R("LL", 0, 128), R("RS", 0, 128), math.exp(32.5), A.mult, A.max)
+        mm(R("P6", 0, 1), R("LH", 0, 128, 1, 0, 1), R("MS", 1, 2, 1, 0, 1), True, True)
+        mm(AFL, idw(I1), R("CB", 32, 64), True, True)
+        cp(R("WP", 0, 1), R("P6", 0, 1))
 
-    def consts_c():
-        act(R("JT", 32, 64), R("JT", 0, 32), bias=float(XP))
-        act(R("JT", 64, 80), R("JT", 0, 16), bias=256.0)
-        act(R("JT", 80, 96), R("JT", 16, 32), bias=-256.0)
-        act(R("JT", 96, 128), R("JT", 0, 32), scale=1.0 / 512)
-
-    def consts_t(t):
-        act(R("DL", 0, 16), R("JT", 0, 16), bias=(512.0 * t - XP) / 512, scale=1.0 / 512)
-        act(R("DL", 16, 32), R("JT", 16, 32), bias=(512.0 * t + NXP - 511 - XP) / 512, scale=1.0 / 512)
-
-    iota(R("SB", 1024, 1280), [[0, 256]], 0, 0)
-    iota(R("RID", 0, 512), [[1, 512]], 0, 0)
-    iota(R("NW", XP, NXP), [[1, 2], [2, 256]], -256, 0)
+    iota(R("DP", 0, 144), [[0, 144]], 0, 0)
+    iota(R("DQ", 0, 144), [[0, 144]], 0, 0)
+    iota(R("SN", 512, 1024), [[0, 512]], 0, 0)
     iota(R("C256", 0, 128), [[0, 128]], 256, 0)
-    dma("y", T.yn[:], T.C256[:], [R("C256", 0, 128)], [R("yn", 0, 2048)])
-    send(prv, [(R(w, NXP, WEND), R(w, 0, 2048)) for w in ("OW", "VW", "NW")], "pre0", engp[:3 * qn])
-    send(prv, [(R("XN", 0, 512), R("XO", 0, 512))], "pre1", engp[3 * qn:])
 
-    LOG = lambda w: R(w, 0, 4096)
-    ALL = lambda w: R(w, 0, WEND)
-    XR = lambda a, b: R("OW", XP + a, XP + b)
-
-    def store_slice(t):
-        a, b = 512 * t, 512 * t + 512
-        dma("g", T.yn[:, a:b], T.NW[0:128:16, a:b], [R("NW", a, b), R("yn", 0, 2048)], [], accum_op=A.add)
-        dma("y", T.yv[:, a:b], ap(R("VW", a, b)), [R("VW", a, b)], [])
-        dma("y", T.yo[:, a:b], ap(R("OW", a, b)), [R("OW", a, b)], [])
-
-    def land(t, w):
-        o = R(w, 512 * t + 1, 512 * t + 512, 2)
-        c = 1024 * t + {"OW": 256, "NW": 512, "VW": 768}[w]
-        (cp if w == "VW" else act)(o, R("LND", c, c + 256))
+    def consts_g():
+        iota(R("ONE", 0, 512), [[0, 512]], 1, 0)
+        iota(R("RID", 0, 512), [[1, 512]], 0, 0)
+        iota(R("SN", 0, 512), [[1, 512]], -256, 0)
+        iota(R("SN", 1024, 1536), [[1, 512]], -256, 0)
 
     for t in range(VIS):
         last = t == VIS - 1
-        sb = STW * t
-        SREP = lambda a, b, st=1: R("STL", sb + a, sb + b, st)
-        ERAW = lambda a, b, st=1: R("STL", sb + 256 + a, sb + 256 + b, st)
-        AFL = R("STL", sb + 512, sb + 544)
-        Z = lambda a, b: R("ZL", 512 * t + a, 512 * t + b)
-        OFF = lambda a, b: R("OFL", 256 * t + a, 256 * t + b)
-        NP = lambda h, a, b, k0=0, k1=8: R3("P%d" % h, a, b, k0, k1)
-        LM = lambda h, k1=8: R3("P3", 128 * h, 128 * h + 128, 0, k1)
-        KEY = lambda h, a, b: R("P%d" % (4 + h), a, b)
-        E = lambda h, d, k0: R3("EQ", 896 * h + 128 * (d - 1), 896 * h + 128 * d, k0, 8)
+        OW, VW = "OW%d" % t, "VW%d" % t
+        sl = (512 * t, 512 * t + 512)
+        XR = blk(5 * t)
+        bo, bv, b2 = (17, 20, 16) if last else (5 * t, 5 * t + 3, 5 * t + 3)
+        Z = R("ZZ", 0, 512)
+        OFF = lambda a, b: R("OFF", a, b)
+        NP = lambda h, k0=0, k1=8: R3("P%d" % h, 0, 16, k0, k1)
+        LM = lambda h, k1=8: R3("P2", 16 * h, 16 * h + 16, 0, k1)
+        KB = lambda h: ("P4", 128) if h == 0 else ("P5", 0)
+        KEY = lambda h: R(KB(h)[0], KB(h)[1], KB(h)[1] + 128)
+        E = lambda h, d, k0: R3("EQ", 112 * h + 16 * (d - 1), 112 * h + 16 * d, k0, 8)
+
+        def forward():
+            if t > 0:
+                for j in range(2):
+                    dma("y", T.NMB[2 * t - 2 + j:128:16, 256 * t:256 * t + 256], rows("NW", sl[0] - 512 + 256 * j, sl[0] - 256 + 256 * j),
+                        [R("NW", sl[0] - 512, sl[0])], [R("NMB", 256 * t, 256 * t + 256)])
+            send([(3 if last else -1, R("NMB", 256 * t + 256, 256 * t + 512), R("NMB", 256 * t, 256 * t + 256))])
+            if last:
+                send([(3, blk(19), XR), (4, blk(17), XR)])
+                send([(3, R("YO", 0, 1536), R(OW, 0, 1536)), (3, R("YV", 0, 1536), R(VW, 0, 1536))])
+            else:
+                send([(-1, blk(bo + 1), R(OW, *sl)), (-1, blk(bv + 1), R(VW, *sl)), (-1, blk(bo + 2), XR)])
+                send([(-1, R("OW%d" % (t + 1), 0, 4096), R(OW, 0, 4096)), (-1, R("VW%d" % (t + 1), 0, 4096), R(VW, 0, 4096))])
+
+        def refill():
+            w = "NR" if last else "NW"
+            dma("y", rows(w, 0, 4096), T.NMB[:, 256 * t + 256:256 * t + 512], [R("NMB", 256 * t + 256, 256 * t + 512)], [R(w, 0, 4096)])
+            dma("y", rows("SN", 512, 1024), rows(w, *sl), [R(w, *sl)], [R("SN", 512, 1024)])
+            if t == 0:
+                dma("y", T.yn[:], T.C256[:], [R("C256", 0, 128)], [R("yn", 0, 2048)])
+                dma("y", ap(blk(18)), T.vo[:, 1536:2048], [], [blk(18)])
+                dma("y", ap(blk(21)), T.vn[:, 1536:2048], [], [blk(21)])
+            if last:
+                dma("g", T.yn[:, 0:1536], rows("NR", 0, 1536), [R("NR", 0, 1536), R("yn", 0, 2048)], [], accum_op=A.add)
+                dma("y", T.yo[:, 0:1536], T.YO[:, 0:1536], [R("YO", 0, 1536)], [])
+                dma("y", T.yv[:, 0:1536], T.YV[:, 0:1536], [R("YV", 0, 1536)], [])
 
         def ngv(i):
-            cp(R("NG", 512 * i, 512 * i + 512), ind(LOG("NW"), OFF(32 * i, 32 * i + 32)))
+            cp(R("NG", 512 * i, 512 * i + 512), ind(R("NW", 0, 4096), OFF(32 * i, 32 * i + 32)))
 
         def ngs(i):
-            act(R("NG", 512 * i, 512 * i + 512), ind(LOG("NW"), OFF(32 * i, 32 * i + 32)))
+            act(R("NG", 512 * i, 512 * i + 512), ind(R("NW", 0, 4096), OFF(32 * i, 32 * i + 32)))
 
-        def npe(c):
-            to_w(NP(c // 2, 64 * (c % 2), 64 * (c % 2) + 64), "ZN", "NG", 1024 * c, 64, True, True)
+        def npe(h):
+            for k in range(16):
+                mm(R("P%d" % h, 8 * (k >> 3) + (k & 7), 128, 16), R("NG", 2048 * h + k, 2048 * h + 2048, 16), SELN, True, True)
 
-        def og(c, a=0, b=1024):
-            act(R("OG", 1024 * c + a, 1024 * c + b), ind(LOG("OW"), OFF(64 * c + a // 16, 64 * c + b // 16)))
-
-        def ogv(c, a=0, b=1024):
-            cp(R("OG", 1024 * c + a, 1024 * c + b), ind(LOG("OW"), OFF(64 * c + a // 16, 64 * c + b // 16)))
+        def og(a, b):
+            act(R("OG", a, b), ind(R(OW, 0, 4096), OFF(a // 16, b // 16)))
 
         def eq(h):
-            cp(R3("NS", 0, 128), NP(h, 0, 128))
+            cp(R3("NS", 0, 16, 0, 8), NP(h))
             for d in range(1, 8):
-                tt(E(h, d, d), NP(h, 0, 128, 0, 8 - d), R3("NS", 0, 128, d, 8), A.is_equal)
+                tt(E(h, d, d), NP(h, 0, 8 - d), R3("NS", 0, 16, d, 8), A.is_equal)
             for d in range(1, 8):
                 mm(LM(h, 8 - d), idw(d), E(h, d, d), d == 1, d == 7)
-            mm(KEY(h, 0, 128), idw(0), R("KH", 128 * h, 128 * h + 128), True, False)
-            mm(KEY(h, 0, 128), idw(0), R("KC", 0, 128), False, False)
+
+        def pen(h):
+            mm(KEY(h), idw(I1), R("CK", 0, 128), True, False)
             for d in range(1, 8):
-                mm(KEY(h, 0, 128), idw(8), E(h, d, 0), False, False)
+                mm(KEY(h), idw(IPEN), E(h, d, 0), False, False)
 
         def ln(h):
-            act(R("LY", 128 * h, 128 * h + 128), LM(h), AF.Ln, math.exp(-0.23), math.exp(-0.23))
+            ly = R("LY", 128 * h, 128 * h + 128)
+            act(ly, LM(h), AF.Ln, math.exp(32.03), math.exp(31.89))
+            mm(R("P3", 256 * h + 128, 256 * h + 256), ly, idw(I4), True, False)
+            mm(R("P3", 256 * h + 128, 256 * h + 256), R("C128", 0, 128), idw(INEG), False, True)
 
         def el(h):
             a, b = 128 * h, 128 * h + 128
-            ts(R("P7", 0, 128), R("LY", a, b), MAG, A.add, MAG, A.subtract)
-            tt(R("P7", 128, 256), R("P7", 0, 128), SREP(a, b), A.mult)
-            tt(R("EI", a, b), R("P7", 128, 256), ERAW(a, b), A.add)
-            ts(R("EJ", a, b), R("EI", a, b), 4095, A.bitwise_and)
-            cp(R("OFE", a, b), R("EJ", a, b))
+            tt(R("P7", 0, 128), R("P3", 256 * h + 128, 256 * h + 256), R("SR", a, b), A.mult)
+            tt(R("EK", a, b), R("P7", 0, 128), R("EJ", a, b), A.add)
+            ts(R("EL", a, b), R("EK", a, b), 4095, A.bitwise_and)
+            cp(R("OFE", a, b), R("EL", a, b))
 
         def dg(a, b):
-            tt(R("DD", a, b), ind(LOG("VW"), R("OFE", a // 16, b // 16)), R("OG", a, b), A.subtract)
+            tt(R("DD", a, b), ind(R(VW, 0, 4096), R("OFE", a // 16, b // 16)), R("OG", a, b), A.subtract)
 
         def ab(a, b):
             act(R("AD", a, b), R("DD", a, b), AF.Abs)
 
-        def kpe(c):
-            to_w(KEY(c // 2, 64 * (c % 2), 64 * (c % 2) + 64), "ZK", "AD", 1024 * c, 64, False, c % 2 == 1)
+        def kpe(a, b):
+            h, p0 = a // 2048, (a % 2048) // 16
+            bank, c0 = KB(h)
+            for k in range(16):
+                mm(R(bank, c0 + k, c0 + 128, 16, p0, p0 + (b - a) // 16), R("AD", a + k, b, 16), SELK, False, k == 15)
 
-        def kscan(h):
-            scan(R("KS", 128 * h, 128 * h + 128), R("RS", 0, 128), KEY(h, 0, 128), 0.0, A.add, A.max)
+        def pick(h):
+            a, b = 16 * h, 16 * h + 16
+            scan(R("KS", 8 * a, 8 * b), R("RS", 0, 128), KEY(h), 0.0, A.add, A.max)
+            ts(R("W8", a, b), R("KS", 8 * a + 7, 8 * b, 8), 16 * MAG, A.add, 16 * MAG, A.subtract)
+            tt(padded("DP", h), R("W8", a, b), R("KS", 8 * a + 7, 8 * b, 8), A.subtract)
 
-        def pick(hh, part):
-            a, b = 16 * hh, 16 * hh + 16
-            if part == 0:
-                cp(R("KI", a, b), R("KS", 8 * a + 7, 8 * b, 8))
-            elif part == 1:
-                ts(R("KX", a, b), R("KI", a, b), 4095, A.bitwise_and)
-            elif part == 2:
-                ts(R("OFD", a, b), R("KX", a, b), -1.0, A.mult, pf(7), A.add)
-            elif part == 3:
-                tt(R("GG", 16 * a, 16 * b), ind(R("AD", 0, 2048 * hh + 2048), R("OFD", a, b)), Z(16 * a, 16 * b), A.is_lt)
-            else:
-                if hh == 0:
-                    mm(R("P6", 128, 160), idw(0), R("CB", 0, 32), True, False)
-                for sub in range(4 * hh, 4 * hh + 4):
-                    for e in range(2):
-                        mm(R("P6", 128 + 4 * sub, 132 + 4 * sub, 1, 64 * e, 64 * e + 64), R("GG", 64 * sub, 64 * sub + 64),
-                           R("BI", 4 * e, 4 * e + 4), False, sub == 7)
+        def late(tp):
+            if tp >= 0:
+                act(R("VW%d" % (tp + 1), 512 * tp, 512 * tp + 512), ind(blk(5 * tp + 3, 3), R("OFS", 0, 32)))
 
-        ngv(0); ngs(1); npe(0)
-        ngv(2); ngs(3); npe(1)
+        def late_z(tp):
+            if tp >= 0:
+                ts(R("OFZ", 0, 32), R("P6", 192, 224), pf(3), A.add)
+                act(Z, ind(R("ZW", 0, 1024), R("OFZ", 0, 32)))
+
+        ngv(0); ngs(1); ngv(2); ngv(3); npe(0)
+        act(R("SR", 0, 256), R3("P4", 0, 2, 0, 128), scale=1.0 / 7)
+        ngv(4); ngs(6); ngs(5)
+        late(t - 1)
+        forward()
         if t == 0:
-            consts_a()
-        else:
-            land(t - 1, "OW")
-            land(t - 1, "VW")
-        ngv(4)
-        og(0); og(1, 0, 512)
+            consts_g()
+        og(0, 512)
         eq(0)
-        ngv(6)
-        ln(0)
-        og(1, 512, 1024)
+        ngv(7)
+        ln(0); npe(1); pen(0)
+        og(512, 1024)
         el(0)
-        ngs(5); npe(2); ngs(7); npe(3)
-        if t > 0:
-            store_slice(t - 1)
+        og(1024, 2048)
+        refill()
         dg(0, 1024)
-        og(2)
         eq(1)
-        ab(0, 1024); kpe(0)
+        og(2048, 3072)
+        ln(1); pen(1)
         dg(1024, 2048)
-        ln(1)
-        og(3)
+        ab(0, 1024)
+        og(3072, 3584)
         el(1)
-        ab(1024, 2048); kpe(1)
-        dg(2048, 3072)
-        ab(2048, 3072); kpe(2)
-        dg(3072, 3584); ab(3072, 3584)
+        ab(1024, 2048); kpe(0, 2048)
+        if t > 0:
+            ts(R("OFZ", 0, 32), R("P6", 192, 224), pf(3), A.add)
+        dg(2048, 2560)
+        og(3584, 4096)
+        ab(2048, 2560); kpe(2048, 2560)
+        dg(2560, 3072); ab(2560, 3072); kpe(2560, 3072)
+        dg(3072, 3584); ab(3072, 3584); kpe(3072, 3584)
         dg(3584, 3840); ab(3584, 3840)
-        dg(3840, 4096); ab(3840, 4096); kpe(3)
+        dg(3840, 4096); ab(3840, 4096); kpe(3584, 4096)
         if t == 0:
-            consts_b()
-        kscan(0)
-        if t == 0:
-            cp(XR(256, 512), R("XN", 1, 512, 2))
-            cp(XR(0, 256), R("XO", 0, 512, 2))
+            consts_s()
+            consts_v()
+            cp(R("XB", 1, 512, 2), R("XB", 1025, 1536, 2))
         else:
-            act(XR(0, 256), ind(R("SB", 768, 1792), R("OF3", 0, 16)))
-        act(R("ZH", 0, 512), Z(0, 512), AF.Identity, -0.5)
-        if t == 0:
-            consts_c()
-        consts_t(t)
-        for part in range(4):
-            pick(0, part)
-        cp(R("SB", 1280, 1536), XR(256, 512))
-        cp(R("SB", 1536, 1792), XR(0, 256))
-        kscan(1)
-        pick(0, 4)
-        ts(R("UI", 0, 32), R("KS", 7, 256, 8), 1.0 / 4096, A.mult, -0.498, A.add)
-        pick(1, 0)
-        tt(R("T1", 0, 32), R("UI", 0, 32), R("UI", 0, 32), A.mult)
-        pick(1, 1)
-        tt(R("T5", 0, 32), R("T1", 0, 32), AFL, A.add)
-        pick(1, 2)
+            act(Z, ind(R("ZW", 0, 1024), R("OFZ", 0, 32)))
+        pick(0)
+        act(R("T4", 0, 32), SS, scale=8.0)
+        pick(1)
+        mm(R("P6", 0, 32), idw(I1), R("A64", 0, 32), True, False)
+        t_to_w(R("P6", 0, 32), "DP", IHALF, False)
+        act(R("SQ", 0, 32), R("W8", 0, 32), AF.Square, 592.0, 1.0 / 16)
+        tt(R("FC", 0, 32), R("W8", 0, 32), R("KS", 7, 256, 8), A.subtract)
+        ts(R("T8", 0, 32), R("W8", 0, 32), 0.125, A.mult, 1.0, A.add)
+        tt(R("T5", 0, 32), R("SQ", 0, 32), AFL, A.add)
+        ts(R("OFD", 0, 32), R("P6", 0, 32), pf(7), A.add)
+        mm(CNT, idw(I1), R("CB", 0, 32), True, False)
+        tt(R("GG", 0, 512), ind(R("AD", 0, 4096), R("OFD", 0, 32)), Z, A.is_lt)
+        for s in range(4):
+            mm(sub5(128, s), R("GG", s, 512, 4), SELK, False, s == 3)
         act(R("DFW", 0, 512), ind(R("DD", 0, 4096), R("OFD", 0, 32)))
-        ts(R("AB", 0, 32), R("T5", 0, 32), 5, A.logical_shift_right, 30, A.bitwise_and)
-        ts(R("AB", 32, 64), R("T5", 0, 32), 5, A.logical_shift_right, 481, A.bitwise_and)
-        ts(R("ABB", 0, 64), R("AB", 0, 64), -240.0, A.add)
-        for gp in range(4):
-            for w in range(4):
-                mm(R("P7", 256 + gp, 320, 4), R("ZT", 176 * gp + 48 - 16 * w, 176 * gp + 176 - 16 * w), R("ABB", w, 64, 4), w == 0, w == 3)
-        pick(1, 3)
-        pick(1, 4)
-        act(R("ZW", 0, 512), Z(0, 512), AF.Relu, -1.0)
-        mm(R3("P1", 0, 256), idw(0), R("VW", 512 * t, 512 * t + 512, 2), True, False)
-        mm(R3("P1", 0, 256), idw(9), XR(0, 256), False, True)
-        mm(R3("P1", 256, 512), idw(0), R("VW", NXP + 512 * t + 1, NXP + 512 * t + 512, 2), True, False)
-        mm(R3("P1", 256, 512), idw(9), XR(256, 512), False, True)
-        act(R("DFW", 512, 1024), R3("P1", 0, 512))
-        ts(R("T7", 0, 32), R("AB", 32, 64), 513.0, A.mult)
-        ts(R("YI", 0, 32), R("KX", 0, 32), 4, A.logical_shift_right, 7, A.bitwise_and)
-        ts(R("T8", 0, 32), R("UI", 0, 32), 432.0, A.add)
-        ts(R("AT", 0, 32), R("P7", 256, 288), 16.0, A.mult, 3600.0, A.add)
-        cp(R("XH", 64, 128, 2), R("P7", 288, 320))
-        ts(R("XH", 65, 128, 2), R("P7", 288, 320), -1.0, A.add)
-        for e in range(2):
-            tt(R("XH", e, 64, 2, 64 * e, 64 * e + 64), R("P6", 128, 160, 1, 64 * e, 64 * e + 64), R("AT", 0, 32, 1, 64 * e, 64 * e + 64), A.max)
+        act(R("F7", 0, 32), R("FC", 0, 32), bias=3.5, scale=-0.5)
+        act(R("BB", 0, 512), R("DFW", 0, 512), AF.Abs)
+        act(R("ZW", 0, 512), Z, AF.Relu, -1.0)
+        ts(R("AB", 32, 64), R("T5", 0, 32), 9, A.logical_shift_right, 31, A.bitwise_and)
+        ts(R("AB", 0, 32), R("T5", 0, 32), 5, A.logical_shift_right, 15, A.bitwise_and)
+        cp(R("XH", 64, 128, 2), R("AB", 32, 64))
+        ts(R("XH", 65, 128, 2), R("AB", 32, 64), -16.0, A.add)
+        tt(R("XH", 0, 64, 2), CNT, R("AB", 0, 32), A.max)
         for v in range(16):
-            ts(R("OH", v, 2048, 16), R("XH", 0, 128), 32.0 * v - 240, A.is_equal, R("WP", 0, 1), A.mult)
-        for sub in range(8):
-            for gp in range(4):
-                i = 4 * sub + gp
-                mm(R("P2", 136 - sub, 416, 9, 32 * gp, 32 * gp + 32), R("OH", 32 * i, 32 * i + 32), R("OH", 1024 + 32 * i, 1056 + 32 * i), True, True)
-        to_w(R("P6", 0, 32), "ZA", "GG", 0, 32, True, True)
-        act(R("HY", 0, 288), R("P2", 128, 416), AF.Ln, 2.0 ** (TOP - 64 * LEV))
-        act(R("HQ", 0, 288), R("HY", 0, 288), AF.Identity, TOP / LEV, -1.0 / (LEV * LN2))
-        ts(R("T6", 0, 32), R("T7", 0, 32), 5, A.logical_shift_right, 31, A.bitwise_and)
-        ts(R("YS", 0, 32), R("T8", 0, 32), 511, A.bitwise_and)
-        ts(R("T3", 0, 32), SREP(0, 256, 8), 8.0, A.mult)
-        tt(R("DC", 0, 32), R("YI", 0, 32), SREP(0, 256, 8), A.mult)
-        tt(R("Z1", 0, 512), ind(R("AD", 0, 4096), R("OFD", 0, 32)), R("ZH", 0, 512), A.add)
-        cp(R("OFB", 0, 32), R("T6", 0, 32))
-        ts(R("SA", 0, 32), R("YS", 0, 32), 2.0, A.mult, 1.0, A.add)
-        tt(R("T4", 0, 32), R("T3", 0, 32), ERAW(0, 256, 8), A.add)
-        ts(R("HE", 0, 288), R("HY", 0, 288), (TOP - 63.5 * LEV) * LN2, A.is_lt)
-        tt(R("DS", 0, 32), R("SA", 0, 32), SREP(0, 256, 8), A.subtract)
-        tt(R("CN", 0, 32), R("T4", 0, 32), R("DC", 0, 32), A.subtract)
-        act(R("Z2", 0, 512), R("Z1", 0, 512), AF.Identity, MAG, 0.5)
-        act(R("ZW", 512, 1024), R("Z2", 0, 512), AF.Identity, -MAG)
-        scan(R("HS", 0, 288), R("HE", 0, 288), R("HQ", 0, 288), 0.0, A.mult, A.add)
-        ts(R("WIN", 0, 32), R("HS", 8, 288, 9), MAG, A.add, MAG, A.subtract)
-        ts(R("UU", 0, 32), R("HS", 8, 288, 9), 511.5, A.is_ge, 512.0, A.mult)
+            ts(R("OH", 16 + v, 2064, 16), R("XH", 0, 128), float(v), A.is_equal, R("WP", 0, 1), A.mult)
+        for h in range(2):
+            for q in range(2):
+                for gr in range(8):
+                    c, e, p0 = 16 * h + 2 * gr + q, gr & 1, 32 * (gr >> 1)
+                    mm(R("P7", 128 + 2 * h + q, 256, 4, p0, p0 + 32), R("OH", 16 + 32 * c - 16 * e, 48 + 32 * c - 16 * e),
+                       R("OH", 1040 + 32 * c, 1072 + 32 * c), e == 0, e == 1)
+        for h in range(2):
+            cp(padded("DQ", h), R("AB", 32 + 16 * h, 48 + 16 * h))
+        t_to_w(R("P6", 32, 64), "DQ", I1, True)
+        mm(R("P0", 0, 512), idw(IHALF), Z, True, False)
+        mm(R("P0", 0, 512), idw(IHALF), R("BB", 0, 512), False, False)
+        mm(R("P0", 0, 512), R("QM", 0, 128, 1, 0, 1), R("ONE", 0, 512, 1, 0, 1), False, True)
+        ts(R("FI", 0, 32), CNT, 8.0, A.is_lt, 32.0, A.mult)
+        ts(R("SA", 0, 32), R("T8", 0, 32), 1023, A.bitwise_and)
+        tt(R("DX", 0, 64, 2), R("F7", 0, 32), SS, A.mult)
+        tt(R("T3", 0, 32), R("T4", 0, 32), CC, A.add)
+        tt(R("DX", 1, 64, 2), R("SA", 0, 32), SS, A.subtract)
+        if last:
+            tt(R("CI", 0, 32), R("T3", 0, 32), R("DX", 0, 64, 2), A.subtract)
+            cp(R("CI", 32, 64), R("T3", 0, 32))
+            ts(R("CJ", 0, 64), R("CI", 0, 64), 4095, A.bitwise_and)
+            cp(CC, R("CJ", 0, 32))
+            tt(R("DX", 0, 64, 2), R("CJ", 32, 64), R("CJ", 0, 32), A.subtract)
+        else:
+            tt(CC, R("T3", 0, 32), R("DX", 0, 64, 2), A.subtract)
+        H = R("P7", 128, 256)
+        ts(R("YH", 0, 128), H, 1.0, A.max, math.exp(-32.0), A.mult)
+        ts(R("YH", 128, 256), H, 1.0, A.min, math.exp(32.0), A.mult)
+        act(R("LH", 0, 128), R("YH", 0, 128), AF.Ln)
+        act(R("LL", 0, 128), R("YH", 128, 256), AF.Ln, math.exp(-40.0))
+        act(R("P2", 256, 384), R("LH", 0, 128), bias=192.23, scale=-1.0)
+        scan(R("HM", 0, 128), R("MS", 0, 128), R("YH", 128, 256), 0.0, A.mult, A.max)
+        ts(R("FL", 0, 32), R("HM", 3, 128, 4), 0.0, A.is_gt, pf(8), A.mult)
+        ts(R("FL", 32, 64), R("HM", 3, 128, 4), 0.0, A.is_gt, pf(9), A.mult)
+        if last:
+            send([(3, R("FR", 96, 128), R("FL", 0, 32)), (4, R("FR", 128, 160), R("FL", 32, 64))])
+        else:
+            send([(-1, R("FR", 32 * t, 32 * t + 32), R("FL", 0, 32))])
+        cp(R("OFB", 0, 32), R("P6", 32, 64))
+        tt(R("HQ", 0, 128), R("P2", 256, 384), R("LL", 0, 128), A.subtract)
+        act(R("Z2", 0, 512), R("P0", 0, 512), bias=MAG)
+        act(R("ZW", 512, 1024), R("Z2", 0, 512), bias=-MAG)
+        scan(R("HS", 0, 128), R("DS", 0, 128), R("HQ", 0, 128), 0.0, A.add, A.min)
+        ts(R("WIN", 0, 32), R("HS", 3, 128, 4), 4.0, A.mult, -509.0, A.add)
+        ts(R("OF1", 0, 32), R("HS", 3, 128, 4), 4.0, A.mult, -509.0, A.add)
 
-        def acts(a, b, bank):
-            tt(R("AQ", 16 * a, 16 * b), ind(R("WIN", 0, 32), R("OFB", a, b)), R("RID", 16 * a, 16 * b), A.is_equal)
-            to_w(R(bank, a, b), "ZA", "AQ", 16 * a, b - a, True, True)
-        if not last:
-            acts(0, 32, "P2")
-        tt(R("U2", 0, 32), R("UU", 0, 32), R("DL", 0, 32), A.mult)
-        tt(R("R1", 0, 32), R("UU", 0, 32), R("JT", 96, 128), A.mult)
-        tt(R("U3", 0, 32), R("U2", 0, 32), R("JT", 32, 64), A.add)
-        tt(R("R2", 0, 32), R("R1", 0, 32), R("WIN", 0, 32), A.add)
-        cp(R("OF2", 0, 32), R("U3", 0, 32))
-        cp(R("OF1", 0, 32), R("R2", 0, 32))
-        act(R("SB", 512, 768), ind(ALL("NW"), R("OF2", 16, 32)))
-        act(R("SB", 256, 512), ind(ALL("OW"), R("OF2", 16, 32)))
-        lb = 1024 * t
-        tt(R("VT", 256, 512), ind(R("DFW", 0, 1024), R("OF1", 16, 32)), XR(256, 512), A.add)
+        def objects():
+            tt(R("VT", 0, 512), ind(R("DFW", 0, 576), R("OF1", 0, 32)), XR, A.add)
+            ts(blk(b2), R("VT", 0, 512), 0.0, A.max, 255.0, A.min)
+            send([(3, blk(22), blk(b2)), (4, blk(20), blk(b2))] if last else [(-1, blk(b2 + 2), blk(b2))])
 
-        def of3():
-            tt(R("U4", 0, 32), R("UU", 0, 32), R("JT", 64, 96), A.add)
-            cp(R("OF3", 0, 32), R("U4", 0, 32))
-        ACT = R("P2", 0, 32)
+        def choice():
+            mm(R("P6", 128, 160), idw(I1), A16, True, False)
+            mm(R("P6", 128, 160), idw(I1), R("FR", 128, 160) if last else R("FL", 32, 64), False, False)
+            mm(R("P6", 128, 160), idw(I1), R("FR", 32 * t, 32 * t + 32), False, True)
+
+        def z_offsets():
+            mm(R("P6", 192, 224), idw(I1), A16, True, False)
+            for r in range(16):
+                mm(R("P6", 192, 224), R("ZA", 15 - r, 143 - r), R("AQ", r, 512, 16), False, r == 15)
+
+        def flags():
+            mm(AFL, idw(I1), R("CB", 32, 64), True, False)
+            mm(AFL, idw(I1), R("FI", 0, 32), False, False)
+            for s in range(4):
+                mm(sub5(160, s), R("AQ", s, 512, 4), SELM, False, s == 3)
         if last:
-            of3()
-        else:
-            tt(R("R3", 0, 32), ACT, R("DS", 0, 32), A.mult)
-        ts(R("SB", 768, 1024), R("VT", 256, 512), 0.0, A.max, 255.0, A.min)
-        if last:
-            cp(R("SB", 0, 256), ind(R("SB", 768, 1536), R("OF3", 16, 32)))
-            send(nxt, [(R("LND", lb, lb + 1024), R("SB", 0, 1024))], "aL%d" % t, engs)
-            acts(0, 32, "P2")
-            tt(R("R3", 0, 32), ACT, R("DS", 0, 32), A.mult)
-        else:
-            send(nxt, [(R("LND", lb + 256, lb + 1024), R("SB", 256, 1024))], "aL%d" % t, engs)
-        act(R("NE", 0, 256), ind(ALL("NW"), R("OF2", 0, 16)))
-        act(R("OE", 0, 256), ind(ALL("OW"), R("OF2", 0, 16)))
-        ev = lambda w: R(w, 512 * t, 512 * t + 512, 2)
-        act(ev("NW"), R("NE", 0, 256))
-        act(ev("OW"), R("OE", 0, 256))
-        tt(R("R4", 0, 32), ACT, R("DC", 0, 32), A.mult)
-        cfn = lambda o, a, b: tt(o, R("R4", a, b), R("CN", a, b), A.add)
-        sfn = lambda o, a, b: tt(o, R("R3", a, b), SREP(8 * a, 8 * b, 8), A.add)
+            objects()
+        tt(R("AQ", 0, 512), ind(R("WIN", 0, 32), R("OFB", 0, 32)), R("RID", 0, 512), A.is_equal)
+        for s in range(4):
+            mm(R3("P6", 16 + 8 * (s >> 1), 24 + 8 * (s >> 1), 2 * (s & 1), 2 * (s & 1) + 2), R("AQ", s, 512, 4), SELA, True, True)
+        tt(R("PR", 0, 64), R("P6", 64, 128), R("DX", 0, 64), A.mult)
+        OFS = R("OFS", 0, 32)
         if not last:
-            ob = 256 * t + 256
-            expand("SST", 0, "SOF", 0, cfn, sfn, 0, 128)
-            send(nxt, [(R("OFL", ob, ob + 128), R("SOF", 0, 128))], "aO%d" % t, engs)
-            aout = R("SST", 512, 544)
+            tt(R("XS", 0, 64), R("XS", 0, 64), R("PR", 0, 64), A.add)
+            tr(R("YY", 0, 64), R("XS", 0, 64))
+            places()
+            choice()
+            objects()
+            ts(OFS, R("P6", 128, 160), pf(10), A.add)
+            act(R("NW", *sl), ind(R("SN", 0, 1536), OFS))
+            act(R("OW%d" % (t + 1), *sl), ind(blk(bo, 3), OFS))
+            strides()
+            z_offsets()
+            flags()
+            offsets()
         else:
-            cfn(R("FC", 0, 32), 0, 32)
-            sfn(R("FO", 32, 64), 0, 32)
-            aout = R("FO", 64, 96)
-        ts(R("ACT", 0, 32), ACT, 512.0, A.mult)
-        ts(R("FI", 0, 32), R("P6", 0, 32), 7.5, A.is_lt, 1.0 if last else 32.0, A.mult)
-        tt(R("R5", 0, 32), R("ACT", 0, 32), R("JT", 0, 32), A.add)
-        if last:
-            tt(aout, R("FI", 0, 32), ACT, A.subtract)
-        else:
-            ts(R("R2", 0, 32), ACT, -32.0, A.mult, 32 * 312.0, A.add)
-            tt(aout, R("FI", 0, 32), R("R2", 0, 32), A.add)
-        cp(R("OFZ", 0, 32), R("R5", 0, 32))
-        act(R("ZS", 0, 512), ind(R("ZW", 0, 1024), R("OFZ", 0, 32)))
-        if not last:
-            of3()
-            act(XR(256, 512), ind(R("SB", 768, 1536), R("OF3", 16, 32)))
-            expand("SST", 0, "SOF", 0, cfn, sfn, 128, 256)
-            send(nxt, [(R("OFL", ob + 128, ob + 256), R("SOF", 128, 256))], "aP%d" % t, engs)
-            cp(R("SST", 0, 256, 8), R("D1", 0, 256, 8))
-            send(nxt, [(R("STL", sb + STW, sb + 2 * STW), R("SST", 0, STW))], "aS%d" % t, engs)
-            send(nxt, [(R("ZL", 512 * t + 512, 512 * t + 1024), R("ZS", 0, 512))], "aZ%d" % t, engs)
-            land(t, "NW")
-        else:
-            dma("y", T.yz[:], T.ZS[:], [R("ZS", 0, 512)], [])
-            ts(R("FD", 0, 32), R("FC", 0, 32), 4095, A.bitwise_and)
-            cp(R("FO", 0, 32), R("FD", 0, 32))
-            op("v", lambda: g.vector.transpose(T.FT[:], T.FO[:]), [R("FO", 0, 96)], [R("FT", 0, 96)])
-            for i, dst in enumerate((T.yc, T.ys, T.ya)):
-                for e in range(2):
-                    r = R("FT", 32 * i + 16 * e, 32 * i + 16 * e + 16)
-                    dma("y", dst[e::2, :], ap(r), [r], [])
-        tt(R("VT", 0, 256), ind(R("DFW", 0, 1024), R("OF1", 0, 16)), XR(0, 256), A.add)
-        ts(R("SB", 1024, 1280), R("VT", 0, 256), 0.0, A.max, 255.0, A.min)
-        ts(ev("VW"), R("VT", 0, 256), 0.0, A.max, 255.0, A.min)
-        if last:
-            cp(R("OE", 0, 256), ind(R("SB", 768, 1792), R("OF3", 0, 16)))
-            land(t, "NW")
-            land(t, "OW")
-            cp(R("YX", 0, 512, 2), R("OE", 0, 256))
-            land(t, "VW")
-            cp(R("YX", 1, 512, 2), R("LND", lb, lb + 256))
-            dma("s", T.yx[:], T.YX[:], [R("YX", 0, 512)], [])
-            store_slice(t)
+            flags()
+            z_offsets()
+            for h in range(2):
+                tt(R("XF", 64 * h, 64 * h + 32), R("XS", 32 * h, 32 * h + 32), R("PR", 32 * h, 32 * h + 32), A.add)
+            for h in range(2):
+                ts(R("XF", 64 * h + 32, 64 * h + 64, 2), R("P5", 160 + 16 * h, 176 + 16 * h), -32 * 312.0, A.add, 1.0 / 32, A.mult)
+            tr(R("YY", 0, 128), R("XF", 0, 128))
+            for s in range(4):
+                h, q = s >> 1, s & 1
+                mm(R("P7", 256 + s, 512, 4), R("SO", 64 * q, 64 * q + 128), R("YY", 64 * h, 64 * h + 64), True, True)
+            late_z(t)
+            send([(3, R("ZL", 0, 512), Z)])
+            cp(R("FO", 0, 256), R("P7", 256, 512))
+            send([(3, R("FN", 0, 256), R("FO", 0, 256))])
+            choice()
+            ts(OFS, R("P6", 128, 160), pf(10), A.add)
+            cp(R("NR", *sl), ind(R("SN", 0, 1536), OFS))
+            act(R("YO", *sl), ind(blk(bo, 3), OFS))
+            dma("g", T.yn[:, 1536:2048], rows("NR", *sl), [R("NR", *sl), R("yn", 0, 2048)], [], accum_op=A.add)
+            dma("y", T.yo[:, 1536:2048], T.YO[:, 1536:2048], [R("YO", *sl)], [])
+            act(R("YV", *sl), ind(blk(bv, 3), OFS))
+            dma("s", T.yv[:, 1536:2048], T.YV[:, 1536:2048], [R("YV", *sl)], [])
+            cp(R("YX", 0, 512, 2), R("XB", 512 * 22, 512 * 23, 2))
+            cp(R("YX", 1, 512, 2), R("XB", 512 * 20 + 1, 512 * 21, 2))
+            dma("y", T.yx[:], T.YX[:], [R("YX", 0, 512)], [])
+            dma("y", T.yz[:], T.ZL[:], [R("ZL", 0, 512)], [])
+            dma("y", T.yc[:], T.FN[0:32, 0:128], [R("FN", 0, 256)], [])
+            dma("y", T.ys[:], T.FN[32:64, 0:128], [R("FN", 0, 256)], [])
+            dma("y", T.ya[:], T.FN[0:32, 128:256], [R("FN", 0, 256)], [])
 
     for s, v in total.items():
         if clock["g"].get(s, 0) < v:

@@ -4,17 +4,18 @@ from concourse.bass import DstId, RemoteDMATransfer
 from concourse.mybir import AluOpType, ActivationFunctionType
 
 VIS = 4
-BF, F32, I32, U16 = "bfloat16", "float32", "int32", "uint16"
+BF, F16, F32, I32, U16 = "bfloat16", "float16", "float32", "int32", "uint16"
 
 SCRATCH = {}
 for _d, _l in (
     (BF, dict(OW0=4096, OW1=4096, OW2=4096, OW3=4096, VW0=4096, VW1=4096, VW2=4096, VW3=4096, NW=4096, NR=4096, NG=4096, OG=4096,
               DD=4096, AD=4096, SN=1536, XB=23 * 512, DFW=576, BB=512, ZW=1024, ZZ=512, ZL=512, NMB=5 * 256, YO=2048, YV=2048, YX=512,
               FL=64, FR=5 * 32, IDW=12 * 128, SEL=48, ZA=144, CK=128, C128=128, A16=32, A64=32, CB=64, ONE=512, QM=128,
-              EQ=(224, 8), LY=256, DP=(36, 4), DQ=(36, 4), GG=512, XH=128, OH=16 + 2048, AQ=512, HQ=128, FI=32, VT=512)),
-    (F32, dict(XD=144, XI=48, TB=128, SO=192, SP=128, EX=512, ES=512, PF=16, LF=128, YY=128, XS=64, XF=128, SR=256, NS=(16, 8), RS=128,
-               KS=256, W8=32, SQ=32, FC=32, F7=32, T3=32, T4=32, DX=64, PR=64, YH=256, LL=128, LH=128, HS=128, HM=128, DS=128, MS=128,
-               WIN=32, RID=512, Z2=512, C256=128, FO=256, FN=256, WP=1)),
+              EQ=(224, 8), LY=256, DP=(36, 4), DQ=(36, 4), GG=512, XH=128, OH=(129, 16), AQ=512, HQ=128, FI=32, VT=512, DM=512)),
+    (F16, dict(SO=192, SP=128, EX=512, ES=512, LF=128, YY=128, XS=64, XF=128)),
+    (F32, dict(XD=144, XI=48, TB=128, PF=16, SR=256, NS=(16, 8), RS=128, ZR=128, KS=256, W8=32, SQ=32, FC=32, F7=32, DC=32, T4=32,
+               DX=64, PR=64, YH=256, LL=128, LH=128, HS=128, HM=128, DS=128, MS=128, WIN=32, RID=512, Z2=512, C256=128, FO=256, FN=256,
+               WP=2)),
     (I32, dict(NMI=256, LI=128, PI=8, EI=256, EJ=256, EK=256, EL=256, T5=32, T8=32, SA=32, AB=64, CI=64, CJ=64)),
     (U16, dict(OFF=256, OFE=256, OFD=32, OFB=32, OF1=32, OFS=32, OFZ=32)),
 ):
@@ -178,7 +179,7 @@ def rank_program(g, core, T, topo):
         op("s", lambda: g.scalar.activation(ap(out), ap(in_), f, **kw), [in_, bias, scale], [out])
 
     def fill(out, w, v):
-        act(out, R("XD", 0, w), AF.Identity, v, 0.0)
+        act(out, R("TB", 0, w), AF.Identity, v, 0.0)
 
     def mm(out, l, r, start, stop):
         op("p", lambda: g.tensor.matmul(ap(out), ap(l), ap(r), start, stop), [l, r], [out])
@@ -212,9 +213,11 @@ def rank_program(g, core, T, topo):
         for i in range(4):
             mm(R3("P4", 0, 2, 32 * i, 32 * i + 32), R("ES", 128 * i, 128 * i + 128), R("YY", 0, 64), True, True)
 
-    def offsets():
+    def offsets(mid=None):
         for h in range(2):
-            cp(R("EI", 128 * h, 128 * h + 128), R("P3", 256 * h, 256 * h + 128))
+            ts(R("EI", 128 * h, 128 * h + 128), R("P3", 256 * h, 256 * h + 128), 2048.0, A.add)
+        if mid:
+            mid()
         for a in (0, 128):
             ts(R("EJ", a, a + 128), R("EI", a, a + 128), 4095, A.bitwise_and)
         for a in (0, 128):
@@ -230,100 +233,103 @@ def rank_program(g, core, T, topo):
     dma("y", T.LI[0:32, :], T.c0[:], [], [R("LI", 0, 128, 1, 0, 32)])
     dma("y", T.LI[32:64, :], T.s0[:], [], [R("LI", 0, 128, 1, 32, 64)])
     dma("y", T.OW0[:, 0:2048], T.vo[:, 0:2048], [], [R("OW0", 0, 2048)])
-    iota(R("PI", 0, 1), [[0, 1]], 0, 1, False)
-    iota(R("XD", 0, 144), [[1, 144]], 0, -1)
     iota(R("TB", 0, 128), [[1, 4], [4, 8], [32, 4]], 0, -1)
+    iota(R("XD", 0, 144), [[1, 144]], 0, -1)
     iota(R("EX", 0, 512), [[0, 64], [1, 8]], 0, 0)
     asel(R("EX", 0, 512), R("EX", 0, 512), A.is_equal, 0.0, -1)
+    iota(R("PI", 0, 1), [[0, 1]], 0, 1, False)
     asel(R("EX", 0, 512), R("EX", 0, 512), A.not_equal, 1.0, 0)
-    iota(R("XI", 0, 32), [[1, 32]], 0, 0)
     iota(R("XI", 32, 48), [[1, 8], [0, 2]], 0, 0)
-    iota(R("CK", 0, 128), [[0, 16], [-2, 8]], 7, 0)
     iota(R("ES", 0, 512), [[0, 512]], 1, 0)
     asel(R("ES", 0, 512), R("ES", 0, 512), A.is_equal, 0.0, -1)
+    iota(R("CK", 0, 128), [[0, 16], [-2, 8]], 7, 0)
     ms(R("NW", 0, 4096), 0.0)
+    ts(idw(I1), R("XD", 0, 128), 0.0, A.is_equal)
     ts(R("SO", 0, 128), R("TB", 0, 128), 0.0, A.is_equal)
     ts(R("SP", 0, 128), R("TB", 0, 128), 64.0, A.is_equal)
+    ms(R3("EQ", 0, 64, 0, 8), 0.0)
     ts(R("NMB", 0, 256), R("NMI", 0, 256), -256.0, A.add)
     dma("y", rows("NW", 0, 4096), T.NMB[:, 0:256], [R("NMB", 0, 256)], [R("NW", 0, 4096)])
     dma("y", T.OW0[:, 2048:4096], T.vo[:, 2048:4096], [], [R("OW0", 2048, 4096)])
     dma("y", ap(blk(0)), T.xo[:], [], [blk(0)])
     dma("y", T.VW0[:], T.vn[:], [], [R("VW0", 0, 4096)])
     dma("y", T.ZZ[:], T.z0[:], [], [R("ZZ", 0, 512)])
-    cp(R("LF", 0, 128, 1, 0, 64), R("LI", 0, 128, 1, 0, 64))
+    ts(R("LF", 0, 128, 1, 0, 32), R("LI", 0, 128, 1, 0, 32), -2048.0, A.add)
+    cp(R("LF", 0, 128, 1, 32, 64), R("LI", 0, 128, 1, 32, 64))
     for h in range(2):
         for q in range(2):
             mm(R("P7", 256 + 32 * h, 288 + 32 * h), R("SP" if q else "SO", 0, 128, 1, 0, 64), R("LF", 2 * h + q, 128, 4, 0, 64), q == 0, q == 1)
-    ts(R("PI", 1, 2), R("PI", 0, 1), 2, A.logical_shift_right, 3, A.bitwise_and)
-    ts(R("PI", 2, 3), R("PI", 0, 1), 1, A.logical_shift_right, 1, A.bitwise_and)
-    ts(R("PI", 3, 4), R("PI", 0, 1), 1, A.bitwise_and)
     ts(R("PI", 4, 5), R("PI", 0, 1), 15, A.bitwise_and)
     ts(R("PI", 5, 6), R("PI", 0, 1), 4, A.logical_shift_right)
-    ts(idw(I1), R("XD", 0, 128), 0.0, A.is_equal)
-    cp(R("PF", 0, 5), R("PI", 1, 6))
+    ts(R("PI", 1, 2), R("PI", 0, 1), 2, A.logical_shift_right, 3, A.bitwise_and)
     cp(R("YY", 0, 64), R("P7", 256, 320))
     places()
-    strides()
-    ts(pf(12), pf(3), 0.0, A.is_equal)
-    ts(SELA, R("XI", 32, 48), pf(4), A.is_equal)
-    ms(R3("EQ", 0, 224, 0, 8), 0.0)
-    act(R3("P2", 0, 32, 7, 8), R("XD", 0, 32), AF.Ln, 1.0, 0.0)
-    act(SELN, R("SEL", 16, 32, 2), scale=pf(12))
+    ts(R("PI", 2, 3), R("PI", 0, 1), 1, A.logical_shift_right, 1, A.bitwise_and)
+    ts(R("PI", 3, 4), R("PI", 0, 1), 1, A.bitwise_and)
+    cp(R("PF", 0, 5), R("PI", 1, 6))
+    ms(R3("EQ", 64, 144, 0, 8), 0.0)
+    act(R3("P2", 0, 32, 7, 8), R("TB", 0, 32), AF.Ln, 1.0, 0.0)
+    fill(R("C128", 0, 128), 128, 128.0)
     for d in range(1, 8):
         act(idw(d), idw(I1), scale=math.exp(STEP * d))
-    act(idw(IPEN), idw(I1), scale=-float(2 ** 17))
     act(idw(I4), idw(I1), scale=4.0)
     act(idw(INEG), idw(I1), scale=-1.0)
-    fill(R("C128", 0, 128), 128, 128.0)
-    act(SELK, R("SEL", 16, 32, 2), scale=16.0)
+    act(idw(IPEN), idw(I1), scale=-float(2 ** 17))
+    act(idw(IHALF), idw(I1), scale=0.5)
+    fill(R("RS", 0, 128), 128, 1.0)
+    fill(R("LL", 0, 128), 128, math.exp(-0.5))
+    fill(R("MS", 0, 128), 128, 1.0)
+    fill(R("ZR", 0, 128), 128, 0.0)
+    fill(R("RS", 0, 128, 8), 16, 0.0)
+    act(pf(5), pf(0), bias=3.5, scale=16.0)
+    act(pf(11), pf(3), bias=15.0, scale=-1.0)
+    act(pf(6), pf(1), bias=pf(5), scale=2048.0)
     offsets()
+    strides()
 
-    def consts_s():
-        act(SELM, R("SEL", 16, 32, 2), scale=-32.0)
-        act(idw(IHALF), idw(I1), scale=0.5)
-        act(pf(5), pf(0), bias=3.5, scale=16.0)
-        act(pf(8), pf(2), bias=512.0, scale=-512.0)
-        act(pf(6), pf(1), bias=pf(5), scale=2048.0)
-        act(pf(9), pf(2), scale=-512.0)
-        act(pf(7), pf(2), bias=pf(6), scale=8.0)
-        act(pf(10), pf(3), bias=512.0)
-        act(pf(11), pf(3), bias=15.0, scale=-1.0)
-        act(A16, R("XI", 0, 32), scale=16.0)
-        act(R("A64", 0, 32), R("XI", 0, 32), scale=64.0)
-        fill(R("RS", 0, 128), 128, 0.0)
-        fill(R("MS", 0, 128), 128, 1.0)
-        fill(R("DS", 0, 128), 128, -0.25)
-        fill(R("LL", 0, 128), 128, math.exp(-0.5))
-        fill(R("RS", 0, 128, 8), 16, -1e9)
-        fill(R("MS", 0, 128, 4), 32, 0.0)
-        fill(R("DS", 0, 128, 4), 32, 1e6)
-        fill(R("CB", 0, 32), 32, -112.0)
-        fill(R("CB", 32, 64), 32, 32 * 312.0)
-        fill(R("XH", 0, 64), 64, -1.0)
-        fill(R("QM", 0, 128), 128, -0.25)
-        fill(R("DFW", 512, 576), 64, 0.0)
-        fill(R("OH", 0, 16), 16, 0.0)
-        fill(R("SO", 128, 192), 64, 0.0)
-        fill(R("XF", 0, 128), 128, 0.0)
+    def consts_a():
+        ts(pf(12), pf(3), 0.0, A.is_equal)
+        ts(SELA, R("XI", 32, 48), pf(4), A.is_equal)
+        ts(SELN, R("XI", 32, 48, 2), pf(4), A.is_equal, pf(12), A.mult)
 
-    def consts_v():
+    def consts_b():
+        ms(R3("EQ", 144, 224, 0, 8), 0.0)
+        act(SELK, R("SEL", 16, 32, 2), scale=16.0)
+
+    def consts_w():
         tr(R("XS", 0, 64), R("YY", 0, 64))
-        ts(R("ZA", 0, 144), R("XD", 0, 144), pf(11), A.is_equal, 512.0, A.mult)
-        scan(R("LH", 0, 128), R("LL", 0, 128), R("RS", 0, 128), math.exp(32.5), A.mult, A.max)
+        scan(R("LH", 0, 128), R("LL", 0, 128), R("ZR", 0, 128), math.exp(32.5), A.mult, A.add)
         mm(R("P6", 0, 1), R("LH", 0, 128, 1, 0, 1), R("MS", 1, 2, 1, 0, 1), True, True)
-        mm(AFL, idw(I1), R("CB", 32, 64), True, True)
-        cp(R("WP", 0, 1), R("P6", 0, 1))
 
-    iota(R("DP", 0, 144), [[0, 144]], 0, 0)
-    iota(R("DQ", 0, 144), [[0, 144]], 0, 0)
+    def consts_c():
+        act(pf(7), pf(2), bias=pf(6), scale=8.0)
+        cp(R("WP", 0, 1), R("P6", 0, 1))
+        fill(R("QM", 0, 128), 128, -0.25)
+        fill(R("DS", 0, 128), 128, -0.25)
+        fill(R("MS", 0, 128, 4), 32, 0.0)
+        act(R("WP", 1, 2), R("WP", 0, 1), scale=-1.0)
+
+    def consts_d():
+        fill(R("DS", 0, 128, 4), 32, 1e6)
+        act(SELM, R("SEL", 16, 32, 2), scale=-32.0)
+        act(pf(8), pf(2), bias=512.0, scale=-512.0)
+        act(pf(9), pf(2), scale=-512.0)
+        act(pf(10), pf(3), bias=512.0)
+
+    def consts_e():
+        ts(R("ZA", 0, 144), R("XD", 0, 144), pf(11), A.is_equal, 512.0, A.mult)
+        ts(pf(13), pf(4), 1.5, A.is_lt, 2048.0, A.mult)
+
     iota(R("SN", 512, 1024), [[0, 512]], 0, 0)
     iota(R("C256", 0, 128), [[0, 128]], 256, 0)
 
     def consts_g():
-        iota(R("ONE", 0, 512), [[0, 512]], 1, 0)
-        iota(R("RID", 0, 512), [[1, 512]], 0, 0)
-        iota(R("SN", 0, 512), [[1, 512]], -256, 0)
-        iota(R("SN", 1024, 1536), [[1, 512]], -256, 0)
+        for r, w, st, v in ((R("A64", 0, 32), 32, 64, 0), (R("DP", 0, 144), 144, 0, 0), (R("CB", 0, 32), 32, 0, -112),
+                            (R("CB", 32, 64), 32, 0, 32 * 312), (R("XH", 0, 64), 64, 0, -1), (R("OH", 0, 16), 16, 0, 0),
+                            (R("DQ", 0, 144), 144, 0, 0), (R("DFW", 512, 576), 64, 0, 0), (A16, 32, 16, 0), (R("ONE", 0, 512), 512, 0, 1),
+                            (R("RID", 0, 512), 512, 1, 0), (R("SN", 0, 512), 512, 1, -256), (R("SN", 1024, 1536), 512, 1, -256),
+                            (R("SO", 128, 192), 64, 0, 0), (R("XF", 0, 128), 128, 0, 0)):
+            iota(r, [[st, w]], v, 0)
 
     for t in range(VIS):
         last = t == VIS - 1
@@ -333,6 +339,7 @@ def rank_program(g, core, T, topo):
         bo, bv, b2 = (17, 20, 16) if last else (5 * t, 5 * t + 3, 5 * t + 3)
         Z = R("ZZ", 0, 512)
         OFF = lambda a, b: R("OFF", a, b)
+        OFS = R("OFS", 0, 32)
         NP = lambda h, k0=0, k1=8: R3("P%d" % h, 0, 16, k0, k1)
         LM = lambda h, k1=8: R3("P2", 16 * h, 16 * h + 16, 0, k1)
         KB = lambda h: ("P4", 128) if h == 0 else ("P5", 0)
@@ -417,35 +424,50 @@ def rank_program(g, core, T, topo):
 
         def pick(h):
             a, b = 16 * h, 16 * h + 16
-            scan(R("KS", 8 * a, 8 * b), R("RS", 0, 128), KEY(h), 0.0, A.add, A.max)
+            scan(R("KS", 8 * a, 8 * b), R("RS", 0, 128), KEY(h), 0.0, A.mult, A.max)
             ts(R("W8", a, b), R("KS", 8 * a + 7, 8 * b, 8), 16 * MAG, A.add, 16 * MAG, A.subtract)
             tt(padded("DP", h), R("W8", a, b), R("KS", 8 * a + 7, 8 * b, 8), A.subtract)
 
         def late(tp):
             if tp >= 0:
-                act(R("VW%d" % (tp + 1), 512 * tp, 512 * tp + 512), ind(blk(5 * tp + 3, 3), R("OFS", 0, 32)))
+                act(R("VW%d" % (tp + 1), 512 * tp, 512 * tp + 512), ind(blk(5 * tp + 3, 3), OFS))
 
-        def late_z(tp):
-            if tp >= 0:
-                ts(R("OFZ", 0, 32), R("P6", 192, 224), pf(3), A.add)
-                act(Z, ind(R("ZW", 0, 1024), R("OFZ", 0, 32)))
+        z_list = lambda: ts(R("OFZ", 0, 32), R("P6", 192, 224), pf(3), A.add)
+        z_new = lambda: act(Z, ind(R("ZW", 0, 1024), R("OFZ", 0, 32)))
 
-        ngv(0); ngs(1); ngv(2); ngv(3); npe(0)
-        act(R("SR", 0, 256), R3("P4", 0, 2, 0, 128), scale=1.0 / 7)
-        ngv(4); ngs(6); ngs(5)
+        stride7 = lambda: ts(R("SR", 0, 256), R3("P4", 0, 2, 0, 128), 1.0 / 7, A.mult)
+        if t > 0:
+            stride7()
+        ngv(0); ngs(1); ngv(2); ngs(3)
+        if t == 0:
+            consts_a()
+        npe(0)
+        if t > 0:
+            act(R(OW, sl[0] - 512, sl[0]), ind(blk(5 * t - 5, 3), OFS))
+        ngv(4)
+        if t == 0:
+            ngs(5)
+            stride7()
+            consts_b()
+        else:
+            ngv(5)
+        ngs(6)
+        eq(0)
+        ngv(7)
         late(t - 1)
         forward()
         if t == 0:
             consts_g()
-        og(0, 512)
-        eq(0)
-        ngv(7)
+        og(0, 512 if t == 0 else 256)
         ln(0); npe(1); pen(0)
-        og(512, 1024)
+        og(512 if t == 0 else 256, 1024)
         el(0)
-        og(1024, 2048)
+        if t == 0:
+            consts_w()
         refill()
-        dg(0, 1024)
+        dg(0, 512)
+        og(1024, 2048)
+        dg(512, 1024)
         eq(1)
         og(2048, 3072)
         ln(1); pen(1)
@@ -455,7 +477,7 @@ def rank_program(g, core, T, topo):
         el(1)
         ab(1024, 2048); kpe(0, 2048)
         if t > 0:
-            ts(R("OFZ", 0, 32), R("P6", 192, 224), pf(3), A.add)
+            z_list()
         dg(2048, 2560)
         og(3584, 4096)
         ab(2048, 2560); kpe(2048, 2560)
@@ -464,14 +486,15 @@ def rank_program(g, core, T, topo):
         dg(3584, 3840); ab(3584, 3840)
         dg(3840, 4096); ab(3840, 4096); kpe(3584, 4096)
         if t == 0:
-            consts_s()
-            consts_v()
+            consts_c()
             cp(R("XB", 1, 512, 2), R("XB", 1025, 1536, 2))
         else:
-            act(Z, ind(R("ZW", 0, 1024), R("OFZ", 0, 32)))
+            z_new()
         pick(0)
-        act(R("T4", 0, 32), SS, scale=8.0)
+        act(R("T4", 0, 32), SS, bias=2048.0, scale=8.0)
         pick(1)
+        if t == 0:
+            mm(AFL, idw(I1), R("CB", 32, 64), True, True)
         mm(R("P6", 0, 32), idw(I1), R("A64", 0, 32), True, False)
         t_to_w(R("P6", 0, 32), "DP", IHALF, False)
         act(R("SQ", 0, 32), R("W8", 0, 32), AF.Square, 592.0, 1.0 / 16)
@@ -486,14 +509,23 @@ def rank_program(g, core, T, topo):
         act(R("DFW", 0, 512), ind(R("DD", 0, 4096), R("OFD", 0, 32)))
         act(R("F7", 0, 32), R("FC", 0, 32), bias=3.5, scale=-0.5)
         act(R("BB", 0, 512), R("DFW", 0, 512), AF.Abs)
-        act(R("ZW", 0, 512), Z, AF.Relu, -1.0)
+        mm(R("P0", 0, 512), idw(IHALF), Z, True, False)
+        mm(R("P0", 0, 512), R("QM", 0, 128, 1, 0, 1), R("ONE", 0, 512, 1, 0, 1), False, False)
+        mm(R("P0", 0, 512), idw(IHALF), R("BB", 0, 512), False, True)
         ts(R("AB", 32, 64), R("T5", 0, 32), 9, A.logical_shift_right, 31, A.bitwise_and)
         ts(R("AB", 0, 32), R("T5", 0, 32), 5, A.logical_shift_right, 15, A.bitwise_and)
         cp(R("XH", 64, 128, 2), R("AB", 32, 64))
         ts(R("XH", 65, 128, 2), R("AB", 32, 64), -16.0, A.add)
         tt(R("XH", 0, 64, 2), CNT, R("AB", 0, 32), A.max)
-        for v in range(16):
+        for v in range(13):
             ts(R("OH", 16 + v, 2064, 16), R("XH", 0, 128), float(v), A.is_equal, R("WP", 0, 1), A.mult)
+        for i in range(3):
+            act(R("VT", i, 384, 3), R("XH", 0, 128), AF.Abs, -13.0 - i)
+        act(R3("OH", 1, 129, 13, 16), R("VT", 0, 384), AF.Relu, R("WP", 0, 1), R("WP", 1, 2))
+        if t == 0:
+            consts_d()
+        act(R("Z2", 0, 512), R("P0", 0, 512), bias=MAG)
+        act(R("ZW", 0, 512), Z, AF.Relu, -1.0)
         for h in range(2):
             for q in range(2):
                 for gr in range(8):
@@ -503,29 +535,24 @@ def rank_program(g, core, T, topo):
         for h in range(2):
             cp(padded("DQ", h), R("AB", 32 + 16 * h, 48 + 16 * h))
         t_to_w(R("P6", 32, 64), "DQ", I1, True)
-        mm(R("P0", 0, 512), idw(IHALF), Z, True, False)
-        mm(R("P0", 0, 512), idw(IHALF), R("BB", 0, 512), False, False)
-        mm(R("P0", 0, 512), R("QM", 0, 128, 1, 0, 1), R("ONE", 0, 512, 1, 0, 1), False, True)
-        ts(R("FI", 0, 32), CNT, 8.0, A.is_lt, 32.0, A.mult)
+        mm(R("P1", 0, 512), idw(I1), XR, True, False)
+        tt(R("DC", 0, 32), R("F7", 0, 32), SS, A.mult)
+        tt(R("CI", 32, 64), R("T4", 0, 32), CC, A.add)
         ts(R("SA", 0, 32), R("T8", 0, 32), 1023, A.bitwise_and)
-        tt(R("DX", 0, 64, 2), R("F7", 0, 32), SS, A.mult)
-        tt(R("T3", 0, 32), R("T4", 0, 32), CC, A.add)
+        tt(R("CI", 0, 32), R("CI", 32, 64), R("DC", 0, 32), A.subtract)
         tt(R("DX", 1, 64, 2), R("SA", 0, 32), SS, A.subtract)
-        if last:
-            tt(R("CI", 0, 32), R("T3", 0, 32), R("DX", 0, 64, 2), A.subtract)
-            cp(R("CI", 32, 64), R("T3", 0, 32))
-            ts(R("CJ", 0, 64), R("CI", 0, 64), 4095, A.bitwise_and)
-            cp(CC, R("CJ", 0, 32))
-            tt(R("DX", 0, 64, 2), R("CJ", 32, 64), R("CJ", 0, 32), A.subtract)
-        else:
-            tt(CC, R("T3", 0, 32), R("DX", 0, 64, 2), A.subtract)
+        ts(R("CJ", 0, 64), R("CI", 0, 64), 4095, A.bitwise_and)
+        ts(R("FI", 0, 32), CNT, 8.0, A.is_lt, 32.0, A.mult)
+        ts(CC, R("CJ", 0, 32), -2048.0, A.add)
+        tt(R("DX", 0, 64, 2), R("CJ", 32, 64), R("CJ", 0, 32), A.subtract)
         H = R("P7", 128, 256)
         ts(R("YH", 0, 128), H, 1.0, A.max, math.exp(-32.0), A.mult)
+        scan(R("HM", 0, 128), R("MS", 0, 128), H, 0.0, A.mult, A.max)
         ts(R("YH", 128, 256), H, 1.0, A.min, math.exp(32.0), A.mult)
         act(R("LH", 0, 128), R("YH", 0, 128), AF.Ln)
-        act(R("LL", 0, 128), R("YH", 128, 256), AF.Ln, math.exp(-40.0))
         act(R("P2", 256, 384), R("LH", 0, 128), bias=192.23, scale=-1.0)
-        scan(R("HM", 0, 128), R("MS", 0, 128), R("YH", 128, 256), 0.0, A.mult, A.max)
+        act(R("LL", 0, 128), R("YH", 128, 256), AF.Ln, math.exp(-40.0))
+        act(R("ZW", 512, 1024), R("Z2", 0, 512), bias=-MAG)
         ts(R("FL", 0, 32), R("HM", 3, 128, 4), 0.0, A.is_gt, pf(8), A.mult)
         ts(R("FL", 32, 64), R("HM", 3, 128, 4), 0.0, A.is_gt, pf(9), A.mult)
         if last:
@@ -533,22 +560,23 @@ def rank_program(g, core, T, topo):
         else:
             send([(-1, R("FR", 32 * t, 32 * t + 32), R("FL", 0, 32))])
         cp(R("OFB", 0, 32), R("P6", 32, 64))
+        if t == 0:
+            consts_e()
         tt(R("HQ", 0, 128), R("P2", 256, 384), R("LL", 0, 128), A.subtract)
-        act(R("Z2", 0, 512), R("P0", 0, 512), bias=MAG)
-        act(R("ZW", 512, 1024), R("Z2", 0, 512), bias=-MAG)
         scan(R("HS", 0, 128), R("DS", 0, 128), R("HQ", 0, 128), 0.0, A.add, A.min)
         ts(R("WIN", 0, 32), R("HS", 3, 128, 4), 4.0, A.mult, -509.0, A.add)
         ts(R("OF1", 0, 32), R("HS", 3, 128, 4), 4.0, A.mult, -509.0, A.add)
 
         def objects():
-            tt(R("VT", 0, 512), ind(R("DFW", 0, 576), R("OF1", 0, 32)), XR, A.add)
-            ts(blk(b2), R("VT", 0, 512), 0.0, A.max, 255.0, A.min)
+            ts(blk(b2), R("P1", 0, 512), 0.0, A.max, 255.0, A.min)
             send([(3, blk(22), blk(b2)), (4, blk(20), blk(b2))] if last else [(-1, blk(b2 + 2), blk(b2))])
 
         def choice():
             mm(R("P6", 128, 160), idw(I1), A16, True, False)
             mm(R("P6", 128, 160), idw(I1), R("FR", 128, 160) if last else R("FL", 32, 64), False, False)
             mm(R("P6", 128, 160), idw(I1), R("FR", 32 * t, 32 * t + 32), False, True)
+
+        choice_list = lambda: ts(OFS, R("P6", 128, 160), pf(10), A.add)
 
         def z_offsets():
             mm(R("P6", 192, 224), idw(I1), A16, True, False)
@@ -560,56 +588,58 @@ def rank_program(g, core, T, topo):
             mm(AFL, idw(I1), R("FI", 0, 32), False, False)
             for s in range(4):
                 mm(sub5(160, s), R("AQ", s, 512, 4), SELM, False, s == 3)
-        if last:
-            objects()
+
+        act(R("DM", 0, 512), ind(R("DFW", 0, 576), R("OF1", 0, 32)))
         tt(R("AQ", 0, 512), ind(R("WIN", 0, 32), R("OFB", 0, 32)), R("RID", 0, 512), A.is_equal)
         for s in range(4):
             mm(R3("P6", 16 + 8 * (s >> 1), 24 + 8 * (s >> 1), 2 * (s & 1), 2 * (s & 1) + 2), R("AQ", s, 512, 4), SELA, True, True)
+        mm(R("P1", 0, 512), idw(I1), R("DM", 0, 512), False, True)
         tt(R("PR", 0, 64), R("P6", 64, 128), R("DX", 0, 64), A.mult)
-        OFS = R("OFS", 0, 32)
         if not last:
             tt(R("XS", 0, 64), R("XS", 0, 64), R("PR", 0, 64), A.add)
             tr(R("YY", 0, 64), R("XS", 0, 64))
             places()
-            choice()
             objects()
-            ts(OFS, R("P6", 128, 160), pf(10), A.add)
+            choice()
+            offsets(choice_list)
             act(R("NW", *sl), ind(R("SN", 0, 1536), OFS))
-            act(R("OW%d" % (t + 1), *sl), ind(blk(bo, 3), OFS))
             strides()
             z_offsets()
             flags()
-            offsets()
         else:
+            for h in range(2):
+                ts(padded("DP", h), mk("P6", 0, 128, (slice(16 + 8 * h, 24 + 8 * h), slice(0, 4, 2))), 512.0, A.mult)
+            mm(R("P6", 192, 224), idw(I1), A16, True, False)
+            t_to_w(R("P6", 192, 224), "DP", I1, False)
             flags()
-            z_offsets()
+            objects()
+            z_list()
+            z_new()
+            choice()
             for h in range(2):
                 tt(R("XF", 64 * h, 64 * h + 32), R("XS", 32 * h, 32 * h + 32), R("PR", 32 * h, 32 * h + 32), A.add)
             for h in range(2):
-                ts(R("XF", 64 * h + 32, 64 * h + 64, 2), R("P5", 160 + 16 * h, 176 + 16 * h), -32 * 312.0, A.add, 1.0 / 32, A.mult)
+                ts(R("XF", 64 * h + 32, 64 * h + 64, 2), R("P5", 160 + 16 * h, 176 + 16 * h), 1.0 / 32, A.mult, -312.0 - 2048.0, A.add)
             tr(R("YY", 0, 128), R("XF", 0, 128))
             for s in range(4):
                 h, q = s >> 1, s & 1
                 mm(R("P7", 256 + s, 512, 4), R("SO", 64 * q, 64 * q + 128), R("YY", 64 * h, 64 * h + 64), True, True)
-            late_z(t)
-            send([(3, R("ZL", 0, 512), Z)])
-            cp(R("FO", 0, 256), R("P7", 256, 512))
-            send([(3, R("FN", 0, 256), R("FO", 0, 256))])
-            choice()
-            ts(OFS, R("P6", 128, 160), pf(10), A.add)
+            choice_list()
+            ts(R("FO", 0, 256), R("P7", 256, 512), pf(13), A.add)
+            send([(3, R("ZL", 0, 512), Z), (3, R("FN", 0, 256), R("FO", 0, 256))])
             cp(R("NR", *sl), ind(R("SN", 0, 1536), OFS))
-            act(R("YO", *sl), ind(blk(bo, 3), OFS))
             dma("g", T.yn[:, 1536:2048], rows("NR", *sl), [R("NR", *sl), R("yn", 0, 2048)], [], accum_op=A.add)
+            act(R("YO", *sl), ind(blk(bo, 3), OFS))
             dma("y", T.yo[:, 1536:2048], T.YO[:, 1536:2048], [R("YO", *sl)], [])
-            act(R("YV", *sl), ind(blk(bv, 3), OFS))
-            dma("s", T.yv[:, 1536:2048], T.YV[:, 1536:2048], [R("YV", *sl)], [])
-            cp(R("YX", 0, 512, 2), R("XB", 512 * 22, 512 * 23, 2))
-            cp(R("YX", 1, 512, 2), R("XB", 512 * 20 + 1, 512 * 21, 2))
-            dma("y", T.yx[:], T.YX[:], [R("YX", 0, 512)], [])
+            cp(R("YV", *sl), ind(blk(bv, 3), OFS))
+            dma("y", T.yv[:, 1536:2048], T.YV[:, 1536:2048], [R("YV", *sl)], [])
+            act(R("YX", 0, 512, 2), R("XB", 512 * 22, 512 * 23, 2))
+            act(R("YX", 1, 512, 2), R("XB", 512 * 20 + 1, 512 * 21, 2))
+            dma("s", T.yx[:], T.YX[:], [R("YX", 0, 512)], [])
             dma("y", T.yz[:], T.ZL[:], [R("ZL", 0, 512)], [])
-            dma("y", T.yc[:], T.FN[0:32, 0:128], [R("FN", 0, 256)], [])
-            dma("y", T.ys[:], T.FN[32:64, 0:128], [R("FN", 0, 256)], [])
-            dma("y", T.ya[:], T.FN[0:32, 128:256], [R("FN", 0, 256)], [])
+            dma("s", T.yc[:], T.FN[0:32, 0:128], [R("FN", 0, 256)], [])
+            dma("s", T.ys[:], T.FN[32:64, 0:128], [R("FN", 0, 256)], [])
+            dma("s", T.ya[:], T.FN[0:32, 128:256], [R("FN", 0, 256)], [])
 
     for s, v in total.items():
         if clock["g"].get(s, 0) < v:

@@ -10,14 +10,14 @@ SCRATCH = {}
 for _d, _l in (
     (BF, dict(OW0=4096, OW1=4096, OW2=4096, OW3=4096, VW0=4096, VW1=4096, VW2=4096, VW3=4096, NW=4096, NR=4096, NG=4096, OG=4096,
               DD=4096, AD=4096, SN=1536, XB=23 * 512, DFW=576, BB=512, ZW=1024, ZZ=512, ZL=512, NMB=5 * 256, YO=2048, YV=2048, YX=512,
-              FL=64, FR=5 * 32, IDW=12 * 128, SEL=48, ZA=144, CK=128, C128=128, A16=32, A64=32, CB=64, ONE=512, QM=128,
-              EQ=(224, 8), LY=256, DP=(36, 4), DQ=(36, 4), GG=512, XH=128, OH=(129, 16), AQ=512, HQ=128, FI=32, VT=512, DM=512)),
-    (F16, dict(SO=192, SP=128, EX=512, ES=512, LF=128, YY=128, XS=64, XF=128)),
+              IDW=12 * 128, SEL=48, ZA=144, CK=136, A16=32, A64=32, CB=64, ONE=512, QM=128,
+              EQ=(224, 8), LY=256, DP=(36, 4), DQ=(36, 4), GG=512, XH=128, OH=(129, 16), AQ=512, HQ=128, FI=32, VT=512, DM=512, XL=512)),
+    (F16, dict(SO=192, SP=128, EX=512, ES=512, EM=512, LF=128, YY=128, XS=64, XF=128)),
     (F32, dict(XD=144, XI=48, TB=128, PF=16, SR=256, NS=(16, 8), RS=128, ZR=128, KS=256, W8=32, SQ=32, FC=32, F7=32, DC=32, T4=32,
                DX=64, PR=64, YH=256, LL=128, LH=128, HS=128, HM=128, DS=128, MS=128, WIN=32, RID=512, Z2=512, C256=128, FO=256, FN=256,
-               WP=2)),
-    (I32, dict(NMI=256, LI=128, PI=8, EI=256, EJ=256, EK=256, EL=256, T5=32, T8=32, SA=32, AB=64, CI=64, CJ=64)),
-    (U16, dict(OFF=256, OFE=256, OFD=32, OFB=32, OF1=32, OFS=32, OFZ=32)),
+               WP=2, JT=32, FL=32, FM=32)),
+    (I32, dict(NMI=256, LI=128, PI=8, EI=256, EJ=256, EK=256, EL=256, T5=32, T8=32, SA=32, AB=96, CI=64, CJ=64)),
+    (U16, dict(OFF=256, OFE=256, OFD=32, OFB=32, OF1=32, OFS=32, OFR=5 * 16, OFZ=32)),
 ):
     for _k, _n in _l.items():
         SCRATCH[_k] = ("sbuf", [128] + (list(_n) if isinstance(_n, tuple) else [_n]), _d)
@@ -212,12 +212,13 @@ def rank_program(g, core, T, topo):
     def strides():
         for i in range(4):
             mm(R3("P4", 0, 2, 32 * i, 32 * i + 32), R("ES", 128 * i, 128 * i + 128), R("YY", 0, 64), True, True)
+        for i in range(4):
+            for j, w in enumerate(("EX", "EM")):
+                mm(R3("P3", 0, 2, 128 + 32 * i, 160 + 32 * i), R(w, 128 * i, 128 * i + 128), R("YY", 0, 64), j == 0, j == 1)
 
-    def offsets(mid=None):
+    def offsets():
         for h in range(2):
-            ts(R("EI", 128 * h, 128 * h + 128), R("P3", 256 * h, 256 * h + 128), 2048.0, A.add)
-        if mid:
-            mid()
+            cp(R("EI", 128 * h, 128 * h + 128), R("P3", 256 * h, 256 * h + 128))
         for a in (0, 128):
             ts(R("EJ", a, a + 128), R("EI", a, a + 128), 4095, A.bitwise_and)
         for a in (0, 128):
@@ -240,9 +241,10 @@ def rank_program(g, core, T, topo):
     iota(R("PI", 0, 1), [[0, 1]], 0, 1, False)
     asel(R("EX", 0, 512), R("EX", 0, 512), A.not_equal, 1.0, 0)
     iota(R("XI", 32, 48), [[1, 8], [0, 2]], 0, 0)
-    iota(R("ES", 0, 512), [[0, 512]], 1, 0)
-    asel(R("ES", 0, 512), R("ES", 0, 512), A.is_equal, 0.0, -1)
-    iota(R("CK", 0, 128), [[0, 16], [-2, 8]], 7, 0)
+    iota(R("ES", 0, 512), [[0, 512]], 0, 0)
+    asel(R("EM", 0, 512), R("ES", 0, 512), A.not_equal, -15.0, -1)
+    asel(R("ES", 0, 512), R("ES", 0, 512), A.not_equal, 0.5, -1)
+    iota(R("CK", 0, 136), [[0, 17], [-2, 8]], 7, 0)
     ms(R("NW", 0, 4096), 0.0)
     ts(idw(I1), R("XD", 0, 128), 0.0, A.is_equal)
     ts(R("SO", 0, 128), R("TB", 0, 128), 0.0, A.is_equal)
@@ -251,11 +253,12 @@ def rank_program(g, core, T, topo):
     ts(R("NMB", 0, 256), R("NMI", 0, 256), -256.0, A.add)
     dma("y", rows("NW", 0, 4096), T.NMB[:, 0:256], [R("NMB", 0, 256)], [R("NW", 0, 4096)])
     dma("y", T.OW0[:, 2048:4096], T.vo[:, 2048:4096], [], [R("OW0", 2048, 4096)])
-    dma("y", ap(blk(0)), T.xo[:], [], [blk(0)])
     dma("y", T.VW0[:], T.vn[:], [], [R("VW0", 0, 4096)])
+    dma("y", ap(blk(0)), T.xo[:], [], [blk(0)])
     dma("y", T.ZZ[:], T.z0[:], [], [R("ZZ", 0, 512)])
-    ts(R("LF", 0, 128, 1, 0, 32), R("LI", 0, 128, 1, 0, 32), -2048.0, A.add)
-    cp(R("LF", 0, 128, 1, 32, 64), R("LI", 0, 128, 1, 32, 64))
+    ts(R("EI", 0, 128, 1, 0, 64), R("LI", 0, 128, 1, 0, 64), 2048.0, A.add)
+    ts(R("EJ", 0, 128, 1, 0, 64), R("EI", 0, 128, 1, 0, 64), 4095, A.bitwise_and)
+    ts(R("LF", 0, 128, 1, 0, 64), R("EJ", 0, 128, 1, 0, 64), -2048.0, A.add)
     for h in range(2):
         for q in range(2):
             mm(R("P7", 256 + 32 * h, 288 + 32 * h), R("SP" if q else "SO", 0, 128, 1, 0, 64), R("LF", 2 * h + q, 128, 4, 0, 64), q == 0, q == 1)
@@ -267,59 +270,57 @@ def rank_program(g, core, T, topo):
     ts(R("PI", 2, 3), R("PI", 0, 1), 1, A.logical_shift_right, 1, A.bitwise_and)
     ts(R("PI", 3, 4), R("PI", 0, 1), 1, A.bitwise_and)
     cp(R("PF", 0, 5), R("PI", 1, 6))
-    ms(R3("EQ", 64, 144, 0, 8), 0.0)
-    act(R3("P2", 0, 32, 7, 8), R("TB", 0, 32), AF.Ln, 1.0, 0.0)
-    fill(R("C128", 0, 128), 128, 128.0)
+    act(R("QM", 0, 128), R("TB", 0, 128), AF.Ln, math.exp(-0.25), 0.0)
     for d in range(1, 8):
-        act(idw(d), idw(I1), scale=math.exp(STEP * d))
+        act(idw(d), idw(I1), scale=math.exp(2.0 * d))
     act(idw(I4), idw(I1), scale=4.0)
-    act(idw(INEG), idw(I1), scale=-1.0)
     act(idw(IPEN), idw(I1), scale=-float(2 ** 17))
     act(idw(IHALF), idw(I1), scale=0.5)
     fill(R("RS", 0, 128), 128, 1.0)
     fill(R("LL", 0, 128), 128, math.exp(-0.5))
-    fill(R("MS", 0, 128), 128, 1.0)
     fill(R("ZR", 0, 128), 128, 0.0)
     fill(R("RS", 0, 128, 8), 16, 0.0)
     act(pf(5), pf(0), bias=3.5, scale=16.0)
     act(pf(11), pf(3), bias=15.0, scale=-1.0)
     act(pf(6), pf(1), bias=pf(5), scale=2048.0)
+    ts(pf(12), pf(3), 0.0, A.is_equal)
+    ts(SELA, R("XI", 32, 48), pf(4), A.is_equal)
+    ts(SELN, R("XI", 32, 48, 2), pf(4), A.is_equal, pf(12), A.mult)
     offsets()
-    strides()
-
-    def consts_a():
-        ts(pf(12), pf(3), 0.0, A.is_equal)
-        ts(SELA, R("XI", 32, 48), pf(4), A.is_equal)
-        ts(SELN, R("XI", 32, 48, 2), pf(4), A.is_equal, pf(12), A.mult)
 
     def consts_b():
-        ms(R3("EQ", 144, 224, 0, 8), 0.0)
+        ms(R3("EQ", 64, 224, 0, 8), 0.0)
         act(SELK, R("SEL", 16, 32, 2), scale=16.0)
 
-    def consts_w():
-        tr(R("XS", 0, 64), R("YY", 0, 64))
-        scan(R("LH", 0, 128), R("LL", 0, 128), R("ZR", 0, 128), math.exp(32.5), A.mult, A.add)
-        mm(R("P6", 0, 1), R("LH", 0, 128, 1, 0, 1), R("MS", 1, 2, 1, 0, 1), True, True)
+    def consts_w(i):
+        if i == 0:
+            tr(R("XS", 0, 64), R("YY", 0, 64))
+        if i == 1:
+            scan(R("LH", 0, 128), R("LL", 0, 128), R("ZR", 0, 128), math.exp(32.5), A.mult, A.add)
+        if i == 2:
+            mm(R("P6", 0, 1), R("LH", 0, 128, 1, 0, 1), R("MS", 1, 2, 1, 0, 1), True, True)
 
     def consts_c():
         act(pf(7), pf(2), bias=pf(6), scale=8.0)
         cp(R("WP", 0, 1), R("P6", 0, 1))
-        fill(R("QM", 0, 128), 128, -0.25)
-        fill(R("DS", 0, 128), 128, -0.25)
-        fill(R("MS", 0, 128, 4), 32, 0.0)
+        act(pf(10), pf(4), scale=-32.0)
         act(R("WP", 1, 2), R("WP", 0, 1), scale=-1.0)
 
     def consts_d():
+        fill(R("DS", 0, 128), 128, -0.25)
+        act(R("JT", 0, 32), R("JT", 0, 32), bias=pf(10))
         fill(R("DS", 0, 128, 4), 32, 1e6)
+
+    def consts_f():
+        act(R("RID", 0, 512), R("RID", 0, 512), bias=127.25, scale=0.25)
         act(SELM, R("SEL", 16, 32, 2), scale=-32.0)
-        act(pf(8), pf(2), bias=512.0, scale=-512.0)
-        act(pf(9), pf(2), scale=-512.0)
-        act(pf(10), pf(3), bias=512.0)
 
     def consts_e():
         ts(R("ZA", 0, 144), R("XD", 0, 144), pf(11), A.is_equal, 512.0, A.mult)
         ts(pf(13), pf(4), 1.5, A.is_lt, 2048.0, A.mult)
 
+    iota(R("MS", 0, 128), [[0, 32], [1, 4]], 0, 0)
+    iota(R("JT", 0, 32), [[1, 2], [32, 16]], 512, 2)
     iota(R("SN", 512, 1024), [[0, 512]], 0, 0)
     iota(R("C256", 0, 128), [[0, 128]], 256, 0)
 
@@ -328,8 +329,21 @@ def rank_program(g, core, T, topo):
                             (R("CB", 32, 64), 32, 0, 32 * 312), (R("XH", 0, 64), 64, 0, -1), (R("OH", 0, 16), 16, 0, 0),
                             (R("DQ", 0, 144), 144, 0, 0), (R("DFW", 512, 576), 64, 0, 0), (A16, 32, 16, 0), (R("ONE", 0, 512), 512, 0, 1),
                             (R("RID", 0, 512), 512, 1, 0), (R("SN", 0, 512), 512, 1, -256), (R("SN", 1024, 1536), 512, 1, -256),
-                            (R("SO", 128, 192), 64, 0, 0), (R("XF", 0, 128), 128, 0, 0)):
+                            (R("SO", 128, 192), 64, 0, 0), (R("XF", 0, 128), 128, 0, 0), (blk(20), 512, 0, 0), (blk(22), 512, 0, 0)):
             iota(r, [[st, w]], v, 0)
+
+    def onward(t, a, b):
+        d, names = (3, ("YO", "YV")) if t == VIS - 1 else (-1, ("OW%d" % (t + 1), "VW%d" % (t + 1)))
+        return [(d, R(names[0], a, b), R("OW%d" % t, a, b)), (d, R(names[1], a, b), R("VW%d" % t, a, b))]
+
+    def early(t):
+        a = 512 * t
+        if t == VIS - 1:
+            send(onward(t, 0, a - 512))
+            return
+        old = [(-1, blk(5 * t + 1), R("OW%d" % t, a, a + 512)), (-1, blk(5 * t + 4), R("VW%d" % t, a, a + 512))]
+        send(old + ([(-1, blk(2), blk(0))] if t == 0 else []) + (onward(t, 0, 512) if t == 2 else []))
+        send(onward(t, a + 512, 4096))
 
     for t in range(VIS):
         last = t == VIS - 1
@@ -339,30 +353,31 @@ def rank_program(g, core, T, topo):
         bo, bv, b2 = (17, 20, 16) if last else (5 * t, 5 * t + 3, 5 * t + 3)
         Z = R("ZZ", 0, 512)
         OFF = lambda a, b: R("OFF", a, b)
-        OFS = R("OFS", 0, 32)
+        even = lambda f, w, win, tp: f(R(w, 512 * tp, 512 * tp + 512, 2), ind(win, R("OFR", 16 * tp, 16 * tp + 16)))
+        odd = lambda f, w, win: f(R(w, sl[0] + 1, sl[1], 2), ind(win, R("OFR", 64, 80) if last else R("OFS", 16, 32)))
         NP = lambda h, k0=0, k1=8: R3("P%d" % h, 0, 16, k0, k1)
-        LM = lambda h, k1=8: R3("P2", 16 * h, 16 * h + 16, 0, k1)
-        KB = lambda h: ("P4", 128) if h == 0 else ("P5", 0)
-        KEY = lambda h: R(KB(h)[0], KB(h)[1], KB(h)[1] + 128)
-        E = lambda h, d, k0: R3("EQ", 112 * h + 16 * (d - 1), 112 * h + 16 * d, k0, 8)
+        LM = lambda h: R("P2", 128 * h, 128 * h + 128)
+        KB = ("P7", "P5")
+        KEY = lambda h: R(KB[h], 0, 128)
+        E = lambda h, d, k1: R3("EQ", 112 * h + 16 * (d - 1), 112 * h + 16 * d, 0, k1)
 
         def forward():
             if t > 0:
                 for j in range(2):
                     dma("y", T.NMB[2 * t - 2 + j:128:16, 256 * t:256 * t + 256], rows("NW", sl[0] - 512 + 256 * j, sl[0] - 256 + 256 * j),
-                        [R("NW", sl[0] - 512, sl[0])], [R("NMB", 256 * t, 256 * t + 256)])
+                        [R("NW", sl[0] - 512, sl[0])], [R("NMB", 256 * t + 128 * j, 256 * t + 128 * j + 128)])
+                send(([(3, blk(19), XR), (4, blk(17), XR)] if last else [(-1, blk(bo + 2), XR)]) + onward(t, sl[0] - 512, sl[0]))
             send([(3 if last else -1, R("NMB", 256 * t + 256, 256 * t + 512), R("NMB", 256 * t, 256 * t + 256))])
-            if last:
-                send([(3, blk(19), XR), (4, blk(17), XR)])
-                send([(3, R("YO", 0, 1536), R(OW, 0, 1536)), (3, R("YV", 0, 1536), R(VW, 0, 1536))])
-            else:
-                send([(-1, blk(bo + 1), R(OW, *sl)), (-1, blk(bv + 1), R(VW, *sl)), (-1, blk(bo + 2), XR)])
-                send([(-1, R("OW%d" % (t + 1), 0, 4096), R(OW, 0, 4096)), (-1, R("VW%d" % (t + 1), 0, 4096), R(VW, 0, 4096))])
+            if t == 0:
+                early(0)
 
         def refill():
             w = "NR" if last else "NW"
-            dma("y", rows(w, 0, 4096), T.NMB[:, 256 * t + 256:256 * t + 512], [R("NMB", 256 * t + 256, 256 * t + 512)], [R(w, 0, 4096)])
-            dma("y", rows("SN", 512, 1024), rows(w, *sl), [R(w, *sl)], [R("SN", 512, 1024)])
+            nb = R("NMB", 256 * t + 256, 256 * t + 512)
+            for j in range(2):
+                dma("y", rows("SN", 512 + 256 * j, 768 + 256 * j), T.NMB[2 * t + j:128:16, 256 * t + 256:256 * t + 512], [nb],
+                    [R("SN", 512 + 256 * j, 768 + 256 * j)])
+            dma("y", rows(w, 0, 4096), T.NMB[:, 256 * t + 256:256 * t + 512], [nb], [R(w, 0, 4096)])
             if t == 0:
                 dma("y", T.yn[:], T.C256[:], [R("C256", 0, 128)], [R("yn", 0, 2048)])
                 dma("y", ap(blk(18)), T.vo[:, 1536:2048], [], [blk(18)])
@@ -388,26 +403,26 @@ def rank_program(g, core, T, topo):
         def eq(h):
             cp(R3("NS", 0, 16, 0, 8), NP(h))
             for d in range(1, 8):
-                tt(E(h, d, d), NP(h, 0, 8 - d), R3("NS", 0, 16, d, 8), A.is_equal)
+                tt(E(h, d, 8 - d), NP(h, 0, 8 - d), R3("NS", 0, 16, d, 8), A.is_equal)
             for d in range(1, 8):
-                mm(LM(h, 8 - d), idw(d), E(h, d, d), d == 1, d == 7)
+                mm(LM(h), E(h, d, 8), idw(d), d == 1, d == 7)
 
         def pen(h):
-            mm(KEY(h), idw(I1), R("CK", 0, 128), True, False)
+            mm(R(KB[h], 0, 136), idw(I1), R("CK", 0, 136), True, False)
             for d in range(1, 8):
-                mm(KEY(h), idw(IPEN), E(h, d, 0), False, False)
+                mm(R(KB[h], d, 128 + d), idw(IPEN), E(h, d, 8), False, False)
 
         def ln(h):
-            ly = R("LY", 128 * h, 128 * h + 128)
-            act(ly, LM(h), AF.Ln, math.exp(32.03), math.exp(31.89))
-            mm(R("P3", 256 * h + 128, 256 * h + 256), ly, idw(I4), True, False)
-            mm(R("P3", 256 * h + 128, 256 * h + 256), R("C128", 0, 128), idw(INEG), False, True)
+            act(R("LY", 128 * h, 128 * h + 128), LM(h), AF.Ln, math.exp(30.0), math.exp(29.96))
 
-        def el(h):
+        def el(h, between=lambda i: None):
             a, b = 128 * h, 128 * h + 128
-            tt(R("P7", 0, 128), R("P3", 256 * h + 128, 256 * h + 256), R("SR", a, b), A.mult)
-            tt(R("EK", a, b), R("P7", 0, 128), R("EJ", a, b), A.add)
+            tt(R("SR", a, b), R("P4", 2 * a, 2 * a + 128), R("LY", a, b), A.mult)
+            between(0)
+            tt(R("EK", a, b), R("P3", 2 * a + 128, 2 * a + 256), R("SR", a, b), A.add)
+            between(1)
             ts(R("EL", a, b), R("EK", a, b), 4095, A.bitwise_and)
+            between(2)
             cp(R("OFE", a, b), R("EL", a, b))
 
         def dg(a, b):
@@ -418,9 +433,8 @@ def rank_program(g, core, T, topo):
 
         def kpe(a, b):
             h, p0 = a // 2048, (a % 2048) // 16
-            bank, c0 = KB(h)
             for k in range(16):
-                mm(R(bank, c0 + k, c0 + 128, 16, p0, p0 + (b - a) // 16), R("AD", a + k, b, 16), SELK, False, k == 15)
+                mm(R(KB[h], k, 128, 16, p0, p0 + (b - a) // 16), R("AD", a + k, b, 16), SELK, False, k == 15)
 
         def pick(h):
             a, b = 16 * h, 16 * h + 16
@@ -428,56 +442,42 @@ def rank_program(g, core, T, topo):
             ts(R("W8", a, b), R("KS", 8 * a + 7, 8 * b, 8), 16 * MAG, A.add, 16 * MAG, A.subtract)
             tt(padded("DP", h), R("W8", a, b), R("KS", 8 * a + 7, 8 * b, 8), A.subtract)
 
-        def late(tp):
-            if tp >= 0:
-                act(R("VW%d" % (tp + 1), 512 * tp, 512 * tp + 512), ind(blk(5 * tp + 3, 3), OFS))
-
         z_list = lambda: ts(R("OFZ", 0, 32), R("P6", 192, 224), pf(3), A.add)
         z_new = lambda: act(Z, ind(R("ZW", 0, 1024), R("OFZ", 0, 32)))
 
-        stride7 = lambda: ts(R("SR", 0, 256), R3("P4", 0, 2, 0, 128), 1.0 / 7, A.mult)
-        if t > 0:
-            stride7()
         ngv(0); ngs(1); ngv(2); ngs(3)
-        if t == 0:
-            consts_a()
         npe(0)
-        if t > 0:
-            act(R(OW, sl[0] - 512, sl[0]), ind(blk(5 * t - 5, 3), OFS))
-        ngv(4)
         if t == 0:
-            ngs(5)
-            stride7()
+            strides()
+            ngv(4); ngs(5)
             consts_b()
+            ngs(6)
         else:
-            ngv(5)
-        ngs(6)
+            cp(R("NG", 2048, 2816), ind(R("NW", 0, 4096), OFF(128, 176)))
+            act(R("NG", 2816, 3584), ind(R("NW", 0, 4096), OFF(176, 224)))
         eq(0)
         ngv(7)
-        late(t - 1)
+        if t > 0:
+            even(act, VW, blk(5 * t - 2, 3), t - 1)
         forward()
         if t == 0:
             consts_g()
-        og(0, 512 if t == 0 else 256)
+        og(0, 512)
         ln(0); npe(1); pen(0)
-        og(512 if t == 0 else 256, 1024)
-        el(0)
-        if t == 0:
-            consts_w()
+        og(512, 1024)
+        el(0, consts_w if t == 0 else lambda i: None)
         refill()
-        dg(0, 512)
         og(1024, 2048)
-        dg(512, 1024)
+        dg(0, 512)
         eq(1)
+        dg(512, 1024)
         og(2048, 3072)
         ln(1); pen(1)
-        dg(1024, 2048)
+        dg(1024, 1664)
         ab(0, 1024)
         og(3072, 3584)
-        el(1)
+        el(1, lambda i: dg(1664 + 128 * i, 1792 + 128 * i))
         ab(1024, 2048); kpe(0, 2048)
-        if t > 0:
-            z_list()
         dg(2048, 2560)
         og(3584, 4096)
         ab(2048, 2560); kpe(2048, 2560)
@@ -489,19 +489,23 @@ def rank_program(g, core, T, topo):
             consts_c()
             cp(R("XB", 1, 512, 2), R("XB", 1025, 1536, 2))
         else:
+            z_list()
             z_new()
         pick(0)
-        act(R("T4", 0, 32), SS, bias=2048.0, scale=8.0)
+        act(R("T4", 0, 32), SS, bias=0.0 if last else 2048.0, scale=8.0)
         pick(1)
         if t == 0:
             mm(AFL, idw(I1), R("CB", 32, 64), True, True)
         mm(R("P6", 0, 32), idw(I1), R("A64", 0, 32), True, False)
         t_to_w(R("P6", 0, 32), "DP", IHALF, False)
         act(R("SQ", 0, 32), R("W8", 0, 32), AF.Square, 592.0, 1.0 / 16)
+        act(R("ZW", 0, 512), Z, AF.Relu, -1.0)
         tt(R("FC", 0, 32), R("W8", 0, 32), R("KS", 7, 256, 8), A.subtract)
-        ts(R("T8", 0, 32), R("W8", 0, 32), 0.125, A.mult, 1.0, A.add)
         tt(R("T5", 0, 32), R("SQ", 0, 32), AFL, A.add)
+        ts(R("T8", 0, 32), R("W8", 0, 32), 0.125, A.mult, 1.0, A.add)
+        ts(R("AB", 32, 64), R("T5", 0, 32), 10, A.logical_shift_right, 15, A.bitwise_and)
         ts(R("OFD", 0, 32), R("P6", 0, 32), pf(7), A.add)
+        ts(R("AB", 64, 96), R("T5", 0, 32), 1, A.logical_shift_right, 16, A.bitwise_and)
         mm(CNT, idw(I1), R("CB", 0, 32), True, False)
         tt(R("GG", 0, 512), ind(R("AD", 0, 4096), R("OFD", 0, 32)), Z, A.is_lt)
         for s in range(4):
@@ -512,39 +516,40 @@ def rank_program(g, core, T, topo):
         mm(R("P0", 0, 512), idw(IHALF), Z, True, False)
         mm(R("P0", 0, 512), R("QM", 0, 128, 1, 0, 1), R("ONE", 0, 512, 1, 0, 1), False, False)
         mm(R("P0", 0, 512), idw(IHALF), R("BB", 0, 512), False, True)
-        ts(R("AB", 32, 64), R("T5", 0, 32), 9, A.logical_shift_right, 31, A.bitwise_and)
-        ts(R("AB", 0, 32), R("T5", 0, 32), 5, A.logical_shift_right, 15, A.bitwise_and)
-        cp(R("XH", 64, 128, 2), R("AB", 32, 64))
-        ts(R("XH", 65, 128, 2), R("AB", 32, 64), -16.0, A.add)
+        tt(R("XH", 64, 128, 2), R("AB", 32, 64), R("AB", 64, 96), A.add)
+        ts(R("AB", 0, 32), R("T5", 0, 32), 6, A.logical_shift_right, 15, A.bitwise_and)
+        ts(R("XH", 65, 128, 2), R("XH", 64, 128, 2), -16.0, A.add)
+        cp(padded("DQ", 0), R("XH", 64, 96, 2))
         tt(R("XH", 0, 64, 2), CNT, R("AB", 0, 32), A.max)
+        cp(padded("DQ", 1), R("XH", 96, 128, 2))
         for v in range(13):
             ts(R("OH", 16 + v, 2064, 16), R("XH", 0, 128), float(v), A.is_equal, R("WP", 0, 1), A.mult)
         for i in range(3):
             act(R("VT", i, 384, 3), R("XH", 0, 128), AF.Abs, -13.0 - i)
         act(R3("OH", 1, 129, 13, 16), R("VT", 0, 384), AF.Relu, R("WP", 0, 1), R("WP", 1, 2))
+        act(R("Z2", 0, 512), R("P0", 0, 512), bias=MAG)
         if t == 0:
             consts_d()
-        act(R("Z2", 0, 512), R("P0", 0, 512), bias=MAG)
-        act(R("ZW", 0, 512), Z, AF.Relu, -1.0)
+        act(R("ZW", 512, 1024), R("Z2", 0, 512), bias=-MAG)
         for h in range(2):
             for q in range(2):
                 for gr in range(8):
                     c, e, p0 = 16 * h + 2 * gr + q, gr & 1, 32 * (gr >> 1)
                     mm(R("P7", 128 + 2 * h + q, 256, 4, p0, p0 + 32), R("OH", 16 + 32 * c - 16 * e, 48 + 32 * c - 16 * e),
                        R("OH", 1040 + 32 * c, 1072 + 32 * c), e == 0, e == 1)
-        for h in range(2):
-            cp(padded("DQ", h), R("AB", 32 + 16 * h, 48 + 16 * h))
-        t_to_w(R("P6", 32, 64), "DQ", I1, True)
-        mm(R("P1", 0, 512), idw(I1), XR, True, False)
+        t_to_w(R("P6", 32, 64), "DQ", I4, True)
+        if not last:
+            mm(R("P1", 0, 512), idw(I1), XR, True, False)
         tt(R("DC", 0, 32), R("F7", 0, 32), SS, A.mult)
         tt(R("CI", 32, 64), R("T4", 0, 32), CC, A.add)
         ts(R("SA", 0, 32), R("T8", 0, 32), 1023, A.bitwise_and)
         tt(R("CI", 0, 32), R("CI", 32, 64), R("DC", 0, 32), A.subtract)
         tt(R("DX", 1, 64, 2), R("SA", 0, 32), SS, A.subtract)
         ts(R("CJ", 0, 64), R("CI", 0, 64), 4095, A.bitwise_and)
-        ts(R("FI", 0, 32), CNT, 8.0, A.is_lt, 32.0, A.mult)
         ts(CC, R("CJ", 0, 32), -2048.0, A.add)
         tt(R("DX", 0, 64, 2), R("CJ", 32, 64), R("CJ", 0, 32), A.subtract)
+        if t == 0:
+            consts_e()
         H = R("P7", 128, 256)
         ts(R("YH", 0, 128), H, 1.0, A.max, math.exp(-32.0), A.mult)
         scan(R("HM", 0, 128), R("MS", 0, 128), H, 0.0, A.mult, A.max)
@@ -552,31 +557,28 @@ def rank_program(g, core, T, topo):
         act(R("LH", 0, 128), R("YH", 0, 128), AF.Ln)
         act(R("P2", 256, 384), R("LH", 0, 128), bias=192.23, scale=-1.0)
         act(R("LL", 0, 128), R("YH", 128, 256), AF.Ln, math.exp(-40.0))
-        act(R("ZW", 512, 1024), R("Z2", 0, 512), bias=-MAG)
-        ts(R("FL", 0, 32), R("HM", 3, 128, 4), 0.0, A.is_gt, pf(8), A.mult)
-        ts(R("FL", 32, 64), R("HM", 3, 128, 4), 0.0, A.is_gt, pf(9), A.mult)
-        if last:
-            send([(3, R("FR", 96, 128), R("FL", 0, 32)), (4, R("FR", 128, 160), R("FL", 32, 64))])
-        else:
-            send([(-1, R("FR", 32 * t, 32 * t + 32), R("FL", 0, 32))])
-        cp(R("OFB", 0, 32), R("P6", 32, 64))
-        if t == 0:
-            consts_e()
+        ts(R("FL", 0, 32), R("HM", 3, 128, 4), 0.0, A.is_gt, 512.0, A.mult)
+        ts(R("OFB", 0, 32), R("P6", 32, 64), 3.0, A.add)
+        tt(R("FM", 0, 16), R("JT", 0, 16), R("FL", 0, 16), A.add)
+        ts(R("FI", 0, 32), CNT, 8.0, A.is_lt, 32.0, A.mult)
+        cp(R("OFS", 0, 16), R("FM", 0, 16))
         tt(R("HQ", 0, 128), R("P2", 256, 384), R("LL", 0, 128), A.subtract)
+        if not last:
+            send([(-1, R("OFR", 16 * t, 16 * t + 16), R("OFS", 0, 16))])
+        if t == 0:
+            consts_f()
+        tt(R("FM", 16, 32), R("JT", 16, 32), R("FL", 16, 32), A.subtract)
         scan(R("HS", 0, 128), R("DS", 0, 128), R("HQ", 0, 128), 0.0, A.add, A.min)
-        ts(R("WIN", 0, 32), R("HS", 3, 128, 4), 4.0, A.mult, -509.0, A.add)
+        own_list = lambda: cp(R("OFS", 16, 32), R("FM", 16, 32))
+        if last:
+            own_list()
         ts(R("OF1", 0, 32), R("HS", 3, 128, 4), 4.0, A.mult, -509.0, A.add)
+        if last:
+            send([(3, R("OFR", 48, 64), R("OFS", 0, 16)), (4, R("OFR", 64, 80), R("OFS", 16, 32))])
 
         def objects():
             ts(blk(b2), R("P1", 0, 512), 0.0, A.max, 255.0, A.min)
-            send([(3, blk(22), blk(b2)), (4, blk(20), blk(b2))] if last else [(-1, blk(b2 + 2), blk(b2))])
-
-        def choice():
-            mm(R("P6", 128, 160), idw(I1), A16, True, False)
-            mm(R("P6", 128, 160), idw(I1), R("FR", 128, 160) if last else R("FL", 32, 64), False, False)
-            mm(R("P6", 128, 160), idw(I1), R("FR", 32 * t, 32 * t + 32), False, True)
-
-        choice_list = lambda: ts(OFS, R("P6", 128, 160), pf(10), A.add)
+            send([(-1, blk(b2 + 2), blk(b2))])
 
         def z_offsets():
             mm(R("P6", 192, 224), idw(I1), A16, True, False)
@@ -589,57 +591,74 @@ def rank_program(g, core, T, topo):
             for s in range(4):
                 mm(sub5(160, s), R("AQ", s, 512, 4), SELM, False, s == 3)
 
-        act(R("DM", 0, 512), ind(R("DFW", 0, 576), R("OF1", 0, 32)))
-        tt(R("AQ", 0, 512), ind(R("WIN", 0, 32), R("OFB", 0, 32)), R("RID", 0, 512), A.is_equal)
+        if not last:
+            for e in range(2):
+                act(R("DM", e, 512, 2), ind(R("DFW", 0, 576), R("OF1", 16 * e, 16 * e + 16)))
+        tt(R("AQ", 0, 512), ind(R("HS", 0, 128), R("OFB", 0, 32)), R("RID", 0, 512), A.is_equal)
+        if not last:
+            own_list()
+            odd(act, "NW", R("SN", 0, 1024))
+            odd(act, "OW%d" % (t + 1), blk(bo, 2))
         for s in range(4):
             mm(R3("P6", 16 + 8 * (s >> 1), 24 + 8 * (s >> 1), 2 * (s & 1), 2 * (s & 1) + 2), R("AQ", s, 512, 4), SELA, True, True)
-        mm(R("P1", 0, 512), idw(I1), R("DM", 0, 512), False, True)
-        tt(R("PR", 0, 64), R("P6", 64, 128), R("DX", 0, 64), A.mult)
+        PR = lambda a, b: R("P2", 384 + a, 384 + b)
         if not last:
-            tt(R("XS", 0, 64), R("XS", 0, 64), R("PR", 0, 64), A.add)
+            mm(R("P1", 0, 512), idw(I1), R("DM", 0, 512), False, True)
+            tt(PR(0, 64), R("P6", 64, 128), R("DX", 0, 64), A.mult)
+            tt(R("XS", 0, 64), PR(0, 64), R("XS", 0, 64), A.add)
             tr(R("YY", 0, 64), R("XS", 0, 64))
             places()
             objects()
-            choice()
-            offsets(choice_list)
-            act(R("NW", *sl), ind(R("SN", 0, 1536), OFS))
+            early(t + 1)
+            offsets()
+            odd(act, "VW%d" % (t + 1), blk(bv, 2))
+            even(act, "NW", R("SN", 0, 1536), t)
+            even(cp, "OW%d" % (t + 1), blk(bo, 3), t)
             strides()
             z_offsets()
             flags()
         else:
+            for e in range(2):
+                tt(R("DM", 256 * e, 256 * e + 256), ind(R("DFW", 0, 576), R("OF1", 16 * e, 16 * e + 16)), R("XB", 512 * 15 + e, 512 * 16, 2), A.add)
             for h in range(2):
-                ts(padded("DP", h), mk("P6", 0, 128, (slice(16 + 8 * h, 24 + 8 * h), slice(0, 4, 2))), 512.0, A.mult)
-            mm(R("P6", 192, 224), idw(I1), A16, True, False)
-            t_to_w(R("P6", 192, 224), "DP", I1, False)
+                act(padded("DP", h), mk("P6", 0, 128, (slice(16 + 8 * h, 24 + 8 * h), slice(0, 4, 2))), scale=512.0)
             flags()
-            objects()
-            z_list()
+            mm(R("P0", 0, 32), idw(I1), A16, True, False)
+            t_to_w(R("P0", 0, 32), "DP", I1, False)
+            tt(PR(0, 64), R("P6", 64, 128), R("DX", 0, 64), A.mult)
+            ts(blk(b2), R("DM", 0, 512), 0.0, A.max, 255.0, A.min)
+            send([(3 + e, R("XL", 256 * e, 256 * e + 256), R("XB", 512 * b2 + 256 * e, 512 * b2 + 256 * e + 256)) for e in range(2)])
+            ts(R("OFZ", 0, 32), R("P0", 0, 32), pf(3), A.add)
             z_new()
-            choice()
+            send([(3, R("ZL", 0, 512), Z)])
             for h in range(2):
-                tt(R("XF", 64 * h, 64 * h + 32), R("XS", 32 * h, 32 * h + 32), R("PR", 32 * h, 32 * h + 32), A.add)
+                tt(R("XF", 64 * h, 64 * h + 32), PR(32 * h, 32 * h + 32), R("XS", 32 * h, 32 * h + 32), A.add)
             for h in range(2):
                 ts(R("XF", 64 * h + 32, 64 * h + 64, 2), R("P5", 160 + 16 * h, 176 + 16 * h), 1.0 / 32, A.mult, -312.0 - 2048.0, A.add)
             tr(R("YY", 0, 128), R("XF", 0, 128))
             for s in range(4):
                 h, q = s >> 1, s & 1
                 mm(R("P7", 256 + s, 512, 4), R("SO", 64 * q, 64 * q + 128), R("YY", 64 * h, 64 * h + 64), True, True)
-            choice_list()
             ts(R("FO", 0, 256), R("P7", 256, 512), pf(13), A.add)
-            send([(3, R("ZL", 0, 512), Z), (3, R("FN", 0, 256), R("FO", 0, 256))])
-            cp(R("NR", *sl), ind(R("SN", 0, 1536), OFS))
+            send([(3, R("FN", 0, 256), R("FO", 0, 256))])
+            even(cp, "NR", R("SN", 0, 1536), t)
+            odd(cp, "NR", R("SN", 0, 1024))
             dma("g", T.yn[:, 1536:2048], rows("NR", *sl), [R("NR", *sl), R("yn", 0, 2048)], [], accum_op=A.add)
-            act(R("YO", *sl), ind(blk(bo, 3), OFS))
+            even(act, "YO", blk(bo, 3), t)
+            odd(act, "YO", blk(bo, 2))
             dma("y", T.yo[:, 1536:2048], T.YO[:, 1536:2048], [R("YO", *sl)], [])
-            cp(R("YV", *sl), ind(blk(bv, 3), OFS))
-            dma("y", T.yv[:, 1536:2048], T.YV[:, 1536:2048], [R("YV", *sl)], [])
-            act(R("YX", 0, 512, 2), R("XB", 512 * 22, 512 * 23, 2))
-            act(R("YX", 1, 512, 2), R("XB", 512 * 20 + 1, 512 * 21, 2))
-            dma("s", T.yx[:], T.YX[:], [R("YX", 0, 512)], [])
+            cp(R("XB", 512 * 20 + 1, 512 * 21, 2), R("XL", 256, 512))
+            cp(R("XB", 512 * 22, 512 * 23, 2), R("XL", 0, 256))
+            odd(act, "YV", blk(bv, 2))
+            even(cp, "YV", blk(bv, 3), t)
             dma("y", T.yz[:], T.ZL[:], [R("ZL", 0, 512)], [])
-            dma("s", T.yc[:], T.FN[0:32, 0:128], [R("FN", 0, 256)], [])
-            dma("s", T.ys[:], T.FN[32:64, 0:128], [R("FN", 0, 256)], [])
-            dma("s", T.ya[:], T.FN[0:32, 128:256], [R("FN", 0, 256)], [])
+            dma("s", T.yv[:, 1536:2048], T.YV[:, 1536:2048], [R("YV", *sl)], [])
+            cp(R("YX", 0, 512, 2), R("XL", 0, 256))
+            cp(R("YX", 1, 512, 2), R("XL", 256, 512))
+            dma("s", T.yx[:], T.YX[:], [R("YX", 0, 512)], [])
+            dma("y", T.yc[:], T.FN[0:32, 0:128], [R("FN", 0, 256)], [])
+            dma("y", T.ys[:], T.FN[32:64, 0:128], [R("FN", 0, 256)], [])
+            dma("y", T.ya[:], T.FN[0:32, 128:256], [R("FN", 0, 256)], [])
 
     for s, v in total.items():
         if clock["g"].get(s, 0) < v:

import math
import numpy as np
from concourse.bass import DstId, RemoteDMATransfer
from concourse.mybir import AluOpType, ActivationFunctionType

VIS = 4
BF, F16, F32, I32, U16 = "bfloat16", "float16", "float32", "int32", "uint16"

SCRATCH = {}
for _d, _l in (
    (BF, dict(OW0=4096, OW1=4096, OW2=4096, OW3=4096, VW0=4096, VW1=4096, VW2=4096, VW3=4096, NW=4096, NR=4096, NG=4096, OG=4096,
              DD=4096, AD=4096, SN=1536, XB=23 * 512, DFW=576, BB=512, ZW=1024, ZZ=512, ZL=512, NMB=5 * 256, YO=2048, YV=2048, YX=512,
              IDW=12 * 128, SEL=48, ZA=144, CK=136, A16=32, A64=32, CB=64, ONE=512, QM=128,
              EQ=(224, 8), LY=256, DP=(36, 4), DQ=(36, 4), GG=512, XH=128, OH=(129, 16), AQ=512, HQ=128, FI=32, VT=512, DM=512, XL=512)),
    (F16, dict(SO=192, SP=128, EX=512, ES=512, EM=512, LF=128, YY=128, XS=64, XF=128)),
    (F32, dict(XD=144, XI=48, TB=128, PF=16, SR=256, NS=(16, 8), RS=128, ZR=128, KS=256, W8=32, SQ=32, FC=32, F7=32, DC=32, T4=32,
               DX=64, PR=64, YH=256, LL=128, LH=128, HS=128, HM=128, DS=128, MS=128, WIN=32, RID=512, Z2=512, C256=128, FO=256, FN=256,
               WP=2, JT=32, FL=32, FM=32)),
    (I32, dict(NMI=256, LI=128, PI=8, EI=256, EJ=256, EK=256, EL=256, T5=32, T8=32, SA=32, AB=96, CI=64, CJ=64)),
    (U16, dict(OFF=256, OFE=256, OFD=32, OFB=32, OF1=32, OFS=32, OFR=5 * 16, OFZ=32)),
):
    for _k, _n in _l.items():
        SCRATCH[_k] = ("sbuf", [128] + (list(_n) if isinstance(_n, tuple) else [_n]), _d)
for _i, _s in enumerate(((64, 8), (64, 8), (64, 8), (2, 256), (2, 256), (512,), (128, 4), (512,))):
    SCRATCH["P%d" % _i] = ("psum", [128] + list(_s), F32)

SEMAPHORES = (["qv", "qs", "qp", "qg"] + ["d%d" % i for i in range(48)] + ["l%d" % i for i in range(32)] + ["a%d" % i for i in range(32)])

MAG = float(3 * 2 ** 22)
STEP = 1.75
MASKS = {}


def R(n, c0, c1, st=1, p0=0, p1=128):
    sh = SCRATCH[n][1] if n in SCRATCH else [128, 4096]
    if len(sh) == 3:
        w = sh[2]
        if c0 // w == (c1 - 1) // w:
            return mk(n, p0, p1, (c0 // w, slice(c0 % w, (c1 - 1) % w + 1, st)))
        if st == 1:
            return R3(n, c0 // w, c1 // w, 0, w, p0, p1)
        return mk(n, p0, p1, (slice(c0 // w, (c1 + w - 1) // w, st // w), c0 % w))
    return mk(n, p0, p1, (slice(c0, c1, st),))


def R3(n, a0, a1, k0, k1, p0=0, p1=128):
    return mk(n, p0, p1, (slice(a0, a1), slice(k0, k1)))


def mk(n, p0, p1, idx):
    sh = SCRATCH[n][1][1:] if n in SCRATCH else [4096]
    key = (tuple(sh), str(idx))
    if key not in MASKS:
        cols = np.arange(int(np.prod(sh))).reshape(sh)[idx].reshape(-1)
        bits = np.zeros(int(np.prod(sh)), np.uint8)
        bits[cols] = 1
        MASKS[key] = int.from_bytes(np.packbits(bits, bitorder="little").tobytes(), "little")
    return (n, p0, p1, idx, MASKS[key])


def rank_program(g, core, T, topo):
    rank = T.rank_of(core)
    if rank is None:
        return
    A = AluOpType
    AF = ActivationFunctionType
    n = len(T.cores)
    peer = lambda d: T.cores[(rank + d) % n]
    Q = {"v": g.vector, "s": g.scalar, "p": g.tensor, "g": g, "y": g.sync}
    QS = {"v": "qv", "s": "qs", "p": "qp", "g": "qg"}
    cnt = {k: 0 for k in QS}
    clock = {k: {} for k in Q}
    hist = {}
    total = {}
    nd = [0, 0]

    def ap(r):
        if r[0] == "ind":
            return ap(r[1]).indirect(ap(r[2]))
        return T[r[0]][(slice(r[1], r[2]),) + r[3]]

    def flat(rs):
        o = []
        for r in rs:
            if isinstance(r, tuple):
                o += [r[1], r[2]] if r[0] == "ind" else [r]
        return o

    def sync(q, reads, writes):
        need = {}
        for r, w in [(x, False) for x in reads] + [(x, True) for x in writes]:
            ps = r[0][0] == "P" and r[0][1:].isdigit()
            for (r2, w2, q2, tok, ck) in hist.get(r[0], []):
                if q2 == q and q == "p":
                    continue
                if (ps and q2 != q) or ((w or w2) and r[1] < r2[2] and r2[1] < r[2] and r[4] & r2[4]):
                    if need.get(tok[0], (0, None))[0] < tok[1]:
                        need[tok[0]] = (tok[1], ck)
        for s, (v, ck) in sorted(need.items(), key=lambda kv: -len(kv[1][1])):
            if clock[q].get(s, 0) < v:
                Q[q].wait_ge(T.sem[s], v)
                clock[q][s] = v
                for s2, v2 in ck.items():
                    if clock[q].get(s2, 0) < v2:
                        clock[q][s2] = v2

    def note(q, reads, writes, tok, ck):
        total[tok[0]] = max(total.get(tok[0], 0), tok[1])
        for r in writes:
            h = [x for x in hist.get(r[0], []) if not (r[1] <= x[0][1] and x[0][2] <= r[2] and x[0][4] & ~r[4] == 0)]
            hist[r[0]] = h + [(r, True, q, tok, ck)]
        for r in reads:
            hist.setdefault(r[0], []).append((r, False, q, tok, ck))

    def op(q, fn, reads, writes):
        reads, writes = flat(reads), flat(writes)
        sync(q, reads, writes)
        cnt[q] += 1
        fn().then_inc(T.sem[QS[q]], 1)
        note(q, reads, writes, (QS[q], cnt[q]), dict(clock[q]))

    def dma(q, out, in_, reads, writes, **kw):
        sync(q, reads, writes)
        s = "d%d" % nd[0]
        nd[0] += 1
        Q[q].dma_start(out, in_, **kw).then_inc(T.sem[s], 16)
        note("dma", reads, writes, (s, 16), dict(clock[q]))

    def send(items):
        reads = [p[2] for p in items]
        sync("g", reads, [])
        s, sem = "l%d" % nd[1], "a%d" % nd[1]
        nd[1] += 1
        trs = []
        for i, (d, land, src) in enumerate(items):
            engs = topo.engines(core, peer(d))
            per = 1 << int(math.log2(len(engs) // len(items)))
            rid, pid, _e = topo.addr(peer(d))
            trs.append((rid, pid, sum(1 << e for e in engs[i * per:(i + 1) * per]), ap(land), ap(src)))
        if len(items) == 1:
            rid, pid, mask, land, src = trs[0]
            g.remote_dma(land, src, T.sem[sem], T.sem[s], pid, rid, mask)
        else:
            g.remote_dma_fused([RemoteDMATransfer(dst_ids=[DstId(rid=rid, pnc=pid)], dma_engine_mask=mask, remote_sem=T.sem[sem], src=src, dst=land)
                                for rid, pid, mask, land, src in trs], local_sem=T.sem[s])
        note("dma", reads, [], (s, per * len(items)), dict(clock["g"]))
        note("dma", [], [p[1] for p in items], (sem, per * len(items)), {})

    def sc(x):
        return ap(x) if isinstance(x, tuple) else x

    def ts(out, in0, s1, o0, s2=None, o1=None):
        if o1 is None:
            op("v", lambda: g.vector.tensor_scalar(ap(out), ap(in0), sc(s1), None, o0), [in0, s1], [out])
        else:
            op("v", lambda: g.vector.tensor_scalar(ap(out), ap(in0), sc(s1), sc(s2), o0, o1), [in0, s1, s2], [out])

    def tt(out, in0, in1, o):
        op("v", lambda: g.vector.tensor_tensor(ap(out), ap(in0), ap(in1), o), [in0, in1], [out])

    def cp(out, in_):
        op("v", lambda: g.vector.tensor_copy(ap(out), ap(in_)), [in_], [out])

    def ms(out, v):
        op("v", lambda: g.vector.memset(ap(out), v), [], [out])

    def tr(out, in_):
        op("v", lambda: g.vector.transpose(ap(out), ap(in_)), [in_], [out])

    def scan(out, d0, d1, init, o0, o1):
        op("v", lambda: g.vector.tensor_tensor_scan(ap(out), ap(d0), ap(d1), init, o0, o1), [d0, d1], [out])

    def act(out, in_, f=AF.Identity, bias=None, scale=None):
        kw = {}
        if bias is not None:
            kw["bias"] = sc(bias)
        if scale is not None:
            kw["scale"] = sc(scale)
        op("s", lambda: g.scalar.activation(ap(out), ap(in_), f, **kw), [in_, bias, scale], [out])

    def fill(out, w, v):
        act(out, R("TB", 0, w), AF.Identity, v, 0.0)

    def mm(out, l, r, start, stop):
        op("p", lambda: g.tensor.matmul(ap(out), ap(l), ap(r), start, stop), [l, r], [out])

    def iota(out, pat, base, mult, flag=True):
        if flag:
            op("g", lambda: g.iota(ap(out), pat, base, mult, allow_small_or_imprecise_dtypes=True), [], [out])
        else:
            op("g", lambda: g.iota(ap(out), pat, base, mult), [], [out])

    def asel(out, in_, cmp, fillv, base):
        op("g", lambda: g.affine_select(ap(out), ap(in_), [[-32, 4], [-2, 16], [0, 8]], cmp, fillv, base, 1), [in_], [out])

    ind = lambda w, o: ("ind", w, o)
    idw = lambda i, a=0, st=1: R("IDW", 128 * i + a, 128 * i + 128, st)
    pf = lambda i: R("PF", i, i + 1)
    blk = lambda b, k=1: R("XB", 512 * b, 512 * (b + k))
    rows = lambda w, a, b: T[w][0:128:16, a:b]
    I1, IPEN, INEG, I4, IHALF = 0, 8, 9, 10, 11
    SELN, SELK, SELA, SELM = R("SEL", 0, 8), R("SEL", 8, 16), R("SEL", 16, 32), R("SEL", 32, 40)
    CC, SS = R("XS", 0, 64, 2), R("XS", 1, 64, 2)
    CNT, AFL = R("P5", 128, 160), R("P5", 160, 192)
    sub5 = lambda c0, s: R("P5", c0 + 16 * (s >> 1) + (s & 1), c0 + 16 * (s >> 1) + 16, 2)
    A16 = R("A16", 0, 32)

    def places():
        for i in range(4):
            mm(R3("P3", 0, 2, 32 * i, 32 * i + 32), R("EX", 128 * i, 128 * i + 128), R("YY", 0, 64), True, True)

    def strides():
        for i in range(4):
            mm(R3("P4", 0, 2, 32 * i, 32 * i + 32), R("ES", 128 * i, 128 * i + 128), R("YY", 0, 64), True, True)
        for i in range(4):
            for j, w in enumerate(("EX", "EM")):
                mm(R3("P3", 0, 2, 128 + 32 * i, 160 + 32 * i), R(w, 128 * i, 128 * i + 128), R("YY", 0, 64), j == 0, j == 1)

    def offsets():
        for h in range(2):
            cp(R("EI", 128 * h, 128 * h + 128), R("P3", 256 * h, 256 * h + 128))
        for a in (0, 128):
            ts(R("EJ", a, a + 128), R("EI", a, a + 128), 4095, A.bitwise_and)
        for a in (0, 128):
            cp(R("OFF", a, a + 128), R("EJ", a, a + 128))

    def t_to_w(out, buf, w, start):
        for i in range(4):
            mm(out, R3(buf, 3 - i, 35 - i, 0, 4), idw(w, i, 4), start and i == 0, i == 3)

    padded = lambda buf, h: mk(buf, 0, 128, (slice(3, 35, 4), slice(2 * h, 2 * h + 2)))

    dma("y", T.NMI[:], T.nm[:], [], [R("NMI", 0, 256)])
    dma("y", T.LI[0:32, :], T.c0[:], [], [R("LI", 0, 128, 1, 0, 32)])
    dma("y", T.LI[32:64, :], T.s0[:], [], [R("LI", 0, 128, 1, 32, 64)])
    dma("y", T.OW0[:, 0:2048], T.vo[:, 0:2048], [], [R("OW0", 0, 2048)])
    iota(R("TB", 0, 128), [[1, 4], [4, 8], [32, 4]], 0, -1)
    iota(R("XD", 0, 144), [[1, 144]], 0, -1)
    iota(R("EX", 0, 512), [[0, 64], [1, 8]], 0, 0)
    asel(R("EX", 0, 512), R("EX", 0, 512), A.is_equal, 0.0, -1)
    iota(R("PI", 0, 1), [[0, 1]], 0, 1, False)
    asel(R("EX", 0, 512), R("EX", 0, 512), A.not_equal, 1.0, 0)
    iota(R("XI", 32, 48), [[1, 8], [0, 2]], 0, 0)
    iota(R("ES", 0, 512), [[0, 512]], 0, 0)
    asel(R("EM", 0, 512), R("ES", 0, 512), A.not_equal, -15.0, -1)
    asel(R("ES", 0, 512), R("ES", 0, 512), A.not_equal, 0.5, -1)
    iota(R("CK", 0, 136), [[0, 17], [-2, 8]], 7, 0)
    ms(R("NW", 0, 4096), 0.0)
    ts(idw(I1), R("XD", 0, 128), 0.0, A.is_equal)
    ts(R("SO", 0, 128), R("TB", 0, 128), 0.0, A.is_equal)
    ts(R("SP", 0, 128), R("TB", 0, 128), 64.0, A.is_equal)
    ms(R3("EQ", 0, 64, 0, 8), 0.0)
    ts(R("NMB", 0, 256), R("NMI", 0, 256), -256.0, A.add)
    dma("y", rows("NW", 0, 4096), T.NMB[:, 0:256], [R("NMB", 0, 256)], [R("NW", 0, 4096)])
    dma("y", T.OW0[:, 2048:4096], T.vo[:, 2048:4096], [], [R("OW0", 2048, 4096)])
    dma("y", T.VW0[:], T.vn[:], [], [R("VW0", 0, 4096)])
    dma("y", ap(blk(0)), T.xo[:], [], [blk(0)])
    dma("y", T.ZZ[:], T.z0[:], [], [R("ZZ", 0, 512)])
    ts(R("EI", 0, 128, 1, 0, 64), R("LI", 0, 128, 1, 0, 64), 2048.0, A.add)
    ts(R("EJ", 0, 128, 1, 0, 64), R("EI", 0, 128, 1, 0, 64), 4095, A.bitwise_and)
    ts(R("LF", 0, 128, 1, 0, 64), R("EJ", 0, 128, 1, 0, 64), -2048.0, A.add)
    for h in range(2):
        for q in range(2):
            mm(R("P7", 256 + 32 * h, 288 + 32 * h), R("SP" if q else "SO", 0, 128, 1, 0, 64), R("LF", 2 * h + q, 128, 4, 0, 64), q == 0, q == 1)
    ts(R("PI", 4, 5), R("PI", 0, 1), 15, A.bitwise_and)
    ts(R("PI", 5, 6), R("PI", 0, 1), 4, A.logical_shift_right)
    ts(R("PI", 1, 2), R("PI", 0, 1), 2, A.logical_shift_right, 3, A.bitwise_and)
    cp(R("YY", 0, 64), R("P7", 256, 320))
    places()
    ts(R("PI", 2, 3), R("PI", 0, 1), 1, A.logical_shift_right, 1, A.bitwise_and)
    ts(R("PI", 3, 4), R("PI", 0, 1), 1, A.bitwise_and)
    cp(R("PF", 0, 5), R("PI", 1, 6))
    act(R("QM", 0, 128), R("TB", 0, 128), AF.Ln, math.exp(-0.25), 0.0)
    for d in range(1, 8):
        act(idw(d), idw(I1), scale=math.exp(2.0 * d))
    act(idw(I4), idw(I1), scale=4.0)
    act(idw(IPEN), idw(I1), scale=-float(2 ** 17))
    act(idw(IHALF), idw(I1), scale=0.5)
    fill(R("RS", 0, 128), 128, 1.0)
    fill(R("LL", 0, 128), 128, math.exp(-0.5))
    fill(R("ZR", 0, 128), 128, 0.0)
    fill(R("RS", 0, 128, 8), 16, 0.0)
    act(pf(5), pf(0), bias=3.5, scale=16.0)
    act(pf(11), pf(3), bias=15.0, scale=-1.0)
    act(pf(6), pf(1), bias=pf(5), scale=2048.0)
    ts(pf(12), pf(3), 0.0, A.is_equal)
    ts(SELA, R("XI", 32, 48), pf(4), A.is_equal)
    ts(SELN, R("XI", 32, 48, 2), pf(4), A.is_equal, pf(12), A.mult)
    offsets()

    def consts_b():
        ms(R3("EQ", 64, 224, 0, 8), 0.0)
        act(SELK, R("SEL", 16, 32, 2), scale=16.0)

    def consts_w(i):
        if i == 0:
            tr(R("XS", 0, 64), R("YY", 0, 64))
        if i == 1:
            scan(R("LH", 0, 128), R("LL", 0, 128), R("ZR", 0, 128), math.exp(32.5), A.mult, A.add)
        if i == 2:
            mm(R("P6", 0, 1), R("LH", 0, 128, 1, 0, 1), R("MS", 1, 2, 1, 0, 1), True, True)

    def consts_c():
        act(pf(7), pf(2), bias=pf(6), scale=8.0)
        cp(R("WP", 0, 1), R("P6", 0, 1))
        act(pf(10), pf(4), scale=-32.0)
        act(R("WP", 1, 2), R("WP", 0, 1), scale=-1.0)

    def consts_d():
        fill(R("DS", 0, 128), 128, -0.25)
        act(R("JT", 0, 32), R("JT", 0, 32), bias=pf(10))
        fill(R("DS", 0, 128, 4), 32, 1e6)

    def consts_f():
        act(R("RID", 0, 512), R("RID", 0, 512), bias=127.25, scale=0.25)
        act(SELM, R("SEL", 16, 32, 2), scale=-32.0)

    def consts_e():
        ts(R("ZA", 0, 144), R("XD", 0, 144), pf(11), A.is_equal, 512.0, A.mult)
        ts(pf(13), pf(4), 1.5, A.is_lt, 2048.0, A.mult)

    iota(R("MS", 0, 128), [[0, 32], [1, 4]], 0, 0)
    iota(R("JT", 0, 32), [[1, 2], [32, 16]], 512, 2)
    iota(R("SN", 512, 1024), [[0, 512]], 0, 0)
    iota(R("C256", 0, 128), [[0, 128]], 256, 0)

    def consts_g():
        for r, w, st, v in ((R("A64", 0, 32), 32, 64, 0), (R("DP", 0, 144), 144, 0, 0), (R("CB", 0, 32), 32, 0, -112),
                            (R("CB", 32, 64), 32, 0, 32 * 312), (R("XH", 0, 64), 64, 0, -1), (R("OH", 0, 16), 16, 0, 0),
                            (R("DQ", 0, 144), 144, 0, 0), (R("DFW", 512, 576), 64, 0, 0), (A16, 32, 16, 0), (R("ONE", 0, 512), 512, 0, 1),
                            (R("RID", 0, 512), 512, 1, 0), (R("SN", 0, 512), 512, 1, -256), (R("SN", 1024, 1536), 512, 1, -256),
                            (R("SO", 128, 192), 64, 0, 0), (R("XF", 0, 128), 128, 0, 0), (blk(20), 512, 0, 0), (blk(22), 512, 0, 0)):
            iota(r, [[st, w]], v, 0)

    def onward(t, a, b):
        d, names = (3, ("YO", "YV")) if t == VIS - 1 else (-1, ("OW%d" % (t + 1), "VW%d" % (t + 1)))
        return [(d, R(names[0], a, b), R("OW%d" % t, a, b)), (d, R(names[1], a, b), R("VW%d" % t, a, b))]

    def early(t):
        a = 512 * t
        if t == VIS - 1:
            send(onward(t, 0, a - 512))
            return
        old = [(-1, blk(5 * t + 1), R("OW%d" % t, a, a + 512)), (-1, blk(5 * t + 4), R("VW%d" % t, a, a + 512))]
        send(old + ([(-1, blk(2), blk(0))] if t == 0 else []) + (onward(t, 0, 512) if t == 2 else []))
        send(onward(t, a + 512, 4096))

    for t in range(VIS):
        last = t == VIS - 1
        OW, VW = "OW%d" % t, "VW%d" % t
        sl = (512 * t, 512 * t + 512)
        XR = blk(5 * t)
        bo, bv, b2 = (17, 20, 16) if last else (5 * t, 5 * t + 3, 5 * t + 3)
        Z = R("ZZ", 0, 512)
        OFF = lambda a, b: R("OFF", a, b)
        even = lambda f, w, win, tp: f(R(w, 512 * tp, 512 * tp + 512, 2), ind(win, R("OFR", 16 * tp, 16 * tp + 16)))
        odd = lambda f, w, win: f(R(w, sl[0] + 1, sl[1], 2), ind(win, R("OFR", 64, 80) if last else R("OFS", 16, 32)))
        NP = lambda h, k0=0, k1=8: R3("P%d" % h, 0, 16, k0, k1)
        LM = lambda h: R("P2", 128 * h, 128 * h + 128)
        KB = ("P7", "P5")
        KEY = lambda h: R(KB[h], 0, 128)
        E = lambda h, d, k1: R3("EQ", 112 * h + 16 * (d - 1), 112 * h + 16 * d, 0, k1)

        def forward():
            if t > 0:
                for j in range(2):
                    dma("y", T.NMB[2 * t - 2 + j:128:16, 256 * t:256 * t + 256], rows("NW", sl[0] - 512 + 256 * j, sl[0] - 256 + 256 * j),
                        [R("NW", sl[0] - 512, sl[0])], [R("NMB", 256 * t + 128 * j, 256 * t + 128 * j + 128)])
                send(([(3, blk(19), XR), (4, blk(17), XR)] if last else [(-1, blk(bo + 2), XR)]) + onward(t, sl[0] - 512, sl[0]))
            send([(3 if last else -1, R("NMB", 256 * t + 256, 256 * t + 512), R("NMB", 256 * t, 256 * t + 256))])
            if t == 0:
                early(0)

        def refill():
            w = "NR" if last else "NW"
            nb = R("NMB", 256 * t + 256, 256 * t + 512)
            for j in range(2):
                dma("y", rows("SN", 512 + 256 * j, 768 + 256 * j), T.NMB[2 * t + j:128:16, 256 * t + 256:256 * t + 512], [nb],
                    [R("SN", 512 + 256 * j, 768 + 256 * j)])
            dma("y", rows(w, 0, 4096), T.NMB[:, 256 * t + 256:256 * t + 512], [nb], [R(w, 0, 4096)])
            if t == 0:
                dma("y", T.yn[:], T.C256[:], [R("C256", 0, 128)], [R("yn", 0, 2048)])
                dma("y", ap(blk(18)), T.vo[:, 1536:2048], [], [blk(18)])
                dma("y", ap(blk(21)), T.vn[:, 1536:2048], [], [blk(21)])
            if last:
                dma("g", T.yn[:, 0:1536], rows("NR", 0, 1536), [R("NR", 0, 1536), R("yn", 0, 2048)], [], accum_op=A.add)
                dma("y", T.yo[:, 0:1536], T.YO[:, 0:1536], [R("YO", 0, 1536)], [])
                dma("y", T.yv[:, 0:1536], T.YV[:, 0:1536], [R("YV", 0, 1536)], [])

        def ngv(i):
            cp(R("NG", 512 * i, 512 * i + 512), ind(R("NW", 0, 4096), OFF(32 * i, 32 * i + 32)))

        def ngs(i):
            act(R("NG", 512 * i, 512 * i + 512), ind(R("NW", 0, 4096), OFF(32 * i, 32 * i + 32)))

        def npe(h):
            for k in range(16):
                mm(R("P%d" % h, 8 * (k >> 3) + (k & 7), 128, 16), R("NG", 2048 * h + k, 2048 * h + 2048, 16), SELN, True, True)

        def og(a, b):
            act(R("OG", a, b), ind(R(OW, 0, 4096), OFF(a // 16, b // 16)))

        def eq(h):
            cp(R3("NS", 0, 16, 0, 8), NP(h))
            for d in range(1, 8):
                tt(E(h, d, 8 - d), NP(h, 0, 8 - d), R3("NS", 0, 16, d, 8), A.is_equal)
            for d in range(1, 8):
                mm(LM(h), E(h, d, 8), idw(d), d == 1, d == 7)

        def pen(h):
            mm(R(KB[h], 0, 136), idw(I1), R("CK", 0, 136), True, False)
            for d in range(1, 8):
                mm(R(KB[h], d, 128 + d), idw(IPEN), E(h, d, 8), False, False)

        def ln(h):
            act(R("LY", 128 * h, 128 * h + 128), LM(h), AF.Ln, math.exp(30.0), math.exp(29.96))

        def el(h, between=lambda i: None):
            a, b = 128 * h, 128 * h + 128
            tt(R("SR", a, b), R("P4", 2 * a, 2 * a + 128), R("LY", a, b), A.mult)
            between(0)
            tt(R("EK", a, b), R("P3", 2 * a + 128, 2 * a + 256), R("SR", a, b), A.add)
            between(1)
            ts(R("EL", a, b), R("EK", a, b), 4095, A.bitwise_and)
            between(2)
            cp(R("OFE", a, b), R("EL", a, b))

        def dg(a, b):
            tt(R("DD", a, b), ind(R(VW, 0, 4096), R("OFE", a // 16, b // 16)), R("OG", a, b), A.subtract)

        def ab(a, b):
            act(R("AD", a, b), R("DD", a, b), AF.Abs)

        def kpe(a, b):
            h, p0 = a // 2048, (a % 2048) // 16
            for k in range(16):
                mm(R(KB[h], k, 128, 16, p0, p0 + (b - a) // 16), R("AD", a + k, b, 16), SELK, False, k == 15)

        def pick(h):
            a, b = 16 * h, 16 * h + 16
            scan(R("KS", 8 * a, 8 * b), R("RS", 0, 128), KEY(h), 0.0, A.mult, A.max)
            ts(R("W8", a, b), R("KS", 8 * a + 7, 8 * b, 8), 16 * MAG, A.add, 16 * MAG, A.subtract)
            tt(padded("DP", h), R("W8", a, b), R("KS", 8 * a + 7, 8 * b, 8), A.subtract)

        z_list = lambda: ts(R("OFZ", 0, 32), R("P6", 192, 224), pf(3), A.add)
        z_new = lambda: act(Z, ind(R("ZW", 0, 1024), R("OFZ", 0, 32)))

        ngv(0); ngs(1); ngv(2); ngs(3)
        npe(0)
        if t == 0:
            strides()
            ngv(4); ngs(5)
            consts_b()
            ngs(6)
        else:
            cp(R("NG", 2048, 2816), ind(R("NW", 0, 4096), OFF(128, 176)))
            act(R("NG", 2816, 3584), ind(R("NW", 0, 4096), OFF(176, 224)))
        eq(0)
        ngv(7)
        if t > 0:
            even(act, VW, blk(5 * t - 2, 3), t - 1)
        forward()
        if t == 0:
            consts_g()
        og(0, 512)
        ln(0); npe(1); pen(0)
        og(512, 1024)
        el(0, consts_w if t == 0 else lambda i: None)
        refill()
        og(1024, 2048)
        dg(0, 512)
        eq(1)
        dg(512, 1024)
        og(2048, 3072)
        ln(1); pen(1)
        dg(1024, 1664)
        ab(0, 1024)
        og(3072, 3584)
        el(1, lambda i: dg(1664 + 128 * i, 1792 + 128 * i))
        ab(1024, 2048); kpe(0, 2048)
        dg(2048, 2560)
        og(3584, 4096)
        ab(2048, 2560); kpe(2048, 2560)
        dg(2560, 3072); ab(2560, 3072); kpe(2560, 3072)
        dg(3072, 3584); ab(3072, 3584); kpe(3072, 3584)
        dg(3584, 3840); ab(3584, 3840)
        dg(3840, 4096); ab(3840, 4096); kpe(3584, 4096)
        if t == 0:
            consts_c()
            cp(R("XB", 1, 512, 2), R("XB", 1025, 1536, 2))
        else:
            z_list()
            z_new()
        pick(0)
        act(R("T4", 0, 32), SS, bias=0.0 if last else 2048.0, scale=8.0)
        pick(1)
        if t == 0:
            mm(AFL, idw(I1), R("CB", 32, 64), True, True)
        mm(R("P6", 0, 32), idw(I1), R("A64", 0, 32), True, False)
        t_to_w(R("P6", 0, 32), "DP", IHALF, False)
        act(R("SQ", 0, 32), R("W8", 0, 32), AF.Square, 592.0, 1.0 / 16)
        act(R("ZW", 0, 512), Z, AF.Relu, -1.0)
        tt(R("FC", 0, 32), R("W8", 0, 32), R("KS", 7, 256, 8), A.subtract)
        tt(R("T5", 0, 32), R("SQ", 0, 32), AFL, A.add)
        ts(R("T8", 0, 32), R("W8", 0, 32), 0.125, A.mult, 1.0, A.add)
        ts(R("AB", 32, 64), R("T5", 0, 32), 10, A.logical_shift_right, 15, A.bitwise_and)
        ts(R("OFD", 0, 32), R("P6", 0, 32), pf(7), A.add)
        ts(R("AB", 64, 96), R("T5", 0, 32), 1, A.logical_shift_right, 16, A.bitwise_and)
        mm(CNT, idw(I1), R("CB", 0, 32), True, False)
        tt(R("GG", 0, 512), ind(R("AD", 0, 4096), R("OFD", 0, 32)), Z, A.is_lt)
        for s in range(4):
            mm(sub5(128, s), R("GG", s, 512, 4), SELK, False, s == 3)
        act(R("DFW", 0, 512), ind(R("DD", 0, 4096), R("OFD", 0, 32)))
        act(R("F7", 0, 32), R("FC", 0, 32), bias=3.5, scale=-0.5)
        act(R("BB", 0, 512), R("DFW", 0, 512), AF.Abs)
        mm(R("P0", 0, 512), idw(IHALF), Z, True, False)
        mm(R("P0", 0, 512), R("QM", 0, 128, 1, 0, 1), R("ONE", 0, 512, 1, 0, 1), False, False)
        mm(R("P0", 0, 512), idw(IHALF), R("BB", 0, 512), False, True)
        tt(R("XH", 64, 128, 2), R("AB", 32, 64), R("AB", 64, 96), A.add)
        ts(R("AB", 0, 32), R("T5", 0, 32), 6, A.logical_shift_right, 15, A.bitwise_and)
        ts(R("XH", 65, 128, 2), R("XH", 64, 128, 2), -16.0, A.add)
        cp(padded("DQ", 0), R("XH", 64, 96, 2))
        tt(R("XH", 0, 64, 2), CNT, R("AB", 0, 32), A.max)
        cp(padded("DQ", 1), R("XH", 96, 128, 2))
        for v in range(13):
            ts(R("OH", 16 + v, 2064, 16), R("XH", 0, 128), float(v), A.is_equal, R("WP", 0, 1), A.mult)
        for i in range(3):
            act(R("VT", i, 384, 3), R("XH", 0, 128), AF.Abs, -13.0 - i)
        act(R3("OH", 1, 129, 13, 16), R("VT", 0, 384), AF.Relu, R("WP", 0, 1), R("WP", 1, 2))
        act(R("Z2", 0, 512), R("P0", 0, 512), bias=MAG)
        if t == 0:
            consts_d()
        act(R("ZW", 512, 1024), R("Z2", 0, 512), bias=-MAG)
        for h in range(2):
            for q in range(2):
                for gr in range(8):
                    c, e, p0 = 16 * h + 2 * gr + q, gr & 1, 32 * (gr >> 1)
                    mm(R("P7", 128 + 2 * h + q, 256, 4, p0, p0 + 32), R("OH", 16 + 32 * c - 16 * e, 48 + 32 * c - 16 * e),
                       R("OH", 1040 + 32 * c, 1072 + 32 * c), e == 0, e == 1)
        t_to_w(R("P6", 32, 64), "DQ", I4, True)
        if not last:
            mm(R("P1", 0, 512), idw(I1), XR, True, False)
        tt(R("DC", 0, 32), R("F7", 0, 32), SS, A.mult)
        tt(R("CI", 32, 64), R("T4", 0, 32), CC, A.add)
        ts(R("SA", 0, 32), R("T8", 0, 32), 1023, A.bitwise_and)
        tt(R("CI", 0, 32), R("CI", 32, 64), R("DC", 0, 32), A.subtract)
        tt(R("DX", 1, 64, 2), R("SA", 0, 32), SS, A.subtract)
        ts(R("CJ", 0, 64), R("CI", 0, 64), 4095, A.bitwise_and)
        ts(CC, R("CJ", 0, 32), -2048.0, A.add)
        tt(R("DX", 0, 64, 2), R("CJ", 32, 64), R("CJ", 0, 32), A.subtract)
        if t == 0:
            consts_e()
        H = R("P7", 128, 256)
        ts(R("YH", 0, 128), H, 1.0, A.max, math.exp(-32.0), A.mult)
        scan(R("HM", 0, 128), R("MS", 0, 128), H, 0.0, A.mult, A.max)
        ts(R("YH", 128, 256), H, 1.0, A.min, math.exp(32.0), A.mult)
        act(R("LH", 0, 128), R("YH", 0, 128), AF.Ln)
        act(R("P2", 256, 384), R("LH", 0, 128), bias=192.23, scale=-1.0)
        act(R("LL", 0, 128), R("YH", 128, 256), AF.Ln, math.exp(-40.0))
        ts(R("FL", 0, 32), R("HM", 3, 128, 4), 0.0, A.is_gt, 512.0, A.mult)
        ts(R("OFB", 0, 32), R("P6", 32, 64), 3.0, A.add)
        tt(R("FM", 0, 16), R("JT", 0, 16), R("FL", 0, 16), A.add)
        ts(R("FI", 0, 32), CNT, 8.0, A.is_lt, 32.0, A.mult)
        cp(R("OFS", 0, 16), R("FM", 0, 16))
        tt(R("HQ", 0, 128), R("P2", 256, 384), R("LL", 0, 128), A.subtract)
        if not last:
            send([(-1, R("OFR", 16 * t, 16 * t + 16), R("OFS", 0, 16))])
        if t == 0:
            consts_f()
        tt(R("FM", 16, 32), R("JT", 16, 32), R("FL", 16, 32), A.subtract)
        scan(R("HS", 0, 128), R("DS", 0, 128), R("HQ", 0, 128), 0.0, A.add, A.min)
        own_list = lambda: cp(R("OFS", 16, 32), R("FM", 16, 32))
        if last:
            own_list()
        ts(R("OF1", 0, 32), R("HS", 3, 128, 4), 4.0, A.mult, -509.0, A.add)
        if last:
            send([(3, R("OFR", 48, 64), R("OFS", 0, 16)), (4, R("OFR", 64, 80), R("OFS", 16, 32))])

        def objects():
            ts(blk(b2), R("P1", 0, 512), 0.0, A.max, 255.0, A.min)
            send([(-1, blk(b2 + 2), blk(b2))])

        def z_offsets():
            mm(R("P6", 192, 224), idw(I1), A16, True, False)
            for r in range(16):
                mm(R("P6", 192, 224), R("ZA", 15 - r, 143 - r), R("AQ", r, 512, 16), False, r == 15)

        def flags():
            mm(AFL, idw(I1), R("CB", 32, 64), True, False)
            mm(AFL, idw(I1), R("FI", 0, 32), False, False)
            for s in range(4):
                mm(sub5(160, s), R("AQ", s, 512, 4), SELM, False, s == 3)

        if not last:
            for e in range(2):
                act(R("DM", e, 512, 2), ind(R("DFW", 0, 576), R("OF1", 16 * e, 16 * e + 16)))
        tt(R("AQ", 0, 512), ind(R("HS", 0, 128), R("OFB", 0, 32)), R("RID", 0, 512), A.is_equal)
        if not last:
            own_list()
            odd(act, "NW", R("SN", 0, 1024))
            odd(act, "OW%d" % (t + 1), blk(bo, 2))
        for s in range(4):
            mm(R3("P6", 16 + 8 * (s >> 1), 24 + 8 * (s >> 1), 2 * (s & 1), 2 * (s & 1) + 2), R("AQ", s, 512, 4), SELA, True, True)
        PR = lambda a, b: R("P2", 384 + a, 384 + b)
        if not last:
            mm(R("P1", 0, 512), idw(I1), R("DM", 0, 512), False, True)
            tt(PR(0, 64), R("P6", 64, 128), R("DX", 0, 64), A.mult)
            tt(R("XS", 0, 64), PR(0, 64), R("XS", 0, 64), A.add)
            tr(R("YY", 0, 64), R("XS", 0, 64))
            places()
            objects()
            early(t + 1)
            offsets()
            odd(act, "VW%d" % (t + 1), blk(bv, 2))
            even(act, "NW", R("SN", 0, 1536), t)
            even(cp, "OW%d" % (t + 1), blk(bo, 3), t)
            strides()
            z_offsets()
            flags()
        else:
            for e in range(2):
                tt(R("DM", 256 * e, 256 * e + 256), ind(R("DFW", 0, 576), R("OF1", 16 * e, 16 * e + 16)), R("XB", 512 * 15 + e, 512 * 16, 2), A.add)
            for h in range(2):
                act(padded("DP", h), mk("P6", 0, 128, (slice(16 + 8 * h, 24 + 8 * h), slice(0, 4, 2))), scale=512.0)
            flags()
            mm(R("P0", 0, 32), idw(I1), A16, True, False)
            t_to_w(R("P0", 0, 32), "DP", I1, False)
            tt(PR(0, 64), R("P6", 64, 128), R("DX", 0, 64), A.mult)
            ts(blk(b2), R("DM", 0, 512), 0.0, A.max, 255.0, A.min)
            send([(3 + e, R("XL", 256 * e, 256 * e + 256), R("XB", 512 * b2 + 256 * e, 512 * b2 + 256 * e + 256)) for e in range(2)])
            ts(R("OFZ", 0, 32), R("P0", 0, 32), pf(3), A.add)
            z_new()
            send([(3, R("ZL", 0, 512), Z)])
            for h in range(2):
                tt(R("XF", 64 * h, 64 * h + 32), PR(32 * h, 32 * h + 32), R("XS", 32 * h, 32 * h + 32), A.add)
            for h in range(2):
                ts(R("XF", 64 * h + 32, 64 * h + 64, 2), R("P5", 160 + 16 * h, 176 + 16 * h), 1.0 / 32, A.mult, -312.0 - 2048.0, A.add)
            tr(R("YY", 0, 128), R("XF", 0, 128))
            for s in range(4):
                h, q = s >> 1, s & 1
                mm(R("P7", 256 + s, 512, 4), R("SO", 64 * q, 64 * q + 128), R("YY", 64 * h, 64 * h + 64), True, True)
            ts(R("FO", 0, 256), R("P7", 256, 512), pf(13), A.add)
            send([(3, R("FN", 0, 256), R("FO", 0, 256))])
            even(cp, "NR", R("SN", 0, 1536), t)
            odd(cp, "NR", R("SN", 0, 1024))
            dma("g", T.yn[:, 1536:2048], rows("NR", *sl), [R("NR", *sl), R("yn", 0, 2048)], [], accum_op=A.add)
            even(act, "YO", blk(bo, 3), t)
            odd(act, "YO", blk(bo, 2))
            dma("y", T.yo[:, 1536:2048], T.YO[:, 1536:2048], [R("YO", *sl)], [])
            cp(R("XB", 512 * 20 + 1, 512 * 21, 2), R("XL", 256, 512))
            cp(R("XB", 512 * 22, 512 * 23, 2), R("XL", 0, 256))
            odd(act, "YV", blk(bv, 2))
            even(cp, "YV", blk(bv, 3), t)
            dma("y", T.yz[:], T.ZL[:], [R("ZL", 0, 512)], [])
            dma("s", T.yv[:, 1536:2048], T.YV[:, 1536:2048], [R("YV", *sl)], [])
            cp(R("YX", 0, 512, 2), R("XL", 0, 256))
            cp(R("YX", 1, 512, 2), R("XL", 256, 512))
            dma("s", T.yx[:], T.YX[:], [R("YX", 0, 512)], [])
            dma("y", T.yc[:], T.FN[0:32, 0:128], [R("FN", 0, 256)], [])
            dma("y", T.ys[:], T.FN[32:64, 0:128], [R("FN", 0, 256)], [])
            dma("y", T.ya[:], T.FN[0:32, 128:256], [R("FN", 0, 256)], [])

    for s, v in total.items():
        if clock["g"].get(s, 0) < v:
            g.wait_ge(T.sem[s], v)
